import numpy as np, ml_dtypes
CORES = [8,9,10,11,12,13]
N = 6
BF = ml_dtypes.bfloat16
def gentries(a):
    return np.ascontiguousarray(a.reshape(8, 16, -1).transpose(0, 2, 1)).reshape(8, -1)
def gtable(e):
    e = np.asarray(e); return np.ascontiguousarray(e.reshape(8, -1, 16).transpose(0, 2, 1)).reshape(128, -1).astype(np.int32)
V, WN, M, S, RO, LIM, PEN, T0 = 4096, 1024, 384, 3, 2, 20, 45, 34816
H = WN // 2
def parts(rng):
    return rng.integers(0, 256, (N, 8, 16, V)), rng.integers(0, V, (N, 8, 16, WN)), rng.integers(0, V, (N, 8, M)), rng.integers(0, 256, (N, 8, 16, M))
def pack(X, O, v, z):
    return {"tracks": np.ascontiguousarray(X.reshape(N, 128, V)).astype(np.float32).astype(BF),
            "nb": np.ascontiguousarray((O[..., :H] + V * O[..., H:]).reshape(N, 128, H)).astype(np.int32),
            "v": np.stack([gtable(a) for a in v]), "z": np.ascontiguousarray(z.reshape(N, 128, M)).astype(np.float32).astype(BF)}
def bits(b):
    return 255 * ((np.asarray(b)[..., None] >> (15 - np.arange(16))) & 1)
def tune(b, goal):
    t = bits(b); t = t - LIM * (t > 0); need = int((goal - np.add.reduce((2 * np.arange(16) + 1) * t)) % V)
    for p in range(15, -1, -1):
        d = min(LIM, need // (2 * p + 1)); t[p] += d; need -= d * (2 * p + 1)
    return t
def ladder(z):
    t = np.tile(np.where(np.abs(z - 128) > 64, 128, 0), (3, 1)); t[:, 0] = z[0]
    for j in (1, 2, 3): t[j - 1, 4 - j] = z[4 - j] + (LIM + j) * (1 if z[4 - j] < 128 else -1)
    return t
def setup_inputs(rng):
    X, O, v, z = parts(rng)
    few = np.take_along_axis(rng.integers(0, V, (N, 8, 16)), rng.integers(0, 16, (N, 8, M)), 2)
    return pack(X, O, np.where(rng.random((N, 8, M)) < 0.25, few, v), z)
def uneven(rng, n):
    a = np.minimum((np.exp2(8 * rng.random((N, 8, 1, n))) * rng.random((N, 8, 16, n))).astype(np.int64), 255)
    return np.where(rng.random(a.shape) < 0.5, 255 - a, a)
def setup_inputs_spread(rng):
    O = np.minimum((V * rng.random((N, 8, 16, WN)) ** 3).astype(np.int64), V - 1); v = np.minimum((V * rng.random((N, 8, M)) ** 2).astype(np.int64), V - 1)
    return pack(uneven(rng, V), O, v, uneven(rng, M))
def setup_inputs_ends(rng):
    X, O, v, z = parts(rng)
    X = 255 * rng.integers(0, 2, X.shape); z = 255 * rng.integers(0, 2, z.shape)
    e = (V - 1) * rng.integers(0, 2, (N, 8, 16, H)); keep = rng.random((N, 8, 16, H)) < 0.75
    keep[..., 0] = True; keep[..., H - 1] = True; e[:, :, 14, H - 1] = V - 1; e[:, :, 15, H - 1] = 0; e[:, :, 14, 0] = 0; e[:, :, 15, 0] = V - 1
    O = np.concatenate([np.where(keep, e, O[..., :H]), np.where(keep, e, O[..., H:])], axis=3)
    v = np.where(rng.random(v.shape) < 0.75, (V - 1) * rng.integers(0, 2, v.shape), v)
    X[:, 1::2, :, V - 1] = X[:, 1::2, :, 0]
    z[..., M // 2:M // 2 + 8] = 255
    v[:, :, M - 2:] = V - 1; z[..., M - 1] = X[..., V - 1]; z[..., M - 2] = 255 - X[..., V - 1]
    v[:, :, :2] = 0; z[..., 0] = X[..., 0]; z[..., 1] = 255 - X[..., 0]
    return pack(X, O, v, z)
def setup_inputs_ties(rng):
    X, O, v, z = parts(rng)
    B = np.broadcast_to(rng.integers(60, 196, (1, 8, 16, 6)), (N, 8, 16, 6)); jog = np.array([LIM, LIM + 1, LIM + 2, LIM + 3, LIM + 4, -LIM, -LIM - 1, -LIM - 2])
    X = np.take_along_axis(B, np.broadcast_to(rng.integers(0, 6, (N, 8, 1, V)), X.shape), 3)
    X = np.where((rng.random((N, 8, 1, V)) < 0.5) & (rng.random(X.shape) < 0.15), X + rng.choice(jog, X.shape), X)
    z = np.take_along_axis(B, np.broadcast_to(rng.integers(0, 6, (N, 8, 1, M)), z.shape), 3)
    z = np.where(rng.random(z.shape) < 0.3, z + rng.choice(jog, z.shape), z)
    O[:, ::2] = np.tile(O[:, ::2, :4], (1, 1, 4, 1))
    return pack(X, O, v, z)
def calm(rng, X, O, v, z, g, low):
    for r in range(N):
        t = rng.integers(0, 256, 16); B = rng.permutation(V)[:5]; f, n, L = int(B[0]), int(B[1]), B[2:]
        w = rng.permutation(np.setdiff1d(np.arange(WN), np.array([f & (WN - 1)])))[:2]; go, end = int(w[0]), int(w[1])
        X[r, g][:, f] = t; X[r, g][:, n] = np.where(np.abs(t - 128) > 64, 128, 0); X[r, g][:, L] = ladder(t).T
        O[r, g][:, go] = f; O[r, g][:, end] = n; O[r, g][:, f & (WN - 1)] = L[rng.permutation(16) % 3]
        stay = np.ones(M, bool); z[r, g] = t[:, None]
        if r in low: stay = np.isin(np.arange(M), rng.permutation(M)[:low[r]])
        else: z[r, g][1:] = rng.integers(0, 256, (15, M))
        v[r, g] = np.where(stay, end, go) + WN * rng.integers(0, V // WN, M)
def setup_inputs_corners(rng):
    X, O, v, z = parts(rng); C = min(M // 4, WN // (4 * N)); own = 1 + np.arange(3 * N * C).reshape(N, 3, C); top = 3 * N * C + 1
    O[..., 0] = rng.choice(np.array([0, V - 1]), (N, 8, 16)); O[..., WN - 1] = rng.choice(np.array([0, V - 1]), (N, 8, 16))
    for r in range(N):
        for g in range(8):
            o = rng.permutation(M); rest = o[3 * C:]
            v[r, g, rest[::2]] = rng.choice(np.array([0, V - 1]), len(rest[::2]))
            for j in range(3):
                E = own[r, j]; ln = o[j * C:(j + 1) * C]; b = rng.integers(0, 65536, C); d = rng.integers(1, 1000, C)
                v[r, g, ln] = E + WN * rng.integers(0, V // WN, C); z[r, g][:, ln] = bits(b).T
                for s in range((S, 1, 2)[j]):
                    q = (r + s) % N
                    t = 65535 - (S - 1 - s) * d if j == 0 else np.full(C, T0 + j - 1)
                    b = b ^ (65535 - t); X[q, g][:, E] = bits(b).T
                    if j == 0:
                        O[q, g][:, E] = rng.integers(top, V, (16, C)); O[q, g][rng.integers(0, 16, C), E] = E
                    else: O[q, g][:, E] = E
    two = rng.permutation(8)[:2]; few = rng.permutation(4)
    for i in range(2): calm(rng, X, O, v, z, int(two[i]), {(i + 2 * j) % N: int(few[(i * (N // 2) + j) % 4]) for j in range(N // 2)})
    return pack(X, O, v, z)
def apart(rng, X, O, v, z, g, q, b):
    K = (S - 1) * M; E = rng.permutation(WN - 1)[:K]; E[K - 1] = WN - 1
    B = E + WN * rng.integers(0, V // WN, K); B[K - 1] = V - 1; B2 = (B[:M] + WN) % V
    left = int(np.setdiff1d(np.arange(WN), E)[0]); X[:, g, :, left] = 128
    for r in range(N):
        k = rng.integers(0, 16, K); k[K - 1] = 15
        X[r, g][:, B] = bits(int(b[r]))[:, None]; O[r, g][:, E] = left; O[r, g][k, E] = B
        if r == q:
            X[r, g][:, B2] = bits(65535 - int(b[q]))[:, None]; O[r, g][(k[:M] + 1 + rng.integers(0, 15, M)) % 16, E[:M]] = B2
    for s in range(1, S):
        r = (q - s) % N; v[r, g] = B[(s - 1) * M:s * M]
        for i in range(M): z[r, g, :, i] = tune(int(b[r]) ^ (65534 - T0), int(rng.integers(1, V)))
    v[q, g] = B2; z[q, g] = bits(65535 - int(b[q]))[:, None]
def setup_inputs_crowd(rng):
    X, O, v, z = parts(rng)
    v = np.take_along_axis(rng.integers(0, V, (N, 8, 3)), rng.integers(0, 3, (N, 8, M)), 2)
    o = rng.permutation(8)
    for i in range(7):
        g = int(o[i]); q = int(rng.integers(0, N)); a = int((V - 1, 0, WN, rng.integers(1, V - 1), V - 1, rng.integers(1, V - 1), 0)[i]); first = q - S + (2 if i < 2 else 1)
        t = np.sort(T0 + 2 + rng.permutation(65534 - T0)[:S - 1]); b = rng.integers(0, 65536, N)
        if i in (2, 3): t[S - 2] = t[S - 3]
        if i >= 4: t[S - 2] = 65535
        for j in range(1, S): b[(first + j) % N] = b[(first + j - 1) % N] ^ (65535 - int(t[j - 1]))
        b = b ^ (int(b[q]) ^ int(rng.integers(1, 65535)))
        if i == 6:
            apart(rng, X, O, v, z, g, q, b); continue
        for r in range(N): X[r, g, :, a] = bits(int(b[r]))
        O[:, g, :, a & (WN - 1)] = a
        if i == 0: X[:, g, :, 0] = 128; O[:, g, :15, a & (WN - 1)] = 0
        v[:, g] = (a + WN * rng.integers(0, V // WN, (N, M))) % V
        for r in range(N):
            m = T0 + 1
            if i in (2, 3) and r == q: m = T0
            if i in (2, 3) and r == (q - 1) % N: m = int(t[S - 2])
            if i >= 4 and r == q: m = 65535
            z[r, g] = tune(int(b[r]) ^ (65535 - m), V - 1)[:, None]
        if i in (2, 3):
            e = (a + 1 + np.arange(3)) % V
            X[q, g][:, e] = ladder(z[q, g, :, 0]).T; O[q, g, :, (a - 1) & (WN - 1)] = e[rng.permutation(16) % 3]
        if i == 2:
            y = tune(int(b[q]) ^ (65535 - T0), V - 2); z[q, g, :, 1::2] = y[:, None]
            f = (a + 4) % V; nx = (q + 1) % N; x = np.full(16, 128); x[[0, 4, 15]] = y[[0, 4, 15]]
            X[q, g, :, f] = x; O[q, g, :, (a - 2) & (WN - 1)] = f
            X[nx, g][:, e] = ladder(x).T; O[nx, g, :, f & (WN - 1)] = e[rng.permutation(16) % 3]
        if i == 1: z[q, g, :, M - 1] = bits(65535 - int(b[q]))
        if i == 3: z[q, g, :, M - 1] = bits(int(b[q]))
        if i == 5: z[q, g, :, M - max(1, S * M - 1024):] = bits(65535 - int(b[q]))[:, None]
    return pack(X, O, v, z)
def check_inputs(d):
    bad = []
    for k, hi in (("tracks", 255), ("nb", V * V - 1), ("v", V - 1), ("z", 255)):
        a = np.asarray(d[k]).astype(np.float64)
        if not np.all((a >= 0) & (a <= hi) & (a == np.floor(a))): bad.append("range of " + k)
    return bad
def reference(tracks, nb, v, z):
    X = np.ascontiguousarray(tracks.astype(np.float32).astype(np.int16).reshape(N, 8, 16, V).transpose(0, 1, 3, 2))
    a = nb.astype(np.int64).reshape(N, 8, 16, H)
    O = np.ascontiguousarray(np.concatenate([a & (V - 1), a // V], axis=3).transpose(0, 1, 3, 2))
    bo = np.stack([gentries(e) for e in v]).astype(np.int64)
    tr = np.ascontiguousarray(z.astype(np.float32).astype(np.int16).reshape(N, 8, 16, M).transpose(0, 1, 3, 2))
    r = np.arange(N)[:, None, None]; g = np.arange(8)[None, :, None]
    two = (1 << (15 - np.arange(16))).astype(np.int32); odd = 2 * np.arange(16) + 1
    settled = np.zeros((N, 8), np.int64)
    for rnd in range(RO):
        u = np.add.reduce(tr * odd, axis=-1) & (V - 1)
        vs, zs, mark, live, c, trail = bo, tr, np.full((N, 8, M), T0), np.ones((N, 8, M), bool), np.zeros((N, 8, M), np.int64), []
        for s in range(S):
            q = (r + s) % N; w = vs & (WN - 1)
            P = O[q, g, w]
            x = X[q[..., None], g[..., None], P]
            near = np.abs(x - zs[:, :, :, None, :]) <= LIM + (settled[q, g] & 3)[..., None, None]
            T = np.add.reduce(np.where(near, two, 0), axis=-1)
            k = np.argmax(T, axis=-1); best = np.max(T, axis=-1)
            go = live & (best > mark)
            nv = np.take_along_axis(P, k[..., None], 3)[..., 0]; nz = np.take_along_axis(x, k[..., None, None], 3)[:, :, :, 0]
            trail.append((w, k, nv))
            vs = np.where(go, nv, vs); zs = np.where(go[..., None], nz, zs); mark = np.where(go, best, mark); c = c + go; live = go
            if s == 0: z1 = zs
        hit = np.zeros((N, 8, V), bool); more = np.zeros((N, 8, WN, 16), np.int64); settled = np.zeros((N, 8), np.int64)
        G = np.broadcast_to(g, (N, 8, M))
        for s in range(S):
            w, k, nv = trail[s]; Q = np.broadcast_to((r + s) % N, (N, 8, M))
            e = c == s + 1; hit[Q[e], G[e], nv[e]] = True
            e = c > s + 1; np.add.at(more, (Q[e], G[e], w[e], k[e]), u[e])
            e = (c == s) if s < S - 1 else (c >= s)
            settled = settled + np.roll(np.add.reduce(e.astype(np.int64), axis=2), s, axis=0)
        X = np.where(hit[..., None], np.maximum(X - PEN, 0), X).astype(np.int16); O = (O + more) & (V - 1)
        bo = np.where(c > 0, vs, (bo + u) & (V - 1)); tr = np.where((c > 0)[..., None], (tr + z1) >> 1, tr).astype(np.int16)
    o = O.transpose(0, 1, 3, 2)
    return {"yx": np.ascontiguousarray(X.transpose(0, 1, 3, 2)).reshape(N, 128, V).astype(np.float32).astype(BF),
            "yn": np.ascontiguousarray(o[..., :H] + V * o[..., H:]).reshape(N, 128, H).astype(np.float32),
            "yv": np.stack([gtable(e) for e in bo]).astype(np.float32),
            "yz": np.ascontiguousarray(tr.transpose(0, 1, 3, 2)).reshape(N, 128, M).astype(np.float32).astype(BF)}

@@ -1,0 +1,486 @@
+from concourse.mybir import dt, AluOpType as OP, ActivationFunctionType as AF, AxisListType
+
+RO, ST, NCH = 2, 3, 3
+CUT0 = 72
+BS = {"float32": 4, "int32": 4, "bfloat16": 2, "float16": 2, "uint16": 2}
+SCRATCH, ALIAS, POOL = {}, {}, {}
+
+
+def _b(names, cols, dtype, where="sbuf"):
+    for n in names.split():
+        SCRATCH[n] = (where, [128, cols], dtype)
+
+
+def _s(names, cols, dtype):
+    for n in names.split():
+        w = 32 // BS[dtype]; o = POOL.get(dtype, 0)
+        ALIAS[n] = ("pool_" + dtype, o, cols); POOL[dtype] = o + (cols + w - 1) // w * w
+
+
+_b("X", 4112, "bfloat16"); _b("O", 4112, "int32"); _b("OX OT OE", 1024, "int32"); _b("NB", 512, "int32"); _b("YN EXS", 512, "float32")
+_b("XG0 XG1 XG2 NR0 NR1", 2048, "bfloat16"); _b("PO0 PO1 PO2 PO3", 128, "uint16"); _b("PF0 PF1 PF2 PF3 SEL0 SEL1 M0_0 M0_1 M0_2 IOH", 128, "float16")
+_b("D0 D1 D2 KEY MI EX0 EX1 PEN", 512, "float32", "psum"); _b("NO0 NO1", 128, "bfloat16")
+_b("S1_0 S1_1 S1_2", 384, "float32"); _b("SG0 SG1 SG2", 24 * 34, "bfloat16"); _b("XOH0 XOH1 YU", 24 * 128, "float16"); _b("HOH", 24 * 128, "bfloat16")
+_s("VMB0 VMB1 VMB2 QB0 QB1 QB2 LOB0 LOB1 LOB2 HP0 HP1 HP2 XC0 XC1 WL0 WL1 FA0 FA FB BB BC BD EF EG EH HM0 HM1 HM2 FC0 FC1 UM0 UM1 CF", 24, "float32")
+_s("VL IA IB IC ID_ LWI BI EA EB EC PA PB_ PC", 24, "int32"); _s("LW", 24, "uint16"); _s("MM PB I16", 8, "float32"); _s("QA QT", 24, "bfloat16")
+for _r in range(RO):
+    for _i in range(3):
+        _b("Z%d_%d" % (_r, _i), 384, "bfloat16")
+        _s("GO%d_%d" % (_r, _i), 24, "float32"); _s("LU%d_%d" % (_r, _i), 24, "uint16")
+        if _i < 2:
+            _s("F%d_%d" % (_r, _i), 24, "float32"); _b("ZO%d_%d" % (_r, _i), 384, "bfloat16")
+        if _i > 0:
+            _s("FL%d_%d GL%d_%d" % (_r, _i, _r, _i), 24, "float32"); _s("LV%d_%d LL%d_%d" % (_r, _i, _r, _i), 24, "uint16")
+    _s("UV%d UL%d" % (_r, _r), 48, "float32")
+_b("HC0", 264, "float32"); _b("HC", 264, "bfloat16"); _b("HS", 4096, "bfloat16")
+_b("RY", 384, "float32"); _b("RB RN RE RD ONE", 384, "bfloat16")
+_b("IOT", 144, "float32"); _b("IOB ID HID NID FI NFI REP NREP KB QROW", 128, "bfloat16"); _s("CI", 8, "int32")
+_s("W8 WU B8B", 8, "bfloat16"); _s("B8", 8, "float16"); _s("BM", 16, "float16"); _b("DB", 144, "float16"); _b("DUB", 144, "bfloat16")
+_b("RST KF GF", 128, "float32"); _b("ZR", 512, "float16")
+_s("AL", 48, "float32"); _s("AR FCOL", 1, "float32"); _s("AC AB", 1, "bfloat16"); _s("AI AJ", 1, "int32")
+for _d in POOL:
+    _b("pool_" + _d, POOL[_d], _d)
+
+SEMAPHORES = ["V", "S", "P", "G", "ls", "dnb", "dv", "dz", "dx0", "dx1", "dx2", "dx3", "dhs", "dex", "dox", "dcp", "oyx0", "oyx1", "oyn", "oyv"]
+for _r in range(RO):
+    for _j in (1, 2):
+        for _i in range(NCH):
+            SEMAPHORES += ["aF%d_%d_%d" % (_r, _j, _i), "aV%d_%d_%d" % (_r, _j, _i), "aZ%d_%d_%d" % (_r, _j, _i)]
+        SEMAPHORES += ["aG%d_%d" % (_r, _j), "aL%d_%d" % (_r, _j)]
+    SEMAPHORES += ["aU%d" % _r]
+
+MAG = 12582912.0
+M16 = 201326592.0
+UP, DOWN, EPS = 4097 / 4096, 4095 / 4096, 0.00015
+THR0 = 16.0 * (34816 + 1) - 0.5
+
+
+def rank_program(g, core, T, topo):
+    rank = T.rank_of(core)
+    if rank is None:
+        return
+    N = len(T.cores)
+    nxt, prv = T.cores[(rank + 1) % N], T.cores[(rank - 1) % N]
+    eng = {"V": g.vector, "S": g.scalar, "P": g.tensor, "G": g, "Y": g.sync}
+    cnt, snap, acc, known = {}, {}, {}, {q: {} for q in eng}
+
+    def A(name, c0=0, c1=None, step=1, p0=0, p1=128):
+        if name in ALIAS:
+            n, o, w = ALIAS[name]
+            return (n, o + c0, o + (w if c1 is None else c1), step, p0, p1)
+        return (name, c0, SCRATCH[name][1][1] if c1 is None else c1, step, p0, p1)
+
+    def ap(a):
+        t = T[a[0]]
+        return t[a[4]:a[5], a[1]:a[2]] if a[3] == 1 else t[a[4]:a[5], a[1]:a[2]:a[3]]
+
+    def span(a):
+        w = BS[SCRATCH[a[0]][2]]
+        if SCRATCH[a[0]][0] == "psum": return (0, 128, 0, 2048)
+        return (a[4], a[5], a[1] * w, a[2] * w)
+
+    def learn(q, comp, n):
+        k = known[q]
+        if k.get(comp, 0) >= n: return
+        k[comp] = n
+        for c2, n2 in snap.get((comp, n), {}).items():
+            if k.get(c2, 0) < n2: k[c2] = n2
+
+    def hazards(q, comp, reads, writes):
+        need = {}
+        for lst, w in ((reads, False), (writes, True)):
+            for a in lst:
+                ps = SCRATCH[a[0]][0] == "psum"; s = span(a)
+                for (t, ow, oc, on, oq) in acc.get(a[0], []):
+                    b = 16 if ow and w and (oc in eng) != (comp in eng) else 1
+                    if not (s[0] < t[1] and t[0] < s[1] and s[2] // b * b < -(-t[3] // b) * b and t[2] // b * b < -(-s[3] // b) * b): continue
+                    if ps:
+                        if oq == q and oc == comp and (q == "P" or not (ow or w)): continue
+                    elif not (ow or w): continue
+                    if oc[0] in "do" and known[q].get(oc, 0) < on: on = cnt[oc]
+                    if need.get(oc, 0) < on: need[oc] = on
+        for oc in sorted(need, key=lambda c: -need[c]):
+            if known[q].get(oc, 0) < need[oc]:
+                eng[q].wait_ge(T.sem[oc], need[oc]); learn(q, oc, need[oc])
+
+    def note(q, comp, n, reads, writes):
+        for a in writes:
+            s = span(a); ps = SCRATCH[a[0]][0] == "psum"
+            if not ps: acc[a[0]] = [r for r in acc.get(a[0], []) if not (s[0] <= r[0][0] and r[0][1] <= s[1] and s[2] <= r[0][2] and r[0][3] <= s[3])]
+        for lst, w in ((reads, False), (writes, True)):
+            for a in lst:
+                s = span(a)
+                l = [r for r in acc.setdefault(a[0], []) if not (r[0] == s and r[1] == w and r[2] == comp and r[4] == q)]
+                acc[a[0]] = l + [(s, w, comp, n, q)]
+
+    def run(q, reads, writes, call):
+        hazards(q, q, reads, writes)
+        i = call(); cnt[q] = cnt.get(q, 0) + 1
+        i.then_inc(T.sem[q], 1)
+        snap[(q, cnt[q])] = dict(known[q])
+        note(q, q, cnt[q], reads, writes)
+
+    def dma(sem, out, in_, q="Y", reads=(), writes=()):
+        hazards(q, sem, reads, writes)
+        eng[q].dma_start(out, in_).then_inc(T.sem[sem], 16)
+        cnt[sem] = cnt.get(sem, 0) + 16
+        snap[(sem, cnt[sem])] = dict(known[q])
+        note(q, sem, cnt[sem], reads, writes)
+
+    def send(dst, out, in_, sem):
+        hazards("G", "ls", [in_], [])
+        rid, pid, _ = topo.addr(dst)
+        g.remote_dma(ap(out), ap(in_), T.sem[sem], T.sem["ls"], pid, rid, topo.mask(core, dst))
+        cnt["ls"] = cnt.get("ls", 0) + len(topo.engines(core, dst))
+
+    def arrives(sem, a, src):
+        cnt[sem] = len(topo.engines(src, core)); note("R", sem, cnt[sem], [], [a])
+
+    def col(x):
+        return (ap(x), [x]) if isinstance(x, tuple) else (x, [])
+
+    def ts(out, in0, s1, op0, s2=None, op1=None):
+        v1, r1 = col(s1); v2, r2 = col(s2)
+        if op1 is None: run("V", [in0] + r1, [out], lambda: g.vector.tensor_scalar(ap(out), ap(in0), v1, None, op0))
+        else: run("V", [in0] + r1 + r2, [out], lambda: g.vector.tensor_scalar(ap(out), ap(in0), v1, v2, op0, op1))
+
+    def tt(out, a, b, op):
+        run("V", [a, b], [out], lambda: g.vector.tensor_tensor(ap(out), ap(a), ap(b), op))
+
+    def cp(out, a):
+        run("V", [a], [out], lambda: g.vector.tensor_copy(ap(out), ap(a)))
+
+    def ms(out, c):
+        run("V", [], [out], lambda: g.vector.memset(ap(out), c))
+
+    def mm(out, l, r, start, stop):
+        run("P", [l, r], [out], lambda: g.tensor.matmul(ap(out), ap(l), ap(r), start, stop))
+
+    def act(out, a, f, bias=None):
+        v, r = col(bias)
+        if bias is None: run("S", [a], [out], lambda: g.scalar.activation(ap(out), ap(a), f))
+        else: run("S", [a] + r, [out], lambda: g.scalar.activation(ap(out), ap(a), f, bias=v))
+
+    def gather_v(out, win, off):
+        run("V", [win, off], [out], lambda: g.vector.tensor_copy(ap(out), ap(win).indirect(ap(off))))
+
+    def gather_s(out, win, off):
+        run("S", [win, off], [out], lambda: g.scalar.activation(ap(out), ap(win).indirect(ap(off)), AF.Copy))
+
+    def iota(out, pat, base, cm, flag=True):
+        if flag: run("G", [], [out], lambda: g.iota(ap(out), pat, base, cm, allow_small_or_imprecise_dtypes=True))
+        else: run("G", [], [out], lambda: g.iota(ap(out), pat, base, cm))
+
+    fq = []
+
+    def tick(k=1):
+        while fq and k: fq.pop(0)(); k -= 1
+
+    def weave(a, b):
+        o = []
+        for i in range(max(len(a), len(b))): o += a[i:i + 1] + b[i:i + 1]
+        return o
+
+    for r in range(RO):
+        for s in (1, 2):
+            for i in range(NCH):
+                arrives("aF%d_%d_%d" % (r, s, i), A("FL%d_%d" % (r, s), 8 * i, 8 * i + 8), prv)
+                arrives("aV%d_%d_%d" % (r, s, i), A("LV%d_%d" % (r, s), 8 * i, 8 * i + 8), prv)
+                arrives("aZ%d_%d_%d" % (r, s, i), A("Z%d_%d" % (r, s), 128 * i, 128 * i + 128), prv)
+            arrives("aG%d_%d" % (r, s), A("GL%d_%d" % (r, s)), nxt)
+            arrives("aL%d_%d" % (r, s), A("LL%d_%d" % (r, s)), T.cores[(rank + s) % N])
+        arrives("aU%d" % r, A("UL%d" % r), prv)
+
+    ms(A("X", 2048, 2049), 512.0); ms(A("X", 4097, 4112), 512.0); ms(A("O", 2048, 2049), 0); ms(A("O", 4097, 4112), 0)
+    dma("dnb", ap(A("NB")), T.nb[:, :], "Y", [], [A("NB")])
+    dma("dv", ap(A("VL")), T.v[:, :], "S", [], [A("VL")])
+    for i in range(4):
+        a = A("X", 1024 * i + i // 2, 1024 * i + i // 2 + 1024)
+        dma("dx%d" % i, ap(a), T.tracks[:, 1024 * i:1024 * i + 1024], "YS"[i % 2], [], [a])
+    dma("dz", ap(A("Z0_0")), T.z[:, :], "Y", [], [A("Z0_0")])
+    iota(A("CI", 0, 1), [[1, 1]], 0, 1, False)
+    iota(A("IOT"), [[1, 144]], 0, 0)
+    iota(A("I16"), [[16, 8]], 0, 0)
+    iota(A("KB", p1=1), [[0, 8], [-1, 16]], 15, 0)
+    iota(A("KF"), [[0, 8], [1, 16]], 0, 0)
+    iota(A("GF"), [[1, 8], [0, 16]], 0, 0)
+    ms(A("ONE"), 1.0); ms(A("QROW", p1=1), -0.25); ms(A("PB", 4, 5), 524288.0)
+    cp(A("CF", 0, 1), A("CI", 0, 1))
+    ts(A("CI", 4, 5), A("CI", 0, 1), 15, OP.bitwise_and); cp(A("CF", 4, 5), A("CI", 4, 5))
+    ts(A("ID"), A("IOT", 0, 128), A("CF", 0, 1), OP.is_equal)
+    tt(A("CF", 8, 9), A("CF", 0, 1), A("CF", 4, 5), OP.subtract)
+    ts(A("FI"), A("ID"), 1.5625 / 64, OP.mult); ts(A("NFI"), A("ID"), -1.5625 / 64, OP.mult)
+    ts(A("CF", 12, 13), A("CF", 8, 9), 15.0, OP.add)
+    ts(A("CF", 16, 17), A("CF", 4, 5), 2.0, OP.mult, 1.0, OP.add)
+    for b in range(4):
+        ts(A("CI", 1, 2), A("CI", 4, 5), b, OP.arith_shift_right, 1, OP.bitwise_and)
+        ts(A("PB", 0, 1), A("CI", 1, 2), 2.0 ** -(1 << b) - 1.0, OP.mult, 1.0, OP.add)
+        tt(A("PB", 4, 5), A("PB", 4, 5), A("PB", 0, 1), OP.mult)
+    ts(A("W8"), A("I16"), A("CF", 8, 9), OP.is_equal, A("PB", 4, 5), OP.mult)
+    ts(A("RST"), A("KF"), 0.0, OP.is_equal, -4194304.0, OP.mult)
+    ts(A("LWI"), A("VL"), 1023, OP.bitwise_and)
+    ts(A("B8"), A("I16"), A("CF", 8, 9), OP.is_equal)
+    cp(A("LW"), A("LWI"))
+    ts(A("BM"), A("IOT", 0, 16), A("CF", 4, 5), OP.is_equal)
+    ts(A("OT", 0, 512), A("NB"), 4095, OP.bitwise_and); ts(A("OT", 512, 1024), A("NB"), 12, OP.arith_shift_right)
+    ts(A("O", 0, 512), A("OT", 0, 512), UP, OP.mult, EPS, OP.add); ts(A("O", 512, 1024), A("OT", 512, 1024), UP, OP.mult, EPS, OP.add)
+
+    def og(n, r):
+        s, i = divmod(n, 3)
+        po = A("PO%d" % (n % 4)); l = A("LV%d_%d" % (r, s), 8 * i, 8 * i + 8) if s else A("LW", 8 * i, 8 * i + 8)
+        gather_v(po, A("O", 0, 4112) if s else A("O", 0, 1024), l); tick()
+        ts(A("PF%d" % (n % 4)), po, -2048.0, OP.add)
+
+    def copies():
+        for a in (1024, 2049, 3073):
+            src, d = A("O", 0, 1024), A("O", a, a + 1024)
+            dma("dcp", ap(d), ap(src), "Y", [src], [d])
+
+    def xg(n):
+        x, po, c = "XG%d" % (n % 3), "PO%d" % (n % 4), 128 if n else CUT0
+        gather_s(A(x, 0, 16 * c), A("X"), A(po, 0, c))
+        if c < 128: gather_v(A(x, 16 * c, 2048), A("X"), A(po, c, 128))
+
+    for q in range(8):
+        src, d = A("OT", p0=16 * q, p1=16 * q + 16), A("OX", 128 * q, 128 * q + 128)
+        dma("dox", ap(d), ap(src), "Y", [src], [d])
+    og(0, 0); og(1, 0); xg(0); xg(1); copies()
+    ts(A("DB"), A("IOT"), A("CF", 12, 13), OP.is_equal)
+    ts(A("WU"), A("I16"), A("CF", 8, 9), OP.is_equal, A("CF", 16, 17), OP.mult)
+    ts(A("DUB"), A("IOT"), A("CF", 12, 13), OP.is_equal, A("CF", 16, 17), OP.mult)
+    ts(A("HID"), A("ID"), 0.5, OP.mult); ts(A("NID"), A("ID"), -1.0, OP.mult)
+    ts(A("REP", p1=8), A("GF", p1=8), A("CF", 0, 1, p1=8), OP.is_equal)
+    ts(A("B8B"), A("I16"), A("CF", 8, 9), OP.is_equal)
+    cp(A("IOH"), A("IOT", 0, 128)); ts(A("IOB"), A("IOT", 0, 128), 1.0, OP.add)
+    ts(A("NREP", p1=8), A("REP", p1=8), -45.0, OP.mult)
+    ts(A("ZR", p1=1), A("O", 0, 512, p1=1), 0.0, OP.mult)
+
+    def round_(r):
+        last = r == RO - 1
+
+        def sub(n, b):
+            s, i = divmod(n, 3); d = "D%d" % ((4 * n + b) % 3); z = A("Z%d_%d" % (r, s), 128 * i, 128 * i + 128)
+            for j in range(4):
+                o = A(d, 128 * j, 128 * j + 128)
+                mm(o, A("FI"), A("XG%d" % (n % 3), 4 * b + j, 2048, 16), True, False); mm(o, A("NFI"), z, False, True)
+
+        def near(n, b, h):
+            ts(A("NR%d" % (n % 2), 512 * b + 256 * h, 512 * b + 256 * h + 256), A("D%d" % ((4 * n + b) % 3), 256 * h, 256 * h + 256), MAG, OP.add, MAG, OP.is_equal)
+
+        def tm(n, b):
+            if b == 0: mm(A("KEY", 0, 128), A("ONE", 0, 128, p1=1), A("KB", p1=1), True, False)
+            for k in range(4 * b, 4 * b + 4):
+                mm(A("KEY", k, 128, 16), A("NR%d" % (n % 2), 128 * k, 128 * k + 128), A("W8"), False, k == 15)
+
+        def pa(n, step):
+            s, i = divmod(n, 3); s1 = A("S1_%d" % s, 128 * i, 128 * i + 128); m = A("S1_%d" % s, 128 * i + 15, 128 * i + 128, 16)
+            if step == 0: run("V", [A("RST"), A("KEY", 0, 128)], [s1], lambda: g.vector.tensor_tensor_scan(ap(s1), ap(A("RST")), ap(A("KEY", 0, 128)), 0.0, OP.add, OP.max))
+            elif step == 1:
+                if s == 0: ts(A("MM"), m, THR0, OP.max)
+                else: tt(A("MM"), m, A("FL%d_%d" % (r, s), 8 * i, 8 * i + 8), OP.max)
+            else:
+                for q in range(8):
+                    ts(A("NO%d" % (n % 2), 16 * q, 16 * q + 16), A("KEY", 16 * q, 16 * q + 16), A("MM", q, q + 1), OP.is_ge)
+                mm(A("MI", 0, 128), A("NO%d" % (n % 2)), A("ID"), True, True)
+
+        def pb(n):
+            s, i = divmod(n, 3); sl = "SEL%d" % (n % 2); m = A("S1_%d" % s, 128 * i + 15, 128 * i + 128, 16)
+            tt(A(sl), A("MI", 0, 128), A("PF%d" % (n % 4)), OP.mult)
+            for b in range(16):
+                mm(A("MI", 128, 136), A("DB", 15 - b, 143 - b), A(sl, b, 128, 16), b == 0, b == 15)
+            mm(A("MI", 136, 144), A(sl), A("B8"), True, True)
+            ts(A("QB%d" % s, 8 * i, 8 * i + 8), m, -7.5, OP.add, M16, OP.add)
+            go = A("GO%d_%d" % (r, s), 8 * i, 8 * i + 8)
+            if s == 0: ts(go, m, THR0, OP.is_gt)
+            else: tt(go, m, A("FL%d_%d" % (r, s), 8 * i, 8 * i + 8), OP.is_gt)
+            if s < 2: ts(A("F%d_%d" % (r, s), 8 * i, 8 * i + 8), A("QB%d" % s, 8 * i, 8 * i + 8), M16, OP.subtract, 15.5, OP.add)
+
+        def pc(n):
+            s, i = divmod(n, 3); c = (8 * i, 8 * i + 8)
+            lu = A("LU%d_%d" % (r, s), *c)
+            ts(lu, A("MI", 128, 136), 2048.0, OP.add)
+            if s < 2: send(nxt, A("LV%d_%d" % (r, s + 1), *c), lu, "aV%d_%d_%d" % (r, s + 1, i))
+            act(A("UV%d" % r, *c) if s == 0 else A("VMB%d" % s, *c), A("MI", 136, 144), AF.Copy)
+            if s < 2:
+                send(nxt, A("FL%d_%d" % (r, s + 1), *c), A("F%d_%d" % (r, s), *c), "aF%d_%d_%d" % (r, s + 1, i))
+                zo = A("ZO%d_%d" % (r, s), 128 * i, 128 * i + 128)
+                gather_s(zo, A("X"), lu)
+                send(nxt, A("Z%d_%d" % (r, s + 1), 128 * i, 128 * i + 128), zo, "aZ%d_%d_%d" % (r, s + 1, i))
+            if i == 2:
+                if s == 0: send(nxt, A("UL%d" % r), A("UV%d" % r), "aU%d" % r)
+                else:
+                    send(prv, A("GL%d_%d" % (r, s)), A("GO%d_%d" % (r, s)), "aG%d_%d" % (r, s))
+                    send(T.cores[(rank - s) % N], A("LL%d_%d" % (r, s)), A("LU%d_%d" % (r, s)), "aL%d_%d" % (r, s))
+
+        def codes():
+            def products():
+                for i in range(3):
+                    mm(A("MI", 256 + 8 * i, 264 + 8 * i), A("Z%d_0" % r, 128 * i, 128 * i + 128), A("WU"), True, True)
+                for b in range(16):
+                    mm(A("MI", 288, 312), A("DUB", 15 - b, 143 - b), A("Z%d_0" % r, b, 384, 16), b == 0, b == 15)
+                ts(A("FA0"), A("VL"), -2048.0, OP.add)
+
+            def spread(i, a):
+                ts(A("M0_%d" % i, 16 * a, 16 * a + 16), A("BM"), A("FA0", 8 * i + a, 8 * i + a + 1), OP.mult)
+                if a == 7: mm(A("MI", 320 + 8 * i, 328 + 8 * i), A("M0_%d" % i), A("B8"), True, True)
+            m = [lambda i=i, a=a: spread(i, a) for i in range(3) for a in range(8)]
+            u = [lambda: cp(A("IA"), A("MI", 256, 280)), lambda: tt(A("ID_"), A("MI", 288, 312), A("VL"), OP.add), lambda: ts(A("IB"), A("IA"), 4095, OP.bitwise_and),
+                 lambda: ts(A("IC"), A("ID_"), 4095, OP.bitwise_and),
+                 lambda: ts(A("FB"), A("IB"), 2048.0, OP.is_gt, -4096.0, OP.mult), lambda: tt(A("UV%d" % r, 24, 48), A("IB"), A("FB"), OP.add)]
+            return [products] + m[:8] + weave(u, m[8:]) + [lambda: cp(A("VMB0"), A("MI", 320, 344))]
+
+        def exdig(s):
+            v = A("VMB0") if s == 0 else A("UL%d" % r, 0, 24)
+
+            def xoh(j): return lambda: ts(A("XOH%d" % s, 128 * j, 128 * j + 128), A("IOH"), A("XC%d" % s, j, j + 1), OP.is_equal)
+            return [lambda: ts(A("EA"), v, 2048.0, OP.add, DOWN if s else 1.0, OP.mult), lambda: ts(A("EF"), A("QB%d" % s), M16, OP.subtract, 15.0, OP.add),
+                    lambda: ts(A("EB"), A("EA"), 127, OP.bitwise_and), lambda: tt(A("EG"), A("EF"), A("S1_%d" % s, 15, 384, 16), OP.subtract),
+                    lambda: cp(A("WL%d" % s), A("EB")), lambda: ts(A("EH"), A("EG"), 8.0, OP.mult),
+                    lambda: ts(A("EC"), A("EA"), 7, OP.arith_shift_right, 7, OP.bitwise_and),
+                    lambda: tt(A("XC%d" % s), A("EH"), A("EC"), OP.add)], [xoh(j) for j in range(24)]
+
+        def exmask(s):
+            def um():
+                tt(A("UM%d" % s), A("UV%d" % r, 24, 48) if s == 0 else A("UL%d" % r, 24, 48), A("GL%d_%d" % (r, s + 1)), OP.mult)
+                if s == 0:
+                    for h in range(2): mm(A("EX%d" % h), A("ZR", 0, 128, p1=1), A("ZR", p1=1), True, False)
+
+            def yu(j):
+                q = j % 8; y = A("YU", 128 * j, 128 * j + 128)
+                ts(y, A("IOH"), A("WL%d" % s, j, j + 1), OP.is_equal, A("UM%d" % s, j, j + 1), OP.mult)
+                mm(A("EX%d" % (q // 4), q % 4 * 128, q % 4 * 128 + 128), A("XOH%d" % s, 128 * j, 128 * j + 128), y, False, s == 1 and j in (19, 23))
+            return [um], [lambda j=j: yu(j) for j in range(24)]
+
+        def pendig(s, c0, c1):
+            v = A("UV%d" % r, c0, c1) if s == 0 else A("VMB%d" % s, c0, c1); a, b, c = A("PA", c0, c1), A("PB_", c0, c1), A("PC", c0, c1)
+
+            def lob():
+                ts(A("LOB%d" % s, c0, c1), b, -1.0, OP.mult, -0.5, OP.add)
+                for j in range(c0, c1):
+                    act(A("SG%d" % s, 34 * j, 34 * j + 33), A("IOT", 0, 33), AF.Sign, A("LOB%d" % s, j, j + 1))
+            return [lambda: ts(a, v, 2048.0, OP.add, DOWN, OP.mult), lambda: ts(b, a, 31, OP.bitwise_and), lambda: ts(c, a, 5, OP.arith_shift_right),
+                    lob, lambda: ts(A("HP%d" % s, c0, c1), c, 1.0, OP.add)]
+
+        def penmask(s, c0, c1, first, end):
+            m = A("HM%d" % s, c0, c1); hp = A("HP%d" % s, c0, c1); go = A("GO%d_%d" % (r, s), c0, c1)
+
+            def hoh(j):
+                q = j % 8; h = A("HOH", 128 * j, 128 * j + 128)
+                if first and j == c0: mm(A("PEN", 0, 264), A("ZR", 0, 128, p1=1), A("ZR", 0, 264, p1=1), True, False)
+                ts(h, A("IOB"), A("HM%d" % s, j, j + 1), OP.is_equal)
+                mm(A("PEN", 33 * q, 33 * q + 33), h, A("SG%d" % s, 34 * j, 34 * j + 33), False, end and j == 23)
+            if s < 2: pre = [lambda: tt(A("FC%d" % s, c0, c1), go, A("GL%d_%d" % (r, s + 1), c0, c1), OP.subtract), lambda: tt(m, hp, A("FC%d" % s, c0, c1), OP.mult)]
+            else: pre = [lambda: tt(m, hp, go, OP.mult)]
+            return pre, [lambda j=j: hoh(j) for j in range(c0, c1)]
+
+        def settle():
+            def alive(s): return lambda: ts(A("AL", 24 * s - 24, 24 * s), A("LV%d_%d" % (r, s)), 2048.0, OP.not_equal)
+
+            def m1():
+                cp(A("AC"), A("AR"))
+                for i in range(3): mm(A("MI", 352, 353, p1=8), A("QT", 8 * i, 8 * i + 8), A("ONE", 0, 1), i == 0, False)
+                mm(A("MI", 352, 353, p1=8), A("B8B"), A("AC"), False, True)
+
+            def m2():
+                cp(A("AB", p1=8), A("AJ", p1=8))
+                mm(A("MI", 360, 361), A("REP", p1=8), A("AB", p1=8), True, True)
+            return [lambda: ts(A("QA"), A("GO%d_0" % r), -1.0, OP.mult, 1.0, OP.add), alive(1), alive(2),
+                lambda: tt(A("QT"), A("QA"), A("GO%d_1" % r), OP.subtract),
+                lambda: run("V", [A("AL")], [A("AR")], lambda: g.vector.tensor_reduce(ap(A("AR")), ap(A("AL")), AxisListType.X, OP.add)),
+                m1], [lambda: cp(A("AI", p1=8), A("MI", 352, 353, p1=8)), lambda: ts(A("AJ", p1=8), A("AI", p1=8), 3, OP.bitwise_and), m2], [
+                lambda: ts(A("FCOL"), A("MI", 360, 361), -0.0625 / 64, OP.mult, 1.5625 / 64, OP.add)]
+
+        def boats():
+            o = [lambda: cp(A("FA"), A("IC"))]
+            for lu in (A("LU%d_0" % r), A("LL%d_1" % r), A("LL%d_2" % r)):
+                o += [lambda lu=lu: ts(A("BI"), lu, DOWN, OP.mult), lambda lu=lu: ts(A("BB"), lu, 2048.0, OP.is_equal), lambda: tt(A("BC"), A("FA"), A("BI"), OP.subtract),
+                      lambda: tt(A("BD"), A("BC"), A("BB"), OP.mult), lambda: tt(A("FA"), A("BD"), A("BI"), OP.add)]
+            if last: return o + [lambda: dma("oyv", T.yv[:, :], ap(A("FA")), "Y", [A("FA")], [])]
+            return o + [lambda: cp(A("VL"), A("FA")), lambda: ts(A("LWI"), A("VL"), 1023, OP.bitwise_and), lambda: cp(A("LW"), A("LWI"))]
+
+        z0, z1, zn, y = A("Z%d_0" % r), A("ZO%d_0" % r), A("Z%d_0" % (r + 1)) if not last else A("RD"), A("PEN", 0, 384)
+
+        def own(part):
+            if part == 0:
+                mm(y, A("HID"), z0, True, False); mm(y, A("HID"), z1, False, False); mm(y, A("QROW", p1=1), A("ONE", p1=1), False, True)
+                ts(A("RN"), z1, 256.0, OP.is_ge)
+                act(A("RY"), y, AF.Copy, MAG); act(A("RB"), A("RY"), AF.Copy, -MAG)
+            if part == 1:
+                mm(y, A("ID"), z0, True, False); mm(y, A("NID"), A("RB"), False, True)
+                tt(A("RE"), y, A("RN"), OP.mult)
+            if part == 2:
+                mm(y, A("ID"), A("RE"), True, False); mm(y, A("ID"), A("RB"), False, True)
+                act(zn, y, AF.Copy)
+                if last: dma("oyv", T.yz[:, :], ap(zn), "Y", [zn], [])
+
+        fq.extend(codes())
+        for n in range(9):
+            s, i = divmod(n, 3)
+            if i == 0 and n:
+                if n == 3: tick(999)
+                pa(n - 1, 0); tick(2); pa(n - 1, 1); tick(2); pa(n - 1, 2); tick(4); pb(n - 1); tick(8); pc(n - 1)
+                og(n + 1, r); xg(n + 1)
+                e, x = exdig(s - 1)
+                fq.extend(weave(e, pendig(s - 1, 0, 24)))
+                if s == 2 and not last:
+                    c0, c1, c2 = settle()
+                    x = weave(x[:6], c0) + x[6:16] + weave(x[16:19], c1) + x[19:] + c2
+                fq.extend(x)
+            sub(n, 0); sub(n, 1); sub(n, 2)
+            if i == 0 and n: tick(8)
+            if n == 7:
+                e, x = penmask(0, 0, 24, True, False); e2, x2 = exmask(0)
+                fq.extend(e[:1] + e2 + e[1:] + x + x2)
+            for b in range(4):
+                near(n, b, 0)
+                if i and b == 0: pa(n - 1, 0)
+                if i and b == 1: pa(n - 1, 2)
+                near(n, b, 1)
+                if b == 0: sub(n, 3)
+                if i and b == 0: pa(n - 1, 1)
+                if b == 1: tm(n, 0)
+                if i and b == 1: tick(2); pb(n - 1)
+                if i and b == 2: pc(n - 1)
+                if b: tm(n, b)
+                if b == 2:
+                    if i == 0: og(n + 2, r); xg(n + 2)
+                    if i == 2 and n < 8: og(n + 1, r); xg(n + 1)
+                tick(3)
+            if n in (3, 5, 6): own((3, 5, 6).index(n))
+        e, x = penmask(2, 0, 16, False, False)
+        fq.extend(pendig(2, 0, 16) + e + x)
+        pa(8, 0); tick(2); pa(8, 1); tick(2); pa(8, 2); tick(5); pb(8); tick(8); pc(8)
+        if not last: fq.extend([lambda: ts(A("FI"), A("ID"), A("FCOL"), OP.mult), lambda: ts(A("NFI"), A("ID"), A("FCOL"), OP.mult, -1.0, OP.mult)])
+        d = pendig(2, 16, 24); e, x = penmask(2, 16, 24, False, False); e1, x1 = penmask(1, 0, 24, False, True); e2, x2 = exmask(1)
+        tick(4); fq.extend(d); tick(10); fq.extend(e + x + e1[:1] + e2 + e1[1:] + x1); tick(999)
+        act(A("HC0"), A("PEN", 0, 264), AF.Copy)
+        fq.extend(x2); tick(8)
+        tt(A("HC", 0, 263), A("HC0", 1, 264), A("HC0", 0, 263), OP.is_gt)
+        for q in range(8):
+            src, d = A("HC", 33 * q, 33 * q + 32), A("HS", p0=q, p1=q + 1)
+            dma("dhs", ap(d), ap(src), "YS"[q % 2], [src], [d])
+        tick(999)
+        fq.extend(boats())
+        for h in range(2):
+            c = (512 * h, 512 * h + 512)
+            tick(2); tt(A("OT", *c), A("EX%d" % h), A("OX", *c), OP.add); tick(1); ts(A("OX", *c), A("OT", *c), 4095, OP.bitwise_and)
+            if not last: tick(1); ts(A("OE", *c), A("OX", *c), UP, OP.mult, EPS, OP.add)
+            for q in range(4 * h, 4 * h + 4):
+                src, d = A("OX" if last else "OE", 128 * q, 128 * q + 128), A("O", 0, 1024, p0=16 * q, p1=16 * q + 16)
+                dma("dex", ap(d), ap(src), "Y", [src], [d])
+        for c in range(8):
+            d = A("D%d" % (c % 3)); x = A("X", 512 * c + c // 4, 512 * c + c // 4 + 512)
+            mm(d, A("ID"), x, True, False); mm(d, A("NREP", p1=8), A("HS", 512 * c, 512 * c + 512, p1=8), False, True)
+            if c in (3, 5, 7): tick(3); ts(x, d, 0.0, OP.max)
+            else: act(x, d, AF.Relu)
+            if last: dma("oyx%d" % (c % 2), T.yx[:, 512 * c:512 * c + 512], ap(x), "Y", [x], [])
+        tick(999)
+        if last:
+            ts(A("EXS"), A("O", 512, 1024), 4096.0, OP.mult); tt(A("YN"), A("EXS"), A("O", 0, 512), OP.add)
+            dma("oyn", T.yn[:, :], ap(A("YN")), "Y", [A("YN")], [])
+        else: og(0, r + 1); og(1, r + 1); xg(0); xg(1); copies()
+
+    for r in range(RO):
+        round_(r)
+    for sem in cnt:
+        if known["G"].get(sem, 0) < cnt[sem]: g.wait_ge(T.sem[sem], cnt[sem])

@@ -1,9 +1,12 @@
 from concourse.mybir import dt, AluOpType as OP, ActivationFunctionType as AF, AxisListType
 
 RO, ST, NCH = 2, 3, 3
-CUT0 = 72
 BS = {"float32": 4, "int32": 4, "bfloat16": 2, "float16": 2, "uint16": 2}
 SCRATCH, ALIAS, POOL = {}, {}, {}
+REVERSE = True
+ZT_ON = "S"
+V_QUARTERS = {(0, 1), (0, 3), (1, 2)}
+RELU_V = (1, 3, 5, 7)
 
 
 def _b(names, cols, dtype, where="sbuf"):
@@ -17,42 +20,101 @@ def _s(names, cols, dtype):
         ALIAS[n] = ("pool_" + dtype, o, cols); POOL[dtype] = o + (cols + w - 1) // w * w
 
 
-_b("X", 4112, "bfloat16"); _b("O", 4112, "int32"); _b("OX OT OE", 1024, "int32"); _b("NB", 512, "int32"); _b("YN EXS", 512, "float32")
-_b("XG0 XG1 XG2 NR0 NR1", 2048, "bfloat16"); _b("PO0 PO1 PO2 PO3", 128, "uint16"); _b("PF0 PF1 PF2 PF3 SEL0 SEL1 M0_0 M0_1 M0_2 IOH", 128, "float16")
-_b("D0 D1 D2 KEY MI EX0 EX1 PEN", 512, "float32", "psum"); _b("NO0 NO1", 128, "bfloat16")
-_b("S1_0 S1_1 S1_2", 384, "float32"); _b("SG0 SG1 SG2", 24 * 34, "bfloat16"); _b("XOH0 XOH1 YU", 24 * 128, "float16"); _b("HOH", 24 * 128, "bfloat16")
-_s("VMB0 VMB1 VMB2 QB0 QB1 QB2 LOB0 LOB1 LOB2 HP0 HP1 HP2 XC0 XC1 WL0 WL1 FA0 FA FB BB BC BD EF EG EH HM0 HM1 HM2 FC0 FC1 UM0 UM1 CF", 24, "float32")
-_s("VL IA IB IC ID_ LWI BI EA EB EC PA PB_ PC", 24, "int32"); _s("LW", 24, "uint16"); _s("MM PB I16", 8, "float32"); _s("QA QT", 24, "bfloat16")
+_b("X", 4112, "bfloat16"); _b("O", 4112, "int32"); _b("OT OM", 1024, "int32"); _b("NB", 512, "int32"); _b("YN YH", 512, "float32")
+_b("XG0 XG1 XG2 NR0 NR1 IR", 2048, "bfloat16"); _b("SELC", 2048, "float16"); _b("WA", 2048, "bfloat16")
+_b("PO0 PO1 PO2 PO3", 128, "uint16"); _b("PI0 PI1", 128, "int32"); _b("PF0 PF1 PF2 PF3 SEL0 SEL1 ZT0 ZT1 IOH ID16 NID16", 128, "float16")
+_b("D0 D1 D2 KEY MI EX0 EX1 PEN", 512, "float32", "psum"); _b("NO0 NO1", 128, "bfloat16"); _b("MB ID32 RST KF GF IOT", 128, "float32")
+_b("S1_0 S1_1 S1_2 WG RY", 384, "float32"); _b("SG0 SG1 SG2", 24 * 34, "bfloat16")
+_b("YL0 YL1 YU0 YU1", 24 * 128, "float16"); _b("HOH0 HOH1 HOH2", 24 * 128, "bfloat16")
+_b("IW EXS", 1024, "float32"); _b("C16", 264, "float16"); _b("HT", 256, "bfloat16"); _b("ZR", 512, "float16")
+_s("VMB1 VMB2 LOB0 LOB1 LOB2 HP0 HP1 HP2 XC0 XC1 WL0 WL1 W0 FA BB BC BD EG EH FC0 FC1 UM0 UM1 UT CF", 24, "float32")
+_s("VL ID_ IC LWI BI EA EB EC PA PB_ PC", 24, "int32"); _s("LW", 24, "uint16"); _s("PB I16 B1", 8, "float32")
 for _r in range(RO):
     for _i in range(3):
         _b("Z%d_%d" % (_r, _i), 384, "bfloat16")
         _s("GO%d_%d" % (_r, _i), 24, "float32"); _s("LU%d_%d" % (_r, _i), 24, "uint16")
         if _i < 2:
-            _s("F%d_%d" % (_r, _i), 24, "float32"); _b("ZO%d_%d" % (_r, _i), 384, "bfloat16")
+            _s("F%d_%d" % (_r, _i), 24, "int32"); _b("ZO%d_%d" % (_r, _i), 384, "bfloat16")
         if _i > 0:
-            _s("FL%d_%d GL%d_%d" % (_r, _i, _r, _i), 24, "float32"); _s("LV%d_%d LL%d_%d" % (_r, _i, _r, _i), 24, "uint16")
-    _s("UV%d UL%d" % (_r, _r), 48, "float32")
-_b("HC0", 264, "float32"); _b("HC", 264, "bfloat16"); _b("HS", 4096, "bfloat16")
-_b("RY", 384, "float32"); _b("RB RN RE RD ONE", 384, "bfloat16")
-_b("IOT", 144, "float32"); _b("IOB ID HID NID FI NFI REP NREP KB QROW", 128, "bfloat16"); _s("CI", 8, "int32")
-_s("W8 WU B8B", 8, "bfloat16"); _s("B8", 8, "float16"); _s("BM", 16, "float16"); _b("DB", 144, "float16"); _b("DUB", 144, "bfloat16")
-_b("RST KF GF", 128, "float32"); _b("ZR", 512, "float16")
-_s("AL", 48, "float32"); _s("AR FCOL", 1, "float32"); _s("AC AB", 1, "bfloat16"); _s("AI AJ", 1, "int32")
+            _s("GL%d_%d" % (_r, _i), 24, "float32"); _s("FL%d_%d" % (_r, _i), 24, "int32"); _s("LV%d_%d LL%d_%d" % (_r, _i, _r, _i), 24, "uint16")
+    _s("U%d UL%d VMB0_%d ML%d" % (_r, _r, _r, _r), 24, "float32")
+_b("RB RD ONE", 384, "bfloat16")
+_b("IOB ID HID NID FI NFI BD16 KB QROW GROW RP8", 128, "bfloat16"); _s("CI", 8, "int32")
+_s("W8 WU", 8, "bfloat16"); _s("B8", 8, "float16"); _b("DB", 144, "float16"); _b("DUB", 144, "bfloat16"); _b("IO144", 144, "float32")
+_s("AL", 96, "float32"); _s("AR FCOL", 1, "float32"); _s("AC", 1, "bfloat16"); _s("AI AJ", 1, "int32")
 for _d in POOL:
     _b("pool_" + _d, POOL[_d], _d)
 
-SEMAPHORES = ["V", "S", "P", "G", "ls", "dnb", "dv", "dz", "dx0", "dx1", "dx2", "dx3", "dhs", "dex", "dox", "dcp", "oyx0", "oyx1", "oyn", "oyv"]
+SEMAPHORES = ["V", "S", "P", "G", "ls", "dnb", "dv", "dz", "dx0", "dx1", "dx2", "dx3", "dcp0", "dcp1", "oyx", "oyn", "oyv", "oyz"]
 for _r in range(RO):
     for _j in (1, 2):
         for _i in range(NCH):
             SEMAPHORES += ["aF%d_%d_%d" % (_r, _j, _i), "aV%d_%d_%d" % (_r, _j, _i), "aZ%d_%d_%d" % (_r, _j, _i)]
-        SEMAPHORES += ["aG%d_%d" % (_r, _j), "aL%d_%d" % (_r, _j)]
-    SEMAPHORES += ["aU%d" % _r]
+        SEMAPHORES += ["aL%d_%d" % (_r, _j)]
+    SEMAPHORES += ["aU%d" % _r, "aM%d" % _r, "aG%d_1" % _r, "aG%d_2a" % _r, "aG%d_2b" % _r]
 
 MAG = 12582912.0
-M16 = 201326592.0
+M4096 = MAG * 4096
 UP, DOWN, EPS = 4097 / 4096, 4095 / 4096, 0.00015
-THR0 = 16.0 * (34816 + 1) - 0.5
+T0 = 34816.0
+CY, PCY, GCY, LAT, HOP, DMA0, DMAB = 0.83, 0.42, 1.56 * 0.83, 120.0, 2200.0, 1500.0, 190.0
+
+
+def A(name, c0=0, c1=None, step=1, p0=0, p1=128):
+    if name in ALIAS:
+        n, o, w = ALIAS[name]
+        return (n, o + c0, o + (w if c1 is None else c1), step, p0, p1)
+    return (name, c0, SCRATCH[name][1][1] if c1 is None else c1, step, p0, p1)
+
+
+def psum(a): return SCRATCH[a[0]][0] == "psum"
+def width(a): return len(range(a[1], a[2], abs(a[3])))
+def two(*l): return all(BS[SCRATCH[a[0]][2]] == 2 for a in l)
+def span(a): w = BS[SCRATCH[a[0]][2]]; return (a[4], a[5], a[1] * w, a[2] * w)
+
+
+def meet(s, t, b):
+    return s[0] < t[1] and t[0] < s[1] and s[2] // b * b < -(-t[3] // b) * b and t[2] // b * b < -(-s[3] // b) * b
+
+
+def schedule(ops):
+    n = len(ops); deps = [dict() for _ in ops]; acc = {}
+    for i, (q, c, d, reads, writes, _) in enumerate(ops):
+        dmai = q in "YG" and d > c + LAT
+        for lst, w in ((reads, False), (writes, True)):
+            for a in lst:
+                s = span(a)
+                for (t, ow, j, dmaj) in acc.get(a[0], []):
+                    if j != i and (ow or w) and meet(s, t, 16 if ow and w and dmai != dmaj else 1):
+                        deps[i][j] = ops[j][1] if ops[j][0] == q == "P" and psum(a) and j not in deps[i] else ops[j][2]
+        for a in writes:
+            s = span(a); acc[a[0]] = [r for r in acc.get(a[0], []) if not (s[0] <= r[0][0] and r[0][1] <= s[1] and s[2] <= r[0][2] and r[0][3] <= s[3])]
+        for lst, w in ((reads, False), (writes, True)):
+            for a in lst: acc.setdefault(a[0], []).append((span(a), w, i, dmai))
+    succ = [[] for _ in ops]; way = [0.0] * n
+    for i in range(n):
+        for j in deps[i]: succ[j].append(i)
+    for i in range(n - 1, -1, -1): way[i] = max([ops[i][2]] + [deps[k][i] + way[k] for k in succ[i]])
+    left = [len(d) for d in deps]; at = [0.0] * n; ready = {q: [] for q in "VSPGY"}; free = {q: 0.0 for q in ready}; bank = {}; order = []
+    banks = [set(a[0] for a in o[3] + o[4] if psum(a)) for o in ops]
+    for i in range(n):
+        if not left[i]: ready[ops[i][0]].append(i)
+    while len(order) < n:
+        best = None
+        for q in ready:
+            for i in ready[q]:
+                t = max([free[q], at[i]] + [bank[b][1] for b in banks[i] if b in bank and bank[b][0] != q])
+                if best is None or (t, -way[i]) < best[:2]: best = (t, -way[i], i)
+        t, _, i = best; q = ops[i][0]
+        ready[q].remove(i); order.append(i); free[q] = t + ops[i][1]
+        for b in banks[i]: bank[b] = (q, t + ops[i][2])
+        for k in succ[i]:
+            at[k] = max(at[k], t + deps[k][i]); left[k] -= 1
+            if not left[k]: ready[ops[k][0]].append(k)
+    return order
+
+
+ORDER = []
 
 
 def rank_program(g, core, T, topo):
@@ -63,21 +125,14 @@ def rank_program(g, core, T, topo):
     nxt, prv = T.cores[(rank + 1) % N], T.cores[(rank - 1) % N]
     eng = {"V": g.vector, "S": g.scalar, "P": g.tensor, "G": g, "Y": g.sync}
     cnt, snap, acc, known = {}, {}, {}, {q: {} for q in eng}
-
-    def A(name, c0=0, c1=None, step=1, p0=0, p1=128):
-        if name in ALIAS:
-            n, o, w = ALIAS[name]
-            return (n, o + c0, o + (w if c1 is None else c1), step, p0, p1)
-        return (name, c0, SCRATCH[name][1][1] if c1 is None else c1, step, p0, p1)
+    ops = []
 
     def ap(a):
         t = T[a[0]]
+        if a[3] < 0: return t[a[4]:a[5], a[2] - 1:(a[1] - 1 if a[1] else None):a[3]]
         return t[a[4]:a[5], a[1]:a[2]] if a[3] == 1 else t[a[4]:a[5], a[1]:a[2]:a[3]]
 
-    def span(a):
-        w = BS[SCRATCH[a[0]][2]]
-        if SCRATCH[a[0]][0] == "psum": return (0, 128, 0, 2048)
-        return (a[4], a[5], a[1] * w, a[2] * w)
+    def bankspan(a): return (0, 128, 0, 2048) if psum(a) else span(a)
 
     def learn(q, comp, n):
         k = known[q]
@@ -90,10 +145,9 @@ def rank_program(g, core, T, topo):
         need = {}
         for lst, w in ((reads, False), (writes, True)):
             for a in lst:
-                ps = SCRATCH[a[0]][0] == "psum"; s = span(a)
+                ps = psum(a); s = bankspan(a)
                 for (t, ow, oc, on, oq) in acc.get(a[0], []):
-                    b = 16 if ow and w and (oc in eng) != (comp in eng) else 1
-                    if not (s[0] < t[1] and t[0] < s[1] and s[2] // b * b < -(-t[3] // b) * b and t[2] // b * b < -(-s[3] // b) * b): continue
+                    if not meet(s, t, 16 if ow and w and (oc in eng) != (comp in eng) else 1): continue
                     if ps:
                         if oq == q and oc == comp and (q == "P" or not (ow or w)): continue
                     elif not (ow or w): continue
@@ -105,382 +159,313 @@ def rank_program(g, core, T, topo):
 
     def note(q, comp, n, reads, writes):
         for a in writes:
-            s = span(a); ps = SCRATCH[a[0]][0] == "psum"
-            if not ps: acc[a[0]] = [r for r in acc.get(a[0], []) if not (s[0] <= r[0][0] and r[0][1] <= s[1] and s[2] <= r[0][2] and r[0][3] <= s[3])]
+            s = bankspan(a)
+            if not psum(a): acc[a[0]] = [r for r in acc.get(a[0], []) if not (s[0] <= r[0][0] and r[0][1] <= s[1] and s[2] <= r[0][2] and r[0][3] <= s[3])]
         for lst, w in ((reads, False), (writes, True)):
             for a in lst:
-                s = span(a)
-                l = [r for r in acc.setdefault(a[0], []) if not (r[0] == s and r[1] == w and r[2] == comp and r[4] == q)]
-                acc[a[0]] = l + [(s, w, comp, n, q)]
+                s = bankspan(a)
+                acc[a[0]] = [r for r in acc.get(a[0], []) if not (r[0] == s and r[1] == w and r[2] == comp and r[4] == q)] + [(s, w, comp, n, q)]
 
-    def run(q, reads, writes, call):
+    def issue(q, reads, writes, call):
         hazards(q, q, reads, writes)
         i = call(); cnt[q] = cnt.get(q, 0) + 1
         i.then_inc(T.sem[q], 1)
         snap[(q, cnt[q])] = dict(known[q])
         note(q, q, cnt[q], reads, writes)
 
-    def dma(sem, out, in_, q="Y", reads=(), writes=()):
-        hazards(q, sem, reads, writes)
-        eng[q].dma_start(out, in_).then_inc(T.sem[sem], 16)
-        cnt[sem] = cnt.get(sem, 0) + 16
-        snap[(sem, cnt[sem])] = dict(known[q])
-        note(q, sem, cnt[sem], reads, writes)
+    group = []
 
-    def send(dst, out, in_, sem):
-        hazards("G", "ls", [in_], [])
-        rid, pid, _ = topo.addr(dst)
-        g.remote_dma(ap(out), ap(in_), T.sem[sem], T.sem["ls"], pid, rid, topo.mask(core, dst))
-        cnt["ls"] = cnt.get("ls", 0) + len(topo.engines(core, dst))
+    def run(q, cost, reads, writes, call):
+        if group: group[0].append((cost, reads, writes, call))
+        else: ops.append((q, cost, cost + LAT, reads, writes, lambda: issue(q, reads, writes, call)))
 
-    def arrives(sem, a, src):
-        cnt[sem] = len(topo.engines(src, core)); note("R", sem, cnt[sem], [], [a])
+    def together(f):
+        group.append([]); f(); l = group.pop()
+        c = sum(x[0] for x in l)
+        ops.append(("P", c, c + LAT, [a for x in l for a in x[1]], [a for x in l for a in x[2]], lambda: [issue("P", x[1], x[2], x[3]) for x in l]))
+
+    def dma(sem, out, in_, size, q="Y", reads=(), writes=(), after=0.0):
+        def f():
+            hazards(q, sem, reads, writes)
+            eng[q].dma_start(out, in_).then_inc(T.sem[sem], 16)
+            cnt[sem] = cnt.get(sem, 0) + 16
+            snap[(sem, cnt[sem])] = dict(known[q])
+            note(q, sem, cnt[sem], reads, writes)
+        ops.append((q, 50.0, DMA0 + (after + size) / DMAB, list(reads), list(writes), f))
+
+    def send(step, out, in_, sem):
+        dst, src = T.cores[(rank + step) % N], T.cores[(rank - step) % N]
+        cnt[sem] = len(topo.engines(src, core)); note("R", sem, cnt[sem], [], [out])
+
+        def f():
+            hazards("G", "ls", [in_], [])
+            rid, pid, _ = topo.addr(dst)
+            g.remote_dma(ap(out), ap(in_), T.sem[sem], T.sem["ls"], pid, rid, topo.mask(core, dst))
+            cnt["ls"] = cnt.get("ls", 0) + len(topo.engines(core, dst))
+        ops.append(("G", 150.0, HOP, [in_], [out], f))
 
     def col(x):
         return (ap(x), [x]) if isinstance(x, tuple) else (x, [])
 
-    def ts(out, in0, s1, op0, s2=None, op1=None):
-        v1, r1 = col(s1); v2, r2 = col(s2)
-        if op1 is None: run("V", [in0] + r1, [out], lambda: g.vector.tensor_scalar(ap(out), ap(in0), v1, None, op0))
-        else: run("V", [in0] + r1 + r2, [out], lambda: g.vector.tensor_scalar(ap(out), ap(in0), v1, v2, op0, op1))
+    def vc(n, *sides): return CY * max(64, n / 2 if two(*sides) else n)
+
+    def ts(out, in0, s1, op0, s2=None, op1=None, off=None):
+        v1, r1 = col(s1); v2, r2 = col(s2); tail = (op0,) if op1 is None else (op0, op1)
+        if off: run("V", 50 + 16 * width(off) * GCY, [in0, off], [out], lambda: g.vector.tensor_scalar(ap(out), ap(in0).indirect(ap(off)), v1, v2, *tail))
+        else: run("V", vc(width(out), out, in0), [in0] + r1 + r2, [out], lambda: g.vector.tensor_scalar(ap(out), ap(in0), v1, v2, *tail))
 
     def tt(out, a, b, op):
-        run("V", [a, b], [out], lambda: g.vector.tensor_tensor(ap(out), ap(a), ap(b), op))
+        run("V", CY * max(64, width(out) * (1 if psum(a) or psum(b) else 2)), [a, b], [out], lambda: g.vector.tensor_tensor(ap(out), ap(a), ap(b), op))
+
+    def scan(out, a, b):
+        run("V", vc(width(out), out, a, b), [a, b], [out], lambda: g.vector.tensor_tensor_scan(ap(out), ap(a), ap(b), 0.0, OP.add, OP.max))
 
     def cp(out, a):
-        run("V", [a], [out], lambda: g.vector.tensor_copy(ap(out), ap(a)))
+        run("V", vc(width(out), out, a), [a], [out], lambda: g.vector.tensor_copy(ap(out), ap(a)))
 
     def ms(out, c):
-        run("V", [], [out], lambda: g.vector.memset(ap(out), c))
+        run("V", vc(width(out), out), [], [out], lambda: g.vector.memset(ap(out), c))
 
-    def mm(out, l, r, start, stop):
-        run("P", [l, r], [out], lambda: g.tensor.matmul(ap(out), ap(l), ap(r), start, stop))
+    def mm(out, l, r, start, stop, whole=False):
+        c = PCY * max(min(64, width(l)), width(r)) * (4 if SCRATCH[l[0]][2] == "float32" else 1)
+        run("P", c, [l, r], [A(out[0]) if whole else out], lambda: g.tensor.matmul(ap(out), ap(l), ap(r), start, stop))
 
-    def act(out, a, f, bias=None):
-        v, r = col(bias)
-        if bias is None: run("S", [a], [out], lambda: g.scalar.activation(ap(out), ap(a), f))
-        else: run("S", [a] + r, [out], lambda: g.scalar.activation(ap(out), ap(a), f, bias=v))
+    def act(out, a, f, bias=0.0, scale=1.0):
+        v, r = col(bias); v2, r2 = col(scale)
+        run("S", CY * max(64, width(out)), [a] + r + r2, [out], lambda: g.scalar.activation(ap(out), ap(a), f, bias=v, scale=v2))
 
-    def gather_v(out, win, off):
-        run("V", [win, off], [out], lambda: g.vector.tensor_copy(ap(out), ap(win).indirect(ap(off))))
-
-    def gather_s(out, win, off):
-        run("S", [win, off], [out], lambda: g.scalar.activation(ap(out), ap(win).indirect(ap(off)), AF.Copy))
+    def gather(q, out, win, off):
+        if q == "V": run("V", 50 + 16 * width(off) * GCY, [win, off], [out], lambda: g.vector.tensor_copy(ap(out), ap(win).indirect(ap(off))))
+        else: run("S", 65 + 16 * width(off) * GCY, [win, off], [out], lambda: g.scalar.activation(ap(out), ap(win).indirect(ap(off)), AF.Copy))
 
     def iota(out, pat, base, cm, flag=True):
-        if flag: run("G", [], [out], lambda: g.iota(ap(out), pat, base, cm, allow_small_or_imprecise_dtypes=True))
-        else: run("G", [], [out], lambda: g.iota(ap(out), pat, base, cm))
+        c = 130 + 2 * CY * width(out)
+        if flag: run("G", c, [], [out], lambda: g.iota(ap(out), pat, base, cm, allow_small_or_imprecise_dtypes=True))
+        else: run("G", c, [], [out], lambda: g.iota(ap(out), pat, base, cm))
 
-    fq = []
-
-    def tick(k=1):
-        while fq and k: fq.pop(0)(); k -= 1
-
-    def weave(a, b):
-        o = []
-        for i in range(max(len(a), len(b))): o += a[i:i + 1] + b[i:i + 1]
-        return o
-
-    for r in range(RO):
-        for s in (1, 2):
-            for i in range(NCH):
-                arrives("aF%d_%d_%d" % (r, s, i), A("FL%d_%d" % (r, s), 8 * i, 8 * i + 8), prv)
-                arrives("aV%d_%d_%d" % (r, s, i), A("LV%d_%d" % (r, s), 8 * i, 8 * i + 8), prv)
-                arrives("aZ%d_%d_%d" % (r, s, i), A("Z%d_%d" % (r, s), 128 * i, 128 * i + 128), prv)
-            arrives("aG%d_%d" % (r, s), A("GL%d_%d" % (r, s)), nxt)
-            arrives("aL%d_%d" % (r, s), A("LL%d_%d" % (r, s)), T.cores[(rank + s) % N])
-        arrives("aU%d" % r, A("UL%d" % r), prv)
+    def xcol(b): return b + b // 2048
 
     ms(A("X", 2048, 2049), 512.0); ms(A("X", 4097, 4112), 512.0); ms(A("O", 2048, 2049), 0); ms(A("O", 4097, 4112), 0)
-    dma("dnb", ap(A("NB")), T.nb[:, :], "Y", [], [A("NB")])
-    dma("dv", ap(A("VL")), T.v[:, :], "S", [], [A("VL")])
+    dma("dv", ap(A("VL")), T.v[:, :], 1 << 14, "S", [], [A("VL")])
+    dma("dnb", ap(A("NB")), T.nb[:, :], 1 << 18, "Y", [], [A("NB")])
     for i in range(4):
-        a = A("X", 1024 * i + i // 2, 1024 * i + i // 2 + 1024)
-        dma("dx%d" % i, ap(a), T.tracks[:, 1024 * i:1024 * i + 1024], "YS"[i % 2], [], [a])
-    dma("dz", ap(A("Z0_0")), T.z[:, :], "Y", [], [A("Z0_0")])
-    iota(A("CI", 0, 1), [[1, 1]], 0, 1, False)
-    iota(A("IOT"), [[1, 144]], 0, 0)
-    iota(A("I16"), [[16, 8]], 0, 0)
-    iota(A("KB", p1=1), [[0, 8], [-1, 16]], 15, 0)
-    iota(A("KF"), [[0, 8], [1, 16]], 0, 0)
-    iota(A("GF"), [[1, 8], [0, 16]], 0, 0)
-    ms(A("ONE"), 1.0); ms(A("QROW", p1=1), -0.25); ms(A("PB", 4, 5), 524288.0)
-    cp(A("CF", 0, 1), A("CI", 0, 1))
-    ts(A("CI", 4, 5), A("CI", 0, 1), 15, OP.bitwise_and); cp(A("CF", 4, 5), A("CI", 4, 5))
-    ts(A("ID"), A("IOT", 0, 128), A("CF", 0, 1), OP.is_equal)
-    tt(A("CF", 8, 9), A("CF", 0, 1), A("CF", 4, 5), OP.subtract)
-    ts(A("FI"), A("ID"), 1.5625 / 64, OP.mult); ts(A("NFI"), A("ID"), -1.5625 / 64, OP.mult)
-    ts(A("CF", 12, 13), A("CF", 8, 9), 15.0, OP.add)
-    ts(A("CF", 16, 17), A("CF", 4, 5), 2.0, OP.mult, 1.0, OP.add)
+        a = A("X", xcol(1024 * i), xcol(1024 * i) + 1024)
+        dma("dx%d" % i, ap(a), T.tracks[:, 1024 * i:1024 * i + 1024], 1 << 18, "Y", [], [a], (i + 1) << 18)
+    dma("dz", ap(A("Z0_0")), T.z[:, :], 3 << 15, "S", [], [A("Z0_0")], 1 << 18)
+    iota(A("CI", 0, 1), [[1, 1]], 0, 1, False); iota(A("IO144"), [[1, 144]], 0, 0); iota(A("I16"), [[16, 8]], 0, 0)
+    iota(A("KB", p1=1), [[0, 8], [1, 16]], 0, 0); iota(A("KF"), [[0, 8], [1, 16]], 0, 0); iota(A("GF"), [[1, 8], [0, 16]], 0, 0)
+    iota(A("IR"), [[1, 128], [0, 16]], 0, 0); iota(A("IW"), [[1, 1024]], 0, 0)
+    io, part, p16, g16 = A("IO144", 0, 128), A("CF", 0, 1), A("CF", 4, 5), A("CF", 8, 9)
+    ms(A("ONE"), 1.0); ms(A("QROW", p1=1), -0.25); ms(A("GROW", p1=1), 512.0); ms(A("PB", 4, 5), 32768.0)
+    cp(part, A("CI", 0, 1))
+    ts(A("CI", 4, 5), A("CI", 0, 1), 15, OP.bitwise_and); cp(p16, A("CI", 4, 5)); tt(g16, part, p16, OP.subtract)
+    ts(A("ID"), io, part, OP.is_equal)
+    ts(A("FI"), A("ID"), 25 / 1024, OP.mult); ts(A("NFI"), A("ID"), -25 / 1024, OP.mult)
+    ts(A("CF", 12, 13), g16, 15.0, OP.add); ts(A("CF", 16, 17), p16, 2.0, OP.mult, 1.0, OP.add)
     for b in range(4):
         ts(A("CI", 1, 2), A("CI", 4, 5), b, OP.arith_shift_right, 1, OP.bitwise_and)
         ts(A("PB", 0, 1), A("CI", 1, 2), 2.0 ** -(1 << b) - 1.0, OP.mult, 1.0, OP.add)
         tt(A("PB", 4, 5), A("PB", 4, 5), A("PB", 0, 1), OP.mult)
-    ts(A("W8"), A("I16"), A("CF", 8, 9), OP.is_equal, A("PB", 4, 5), OP.mult)
+    ts(A("W8"), A("I16"), g16, OP.is_equal, A("PB", 4, 5), OP.mult)
+    ts(A("KB", p1=1), A("KB", p1=1), 0.5, OP.add, -1 / 16, OP.mult)
     ts(A("RST"), A("KF"), 0.0, OP.is_equal, -4194304.0, OP.mult)
-    ts(A("LWI"), A("VL"), 1023, OP.bitwise_and)
-    ts(A("B8"), A("I16"), A("CF", 8, 9), OP.is_equal)
-    cp(A("LW"), A("LWI"))
-    ts(A("BM"), A("IOT", 0, 16), A("CF", 4, 5), OP.is_equal)
+    ts(A("SELC"), A("IR"), part, OP.is_equal)
+    ts(A("B8"), A("I16"), g16, OP.is_equal); ts(A("B1"), A("I16"), part, OP.is_equal)
+    ts(A("DB"), A("IO144"), A("CF", 12, 13), OP.is_equal)
+    ts(A("WU"), A("I16"), g16, OP.is_equal, A("CF", 16, 17), OP.mult)
+    ts(A("DUB"), A("IO144"), A("CF", 12, 13), OP.is_equal, A("CF", 16, 17), OP.mult)
+    ts(A("HID"), A("ID"), 0.5, OP.mult); ts(A("NID"), A("ID"), -1.0, OP.mult)
+    cp(A("ID16"), A("ID")); cp(A("NID16"), A("NID")); cp(A("ID32"), A("ID")); cp(A("IOH"), io); cp(A("IOB"), io)
+    ts(A("BD16"), A("GF"), 16.0, OP.mult, g16, OP.is_equal)
+    ts(A("CI", 2, 3), A("CI", 0, 1), 7, OP.bitwise_and); cp(A("CF", 20, 21), A("CI", 2, 3))
+    ts(A("CI", 3, 4), A("CI", 0, 1), 3, OP.arith_shift_right); cp(A("CF", 21, 22), A("CI", 3, 4))
+    ts(A("RP8"), A("GF"), A("CF", 20, 21), OP.is_equal, -45.0, OP.mult)
+    for a in range(16):
+        ts(A("PB", 1 + a % 2, 2 + a % 2), A("CF", 21, 22), float(a), OP.is_equal)
+        ts(A("WA", 128 * a, 128 * a + 128), A("RP8"), A("PB", 1 + a % 2, 2 + a % 2), OP.mult)
+    ts(A("ZR", p1=1), A("IW", 0, 512, p1=1), 0.0, OP.mult)
+    ts(A("LWI"), A("VL"), 1023, OP.bitwise_and); cp(A("LW"), A("LWI"))
     ts(A("OT", 0, 512), A("NB"), 4095, OP.bitwise_and); ts(A("OT", 512, 1024), A("NB"), 12, OP.arith_shift_right)
     ts(A("O", 0, 512), A("OT", 0, 512), UP, OP.mult, EPS, OP.add); ts(A("O", 512, 1024), A("OT", 512, 1024), UP, OP.mult, EPS, OP.add)
 
-    def og(n, r):
-        s, i = divmod(n, 3)
-        po = A("PO%d" % (n % 4)); l = A("LV%d_%d" % (r, s), 8 * i, 8 * i + 8) if s else A("LW", 8 * i, 8 * i + 8)
-        gather_v(po, A("O", 0, 4112) if s else A("O", 0, 1024), l); tick()
-        ts(A("PF%d" % (n % 4)), po, -2048.0, OP.add)
-
-    def copies():
-        for a in (1024, 2049, 3073):
-            src, d = A("O", 0, 1024), A("O", a, a + 1024)
-            dma("dcp", ap(d), ap(src), "Y", [src], [d])
-
-    def xg(n):
-        x, po, c = "XG%d" % (n % 3), "PO%d" % (n % 4), 128 if n else CUT0
-        gather_s(A(x, 0, 16 * c), A("X"), A(po, 0, c))
-        if c < 128: gather_v(A(x, 16 * c, 2048), A("X"), A(po, c, 128))
-
-    for q in range(8):
-        src, d = A("OT", p0=16 * q, p1=16 * q + 16), A("OX", 128 * q, 128 * q + 128)
-        dma("dox", ap(d), ap(src), "Y", [src], [d])
-    og(0, 0); og(1, 0); xg(0); xg(1); copies()
-    ts(A("DB"), A("IOT"), A("CF", 12, 13), OP.is_equal)
-    ts(A("WU"), A("I16"), A("CF", 8, 9), OP.is_equal, A("CF", 16, 17), OP.mult)
-    ts(A("DUB"), A("IOT"), A("CF", 12, 13), OP.is_equal, A("CF", 16, 17), OP.mult)
-    ts(A("HID"), A("ID"), 0.5, OP.mult); ts(A("NID"), A("ID"), -1.0, OP.mult)
-    ts(A("REP", p1=8), A("GF", p1=8), A("CF", 0, 1, p1=8), OP.is_equal)
-    ts(A("B8B"), A("I16"), A("CF", 8, 9), OP.is_equal)
-    cp(A("IOH"), A("IOT", 0, 128)); ts(A("IOB"), A("IOT", 0, 128), 1.0, OP.add)
-    ts(A("NREP", p1=8), A("REP", p1=8), -45.0, OP.mult)
-    ts(A("ZR", p1=1), A("O", 0, 512, p1=1), 0.0, OP.mult)
-
     def round_(r):
         last = r == RO - 1
+        z0 = A("Z%d_0" % r)
 
-        def sub(n, b):
-            s, i = divmod(n, 3); d = "D%d" % ((4 * n + b) % 3); z = A("Z%d_%d" % (r, s), 128 * i, 128 * i + 128)
-            for j in range(4):
-                o = A(d, 128 * j, 128 * j + 128)
-                mm(o, A("FI"), A("XG%d" % (n % 3), 4 * b + j, 2048, 16), True, False); mm(o, A("NFI"), z, False, True)
-
-        def near(n, b, h):
-            ts(A("NR%d" % (n % 2), 512 * b + 256 * h, 512 * b + 256 * h + 256), A("D%d" % ((4 * n + b) % 3), 256 * h, 256 * h + 256), MAG, OP.add, MAG, OP.is_equal)
-
-        def tm(n, b):
-            if b == 0: mm(A("KEY", 0, 128), A("ONE", 0, 128, p1=1), A("KB", p1=1), True, False)
-            for k in range(4 * b, 4 * b + 4):
-                mm(A("KEY", k, 128, 16), A("NR%d" % (n % 2), 128 * k, 128 * k + 128), A("W8"), False, k == 15)
-
-        def pa(n, step):
-            s, i = divmod(n, 3); s1 = A("S1_%d" % s, 128 * i, 128 * i + 128); m = A("S1_%d" % s, 128 * i + 15, 128 * i + 128, 16)
-            if step == 0: run("V", [A("RST"), A("KEY", 0, 128)], [s1], lambda: g.vector.tensor_tensor_scan(ap(s1), ap(A("RST")), ap(A("KEY", 0, 128)), 0.0, OP.add, OP.max))
-            elif step == 1:
-                if s == 0: ts(A("MM"), m, THR0, OP.max)
-                else: tt(A("MM"), m, A("FL%d_%d" % (r, s), 8 * i, 8 * i + 8), OP.max)
+        def front(n):
+            s, i = divmod(n, 3)
+            po = A("PO%d" % (n % 4)); l = A("LV%d_%d" % (r, s), 8 * i, 8 * i + 8) if s else A("LW", 8 * i, 8 * i + 8); w = A("O", 0, 4112 if s else 1024)
+            if r == 0: gather("V", po, w, l)
             else:
-                for q in range(8):
-                    ts(A("NO%d" % (n % 2), 16 * q, 16 * q + 16), A("KEY", 16 * q, 16 * q + 16), A("MM", q, q + 1), OP.is_ge)
-                mm(A("MI", 0, 128), A("NO%d" % (n % 2)), A("ID"), True, True)
+                pi = A("PI%d" % (n % 2))
+                ts(pi, w, 4095, OP.bitwise_and, off=l); ts(po, pi, UP, OP.mult, EPS, OP.add)
+            ts(A("PF%d" % (n % 4)), po, -2048.0, OP.add)
+            b = 0
+            while b < 4:
+                q = "V" if (n, b) in V_QUARTERS else "S"; e = b + 1
+                if q == "S" and b % 2 == 0 and (n, e) not in V_QUARTERS: e += 1
+                gather(q, A("XG%d" % (n % 3), 512 * b, 512 * e), A("X"), A(po[0], 32 * b, 32 * e)); b = e
 
-        def pb(n):
-            s, i = divmod(n, 3); sl = "SEL%d" % (n % 2); m = A("S1_%d" % s, 128 * i + 15, 128 * i + 128, 16)
-            tt(A(sl), A("MI", 0, 128), A("PF%d" % (n % 4)), OP.mult)
-            for b in range(16):
-                mm(A("MI", 128, 136), A("DB", 15 - b, 143 - b), A(sl, b, 128, 16), b == 0, b == 15)
-            mm(A("MI", 136, 144), A(sl), A("B8"), True, True)
-            ts(A("QB%d" % s, 8 * i, 8 * i + 8), m, -7.5, OP.add, M16, OP.add)
-            go = A("GO%d_%d" % (r, s), 8 * i, 8 * i + 8)
-            if s == 0: ts(go, m, THR0, OP.is_gt)
-            else: tt(go, m, A("FL%d_%d" % (r, s), 8 * i, 8 * i + 8), OP.is_gt)
-            if s < 2: ts(A("F%d_%d" % (r, s), 8 * i, 8 * i + 8), A("QB%d" % s, 8 * i, 8 * i + 8), M16, OP.subtract, 15.5, OP.add)
-
-        def pc(n):
-            s, i = divmod(n, 3); c = (8 * i, 8 * i + 8)
-            lu = A("LU%d_%d" % (r, s), *c)
-            ts(lu, A("MI", 128, 136), 2048.0, OP.add)
-            if s < 2: send(nxt, A("LV%d_%d" % (r, s + 1), *c), lu, "aV%d_%d_%d" % (r, s + 1, i))
-            act(A("UV%d" % r, *c) if s == 0 else A("VMB%d" % s, *c), A("MI", 136, 144), AF.Copy)
+        def hear(n):
+            s, i = divmod(n, 3); c = (8 * i, 8 * i + 8); zt = A("ZT%d" % (n % 2)); nr = "NR%d" % (n % 2); key = A("KEY", 0, 128)
+            mm(A("KEY", 128, 256), A("Z%d_%d" % (r, s), 128 * i, 128 * i + 128), A("NFI"), True, True)
+            if ZT_ON == "S": act(zt, A("KEY", 128, 256), AF.Copy)
+            else: cp(zt, A("KEY", 128, 256))
+            for b in range(4):
+                d = A("D%d" % ((4 * n + b) % 3))
+                together(lambda: (mm(d, A("FI"), A("XG%d" % (n % 3), 512 * b, 512 * b + 512), True, False), mm(d, zt, A("SELC", 512 * b, 512 * b + 512), False, True)))
+                ts(A(nr, 512 * b, 512 * b + 512), d, MAG, OP.add, MAG, OP.is_equal)
+            together(lambda: [mm(key, A("ONE", 0, 128, p1=1), A("KB", p1=1), True, False)] +
+                     [mm(A("KEY", k, 128, 16), A(nr, k, 2048, 16), A("W8"), False, k == 15) for k in range(16)])
+            s1 = A("S1_%d" % s, 128 * i, 128 * i + 128); m = A("S1_%d" % s, 128 * i + 15, 128 * i + 128, 16); no = A("NO%d" % (n % 2))
+            scan(s1, A("RST"), key)
+            go = A("GO%d_%d" % (r, s), *c); fl = A("FL%d_%d" % (r, s), *c) if s else None
+            if s == 0: ts(m, m, T0, OP.max)
+            else: tt(m, m, fl, OP.max)
+            if REVERSE:
+                scan(A("MB", 0, 128, -1), A("RST"), s1[:3] + (-1,) + s1[4:]); tt(no, key, A("MB"), OP.is_ge)
+            else:
+                for q in range(8): ts(A(no[0], 16 * q, 16 * q + 16), A("KEY", 16 * q, 16 * q + 16), A(s1[0], s1[1] + 16 * q + 15, s1[1] + 16 * q + 16), OP.is_ge)
+            if s == 2: tt(go, m, fl, OP.is_gt)
             if s < 2:
-                send(nxt, A("FL%d_%d" % (r, s + 1), *c), A("F%d_%d" % (r, s), *c), "aF%d_%d_%d" % (r, s + 1, i))
+                ts(A("F%d_%d" % (r, s), *c), m, 0.5, OP.add)
+                send(1, A("FL%d_%d" % (r, s + 1), *c), A("F%d_%d" % (r, s), *c), "aF%d_%d_%d" % (r, s + 1, i))
+            sl = "SEL%d" % (n % 2); lu = A("LU%d_%d" % (r, s), *c)
+            mm(A("MI", 0, 128), no, A("ID"), True, True)
+            tt(A(sl), A("MI", 0, 128), A("PF%d" % (n % 4)), OP.mult)
+            together(lambda: [mm(A("MI", 128, 136), A("DB", 15 - b, 143 - b), A(sl, b, 128, 16), b == 0, b == 15) for b in range(16)] +
+                     [mm(A("MI", 136, 144), A(sl), A("B8"), True, True)])
+            ts(lu, A("MI", 128, 136), 2048.0, OP.add)
+            act(A(vmb(s), *c), A("MI", 136, 144), AF.Copy)
+            if s < 2:
+                send(1, A("LV%d_%d" % (r, s + 1), *c), lu, "aV%d_%d_%d" % (r, s + 1, i))
                 zo = A("ZO%d_%d" % (r, s), 128 * i, 128 * i + 128)
-                gather_s(zo, A("X"), lu)
-                send(nxt, A("Z%d_%d" % (r, s + 1), 128 * i, 128 * i + 128), zo, "aZ%d_%d_%d" % (r, s + 1, i))
-            if i == 2:
-                if s == 0: send(nxt, A("UL%d" % r), A("UV%d" % r), "aU%d" % r)
-                else:
-                    send(prv, A("GL%d_%d" % (r, s)), A("GO%d_%d" % (r, s)), "aG%d_%d" % (r, s))
-                    send(T.cores[(rank - s) % N], A("LL%d_%d" % (r, s)), A("LU%d_%d" % (r, s)), "aL%d_%d" % (r, s))
+                gather("S", zo, A("X"), lu)
+                send(1, A("Z%d_%d" % (r, s + 1), 128 * i, 128 * i + 128), zo, "aZ%d_%d_%d" % (r, s + 1, i))
+
+        def vmb(s): return "VMB%d" % s if s else "VMB0_%d" % r
 
         def codes():
-            def products():
-                for i in range(3):
-                    mm(A("MI", 256 + 8 * i, 264 + 8 * i), A("Z%d_0" % r, 128 * i, 128 * i + 128), A("WU"), True, True)
-                for b in range(16):
-                    mm(A("MI", 288, 312), A("DUB", 15 - b, 143 - b), A("Z%d_0" % r, b, 384, 16), b == 0, b == 15)
-                ts(A("FA0"), A("VL"), -2048.0, OP.add)
-
-            def spread(i, a):
-                ts(A("M0_%d" % i, 16 * a, 16 * a + 16), A("BM"), A("FA0", 8 * i + a, 8 * i + a + 1), OP.mult)
-                if a == 7: mm(A("MI", 320 + 8 * i, 328 + 8 * i), A("M0_%d" % i), A("B8"), True, True)
-            m = [lambda i=i, a=a: spread(i, a) for i in range(3) for a in range(8)]
-            u = [lambda: cp(A("IA"), A("MI", 256, 280)), lambda: tt(A("ID_"), A("MI", 288, 312), A("VL"), OP.add), lambda: ts(A("IB"), A("IA"), 4095, OP.bitwise_and),
-                 lambda: ts(A("IC"), A("ID_"), 4095, OP.bitwise_and),
-                 lambda: ts(A("FB"), A("IB"), 2048.0, OP.is_gt, -4096.0, OP.mult), lambda: tt(A("UV%d" % r, 24, 48), A("IB"), A("FB"), OP.add)]
-            return [products] + m[:8] + weave(u, m[8:]) + [lambda: cp(A("VMB0"), A("MI", 320, 344))]
+            together(lambda: [mm(A("MI", 256 + 8 * i, 264 + 8 * i), A(z0[0], 128 * i, 128 * i + 128), A("WU"), True, True) for i in range(3)] +
+                     [mm(A("MI", 288, 312), A("DUB", 15 - b, 143 - b), A(z0[0], b, 384, 16), b == 0, b == 15) for b in range(16)])
+            ts(A("UT"), A("MI", 256, 280), M4096, OP.add, M4096, OP.subtract); tt(A("U%d" % r), A("MI", 256, 280), A("UT"), OP.subtract)
+            tt(A("ID_"), A("MI", 288, 312), A("VL"), OP.add); ts(A("IC"), A("ID_"), 4095, OP.bitwise_and); cp(A("FA"), A("IC"))
+            send(1, A("UL%d" % r), A("U%d" % r), "aU%d" % r)
+            gather("S", A("WG"), A("IW"), A("LW"))
+            together(lambda: [mm(A("MI", 320 + 8 * i, 328 + 8 * i), A("WG", 128 * i, 128 * i + 128), A("B1"), True, True) for i in range(3)])
+            act(A("W0"), A("MI", 320, 344), AF.Copy)
 
         def exdig(s):
-            v = A("VMB0") if s == 0 else A("UL%d" % r, 0, 24)
+            if s == 0: cp(A("EA"), A("W0"))
+            else: ts(A("EA"), A("ML%d" % r), 2048.0, OP.add, DOWN, OP.mult)
+            ts(A("EB"), A("EA"), 127, OP.bitwise_and); cp(A("WL%d" % s), A("EB"))
+            for j in range(24): ts(A("YL%d" % s, 128 * j, 128 * j + 128), A("IOH"), A("WL%d" % s, j, j + 1), OP.is_equal)
+            ts(A("EC"), A("EA"), 7, OP.arith_shift_right, 7, OP.bitwise_and)
+            tt(A("EG"), A("F%d_%d" % (r, s)), A("S1_%d" % s, 15, 384, 16), OP.subtract)
+            ts(A("EH"), A("EG"), 128.0, OP.mult, -4.0, OP.add); tt(A("XC%d" % s), A("EH"), A("EC"), OP.add)
 
-            def xoh(j): return lambda: ts(A("XOH%d" % s, 128 * j, 128 * j + 128), A("IOH"), A("XC%d" % s, j, j + 1), OP.is_equal)
-            return [lambda: ts(A("EA"), v, 2048.0, OP.add, DOWN if s else 1.0, OP.mult), lambda: ts(A("EF"), A("QB%d" % s), M16, OP.subtract, 15.0, OP.add),
-                    lambda: ts(A("EB"), A("EA"), 127, OP.bitwise_and), lambda: tt(A("EG"), A("EF"), A("S1_%d" % s, 15, 384, 16), OP.subtract),
-                    lambda: cp(A("WL%d" % s), A("EB")), lambda: ts(A("EH"), A("EG"), 8.0, OP.mult),
-                    lambda: ts(A("EC"), A("EA"), 7, OP.arith_shift_right, 7, OP.bitwise_and),
-                    lambda: tt(A("XC%d" % s), A("EH"), A("EC"), OP.add)], [xoh(j) for j in range(24)]
-
-        def exmask(s):
-            def um():
-                tt(A("UM%d" % s), A("UV%d" % r, 24, 48) if s == 0 else A("UL%d" % r, 24, 48), A("GL%d_%d" % (r, s + 1)), OP.mult)
-                if s == 0:
-                    for h in range(2): mm(A("EX%d" % h), A("ZR", 0, 128, p1=1), A("ZR", p1=1), True, False)
-
-            def yu(j):
-                q = j % 8; y = A("YU", 128 * j, 128 * j + 128)
-                ts(y, A("IOH"), A("WL%d" % s, j, j + 1), OP.is_equal, A("UM%d" % s, j, j + 1), OP.mult)
-                mm(A("EX%d" % (q // 4), q % 4 * 128, q % 4 * 128 + 128), A("XOH%d" % s, 128 * j, 128 * j + 128), y, False, s == 1 and j in (19, 23))
-            return [um], [lambda j=j: yu(j) for j in range(24)]
+        def exadd(s, c0, c1):
+            tt(A("UM%d" % s, c0, c1), A(("UL%d" if s else "U%d") % r, c0, c1), A("GL%d_%d" % (r, s + 1), c0, c1), OP.mult)
+            for j in range(c0, c1):
+                q = j % 8; y = A("YU%d" % s, 128 * j, 128 * j + 128)
+                ts(y, A("IOH"), A("XC%d" % s, j, j + 1), OP.is_equal, A("UM%d" % s, j, j + 1), OP.mult)
+                mm(A("EX%d" % (q // 4), q % 4 * 128, q % 4 * 128 + 128), A("YL%d" % s, 128 * j, 128 * j + 128), y, False, s == 1 and j in (19, 23), True)
 
         def pendig(s, c0, c1):
-            v = A("UV%d" % r, c0, c1) if s == 0 else A("VMB%d" % s, c0, c1); a, b, c = A("PA", c0, c1), A("PB_", c0, c1), A("PC", c0, c1)
+            a, b, c = A("PA", c0, c1), A("PB_", c0, c1), A("PC", c0, c1)
+            ts(a, A(vmb(s), c0, c1), 2048.0, OP.add, DOWN, OP.mult)
+            ts(c, a, 7, OP.arith_shift_right); ts(b, a, 127, OP.bitwise_and)
+            ts(A("LOB%d" % s, c0, c1), c, -1.0, OP.mult, -0.5, OP.add); cp(A("HP%d" % s, c0, c1), b)
+            for j in range(c0, c1): ts(A("HOH%d" % s, 128 * j, 128 * j + 128), A("IOB"), A("HP%d" % s, j, j + 1), OP.is_equal)
 
-            def lob():
-                ts(A("LOB%d" % s, c0, c1), b, -1.0, OP.mult, -0.5, OP.add)
-                for j in range(c0, c1):
-                    act(A("SG%d" % s, 34 * j, 34 * j + 33), A("IOT", 0, 33), AF.Sign, A("LOB%d" % s, j, j + 1))
-            return [lambda: ts(a, v, 2048.0, OP.add, DOWN, OP.mult), lambda: ts(b, a, 31, OP.bitwise_and), lambda: ts(c, a, 5, OP.arith_shift_right),
-                    lob, lambda: ts(A("HP%d" % s, c0, c1), c, 1.0, OP.add)]
-
-        def penmask(s, c0, c1, first, end):
-            m = A("HM%d" % s, c0, c1); hp = A("HP%d" % s, c0, c1); go = A("GO%d_%d" % (r, s), c0, c1)
-
-            def hoh(j):
-                q = j % 8; h = A("HOH", 128 * j, 128 * j + 128)
-                if first and j == c0: mm(A("PEN", 0, 264), A("ZR", 0, 128, p1=1), A("ZR", 0, 264, p1=1), True, False)
-                ts(h, A("IOB"), A("HM%d" % s, j, j + 1), OP.is_equal)
-                mm(A("PEN", 33 * q, 33 * q + 33), h, A("SG%d" % s, 34 * j, 34 * j + 33), False, end and j == 23)
-            if s < 2: pre = [lambda: tt(A("FC%d" % s, c0, c1), go, A("GL%d_%d" % (r, s + 1), c0, c1), OP.subtract), lambda: tt(m, hp, A("FC%d" % s, c0, c1), OP.mult)]
-            else: pre = [lambda: tt(m, hp, go, OP.mult)]
-            return pre, [lambda j=j: hoh(j) for j in range(c0, c1)]
+        def penadd(s, c0, c1, end=False):
+            m = "GO%d_%d" % (r, s)
+            if s < 2:
+                tt(A("FC%d" % s, c0, c1), A(m, c0, c1), A("GL%d_%d" % (r, s + 1), c0, c1), OP.subtract); m = "FC%d" % s
+            for j in range(c0, c1):
+                sg = A("SG%d" % s, 34 * j, 34 * j + 33)
+                act(sg, A("IO144", 0, 33), AF.Sign, A("LOB%d" % s, j, j + 1), A(m, j, j + 1))
+                mm(A("PEN", j % 8, 264, 8), A("HOH%d" % s, 128 * j, 128 * j + 128), sg, False, end and j == c1 - 1, True)
 
         def settle():
-            def alive(s): return lambda: ts(A("AL", 24 * s - 24, 24 * s), A("LV%d_%d" % (r, s)), 2048.0, OP.not_equal)
+            for j, (l, w) in enumerate((("LU%d_0", 1.0), ("LU%d_1", 1.0), ("LV%d_1", 3.0), ("LV%d_2", 3.0))):
+                ts(A("AL", 24 * j, 24 * j + 24), A(l % r), 2048.0, OP.is_equal, w, OP.mult)
+            run("V", 96 * CY, [A("AL")], [A("AR")], lambda: g.vector.tensor_reduce(ap(A("AR")), ap(A("AL")), AxisListType.X, OP.add))
+            cp(A("AC"), A("AR")); mm(A("MI", 352, 353), A("BD16"), A("AC"), True, True)
+            cp(A("AI"), A("MI", 352, 353)); ts(A("AJ"), A("AI"), 3, OP.bitwise_and)
+            ts(A("FCOL"), A("AJ"), -1 / 1024, OP.mult, 25 / 1024, OP.add)
 
-            def m1():
-                cp(A("AC"), A("AR"))
-                for i in range(3): mm(A("MI", 352, 353, p1=8), A("QT", 8 * i, 8 * i + 8), A("ONE", 0, 1), i == 0, False)
-                mm(A("MI", 352, 353, p1=8), A("B8B"), A("AC"), False, True)
+        def boats(lu):
+            ts(A("BI"), lu, DOWN, OP.mult); ts(A("BB"), lu, 2048.0, OP.is_equal); tt(A("BC"), A("FA"), A("BI"), OP.subtract)
+            tt(A("BD"), A("BC"), A("BB"), OP.mult); tt(A("FA"), A("BD"), A("BI"), OP.add)
 
-            def m2():
-                cp(A("AB", p1=8), A("AJ", p1=8))
-                mm(A("MI", 360, 361), A("REP", p1=8), A("AB", p1=8), True, True)
-            return [lambda: ts(A("QA"), A("GO%d_0" % r), -1.0, OP.mult, 1.0, OP.add), alive(1), alive(2),
-                lambda: tt(A("QT"), A("QA"), A("GO%d_1" % r), OP.subtract),
-                lambda: run("V", [A("AL")], [A("AR")], lambda: g.vector.tensor_reduce(ap(A("AR")), ap(A("AL")), AxisListType.X, OP.add)),
-                m1], [lambda: cp(A("AI", p1=8), A("MI", 352, 353, p1=8)), lambda: ts(A("AJ", p1=8), A("AI", p1=8), 3, OP.bitwise_and), m2], [
-                lambda: ts(A("FCOL"), A("MI", 360, 361), -0.0625 / 64, OP.mult, 1.5625 / 64, OP.add)]
+        def own():
+            z1, zn, y = A("ZO%d_0" % r), A("RD" if last else "Z%d_0" % (r + 1)), A("PEN", 0, 384); one = A("ONE", p1=1)
+            together(lambda: (mm(y, A("HID"), z0, True, False), mm(y, A("HID"), z1, False, False), mm(y, A("QROW", p1=1), one, False, True)))
+            act(A("RY"), y, AF.Copy, MAG); act(A("RB"), A("RY"), AF.Copy, -MAG)
+            together(lambda: (mm(y, A("ID"), z0, True, False), mm(y, A("NID"), z1, False, False), mm(y, A("GROW", p1=1), one, False, True)))
+            tt(zn, y, A("RB"), OP.min)
+            if last: dma("oyz", T.yz[:, :], ap(zn), 3 << 15, "Y", [zn], [])
 
-        def boats():
-            o = [lambda: cp(A("FA"), A("IC"))]
-            for lu in (A("LU%d_0" % r), A("LL%d_1" % r), A("LL%d_2" % r)):
-                o += [lambda lu=lu: ts(A("BI"), lu, DOWN, OP.mult), lambda lu=lu: ts(A("BB"), lu, 2048.0, OP.is_equal), lambda: tt(A("BC"), A("FA"), A("BI"), OP.subtract),
-                      lambda: tt(A("BD"), A("BC"), A("BB"), OP.mult), lambda: tt(A("FA"), A("BD"), A("BI"), OP.add)]
-            if last: return o + [lambda: dma("oyv", T.yv[:, :], ap(A("FA")), "Y", [A("FA")], [])]
-            return o + [lambda: cp(A("VL"), A("FA")), lambda: ts(A("LWI"), A("VL"), 1023, OP.bitwise_and), lambda: cp(A("LW"), A("LWI"))]
+        def passed(s):
+            if s == 0: ts(A("GO%d_0" % r), A("S1_0", 15, 384, 16), T0, OP.is_gt)
+            else: tt(A("GO%d_1" % r), A("S1_1", 15, 384, 16), A("FL%d_1" % r), OP.is_gt)
 
-        z0, z1, zn, y = A("Z%d_0" % r), A("ZO%d_0" % r), A("Z%d_0" % (r + 1)) if not last else A("RD"), A("PEN", 0, 384)
-
-        def own(part):
-            if part == 0:
-                mm(y, A("HID"), z0, True, False); mm(y, A("HID"), z1, False, False); mm(y, A("QROW", p1=1), A("ONE", p1=1), False, True)
-                ts(A("RN"), z1, 256.0, OP.is_ge)
-                act(A("RY"), y, AF.Copy, MAG); act(A("RB"), A("RY"), AF.Copy, -MAG)
-            if part == 1:
-                mm(y, A("ID"), z0, True, False); mm(y, A("NID"), A("RB"), False, True)
-                tt(A("RE"), y, A("RN"), OP.mult)
-            if part == 2:
-                mm(y, A("ID"), A("RE"), True, False); mm(y, A("ID"), A("RB"), False, True)
-                act(zn, y, AF.Copy)
-                if last: dma("oyv", T.yz[:, :], ap(zn), "Y", [zn], [])
-
-        fq.extend(codes())
+        front(0); front(1); front(2)
+        for a in (1024, 2049, 3073):
+            src, d = A("O", 0, 1024), A("O", a, a + 1024)
+            dma("dcp%d" % r, ap(d), ap(src), 1 << 19, "Y", [src, A("X")], [d], (a // 1024 - 1) << 19)
+        codes()
         for n in range(9):
-            s, i = divmod(n, 3)
-            if i == 0 and n:
-                if n == 3: tick(999)
-                pa(n - 1, 0); tick(2); pa(n - 1, 1); tick(2); pa(n - 1, 2); tick(4); pb(n - 1); tick(8); pc(n - 1)
-                og(n + 1, r); xg(n + 1)
-                e, x = exdig(s - 1)
-                fq.extend(weave(e, pendig(s - 1, 0, 24)))
-                if s == 2 and not last:
-                    c0, c1, c2 = settle()
-                    x = weave(x[:6], c0) + x[6:16] + weave(x[16:19], c1) + x[19:] + c2
-                fq.extend(x)
-            sub(n, 0); sub(n, 1); sub(n, 2)
-            if i == 0 and n: tick(8)
+            hear(n)
+            if n < 6: front(n + 3)
+            if n == 2:
+                send(1, A("ML%d" % r), A(vmb(0)), "aM%d" % r)
+                passed(0); own(); exdig(0); pendig(0, 0, 24); boats(A("LU%d_0" % r))
+            if n == 5:
+                passed(1)
+                send(-1, A("GL%d_1" % r), A("GO%d_1" % r), "aG%d_1" % r); send(-1, A("LL%d_1" % r), A("LU%d_1" % r), "aL%d_1" % r)
+                for h in ("EX0", "EX1"): mm(A(h), A("ZR", 0, 128, p1=1), A("ZR", p1=1), True, False)
+                mm(A("PEN", 0, 264), A("ZR", 0, 128, p1=1), A("ZR", 0, 264, p1=1), True, False, True)
+                exadd(0, 0, 24); penadd(0, 0, 24); exdig(1); pendig(1, 0, 24); boats(A("LL%d_1" % r))
+                if not last: settle()
             if n == 7:
-                e, x = penmask(0, 0, 24, True, False); e2, x2 = exmask(0)
-                fq.extend(e[:1] + e2 + e[1:] + x + x2)
-            for b in range(4):
-                near(n, b, 0)
-                if i and b == 0: pa(n - 1, 0)
-                if i and b == 1: pa(n - 1, 2)
-                near(n, b, 1)
-                if b == 0: sub(n, 3)
-                if i and b == 0: pa(n - 1, 1)
-                if b == 1: tm(n, 0)
-                if i and b == 1: tick(2); pb(n - 1)
-                if i and b == 2: pc(n - 1)
-                if b: tm(n, b)
-                if b == 2:
-                    if i == 0: og(n + 2, r); xg(n + 2)
-                    if i == 2 and n < 8: og(n + 1, r); xg(n + 1)
-                tick(3)
-            if n in (3, 5, 6): own((3, 5, 6).index(n))
-        e, x = penmask(2, 0, 16, False, False)
-        fq.extend(pendig(2, 0, 16) + e + x)
-        pa(8, 0); tick(2); pa(8, 1); tick(2); pa(8, 2); tick(5); pb(8); tick(8); pc(8)
-        if not last: fq.extend([lambda: ts(A("FI"), A("ID"), A("FCOL"), OP.mult), lambda: ts(A("NFI"), A("ID"), A("FCOL"), OP.mult, -1.0, OP.mult)])
-        d = pendig(2, 16, 24); e, x = penmask(2, 16, 24, False, False); e1, x1 = penmask(1, 0, 24, False, True); e2, x2 = exmask(1)
-        tick(4); fq.extend(d); tick(10); fq.extend(e + x + e1[:1] + e2 + e1[1:] + x1); tick(999)
-        act(A("HC0"), A("PEN", 0, 264), AF.Copy)
-        fq.extend(x2); tick(8)
-        tt(A("HC", 0, 263), A("HC0", 1, 264), A("HC0", 0, 263), OP.is_gt)
-        for q in range(8):
-            src, d = A("HC", 33 * q, 33 * q + 32), A("HS", p0=q, p1=q + 1)
-            dma("dhs", ap(d), ap(src), "YS"[q % 2], [src], [d])
-        tick(999)
-        fq.extend(boats())
-        for h in range(2):
-            c = (512 * h, 512 * h + 512)
-            tick(2); tt(A("OT", *c), A("EX%d" % h), A("OX", *c), OP.add); tick(1); ts(A("OX", *c), A("OT", *c), 4095, OP.bitwise_and)
-            if not last: tick(1); ts(A("OE", *c), A("OX", *c), UP, OP.mult, EPS, OP.add)
-            for q in range(4 * h, 4 * h + 4):
-                src, d = A("OX" if last else "OE", 128 * q, 128 * q + 128), A("O", 0, 1024, p0=16 * q, p1=16 * q + 16)
-                dma("dex", ap(d), ap(src), "Y", [src], [d])
+                send(-1, A("GL%d_2" % r, 0, 16), A("GO%d_2" % r, 0, 16), "aG%d_2a" % r)
+                pendig(2, 0, 16); penadd(2, 0, 16); exadd(1, 0, 16); penadd(1, 0, 16)
+        send(-1, A("GL%d_2" % r, 16, 24), A("GO%d_2" % r, 16, 24), "aG%d_2b" % r); send(-2, A("LL%d_2" % r), A("LU%d_2" % r), "aL%d_2" % r)
+        pendig(2, 16, 24); penadd(2, 16, 24); exadd(1, 16, 24); penadd(1, 16, 24, True)
+        boats(A("LL%d_2" % r))
+        if last: dma("oyv", T.yv[:, :], ap(A("FA")), 1 << 14, "Y", [A("FA")], [])
+        else:
+            cp(A("VL"), A("FA")); ts(A("LWI"), A("VL"), 1023, OP.bitwise_and); cp(A("LW"), A("LWI"))
+            ts(A("FI"), A("ID"), A("FCOL"), OP.mult); ts(A("NFI"), A("ID"), A("FCOL"), OP.mult, -1.0, OP.mult)
+        cp(A("C16"), A("PEN", 0, 264))
+        together(lambda: [mm(A("PEN", 128 * h, 128 * h + 128), A("C16", 128 * h + d, 128 * h + d + 128), A(w), d == 8, d == 0, True)
+                          for h in range(2) for d, w in ((8, "ID16"), (0, "NID16"))])
+        ts(A("HT"), A("PEN", 0, 256), 0.0, OP.is_gt)
         for c in range(8):
-            d = A("D%d" % (c % 3)); x = A("X", 512 * c + c // 4, 512 * c + c // 4 + 512)
-            mm(d, A("ID"), x, True, False); mm(d, A("NREP", p1=8), A("HS", 512 * c, 512 * c + 512, p1=8), False, True)
-            if c in (3, 5, 7): tick(3); ts(x, d, 0.0, OP.max)
-            else: act(x, d, AF.Relu)
-            if last: dma("oyx%d" % (c % 2), T.yx[:, 512 * c:512 * c + 512], ap(x), "Y", [x], [])
-        tick(999)
+            d = ("D0", "D1", "D2", "KEY")[c % 4]; x = A("X", xcol(512 * c), xcol(512 * c) + 512)
+            mm(A(d), A("ID"), x, True, False)
+            together(lambda: [mm(A(d, 128 * b, 128 * b + 128), A("WA", 128 * ((4 * c + b) % 16), 128 * ((4 * c + b) % 16) + 128),
+                                 A("HT", 128 * (c // 4), 128 * (c // 4) + 128), False, b == 3, True) for b in range(4)])
+            if c in RELU_V: ts(x, A(d), 0.0, OP.max)
+            else: act(x, A(d), AF.Relu)
+            if last: dma("oyx", T.yx[:, 512 * c:512 * c + 512], ap(x), 1 << 17, "Y", [x], [], c << 17)
+        for h in range(2): act(A("EXS", 512 * h, 512 * h + 512), A("EX%d" % h), AF.Copy)
+        for h in range(2):
+            e = "EX%d" % h; c = (512 * h, 512 * h + 512)
+            together(lambda: [run("P", 4 * 128 * PCY, [A("EXS", 4 * h + b, 1024, 8), A("ID32")], [A(e, 128 * b, 128 * b + 128)],
+                                  lambda b=b, e=e, h=h: g.tensor.transpose(ap(A(e, 128 * b, 128 * b + 128)), ap(A("EXS", 4 * h + b, 1024, 8)), ap(A("ID32")))) for b in range(4)])
+            if not last: tt(A("O", *c), A(e), A("OT", *c), OP.add)
+            else:
+                tt(A("OT", *c), A(e), A("O", *c), OP.add); ts(A("OM", *c), A("OT", *c), 4095, OP.bitwise_and)
         if last:
-            ts(A("EXS"), A("O", 512, 1024), 4096.0, OP.mult); tt(A("YN"), A("EXS"), A("O", 0, 512), OP.add)
-            dma("oyn", T.yn[:, :], ap(A("YN")), "Y", [A("YN")], [])
-        else: og(0, r + 1); og(1, r + 1); xg(0); xg(1); copies()
+            ts(A("YH"), A("OM", 512, 1024), 4096.0, OP.mult); tt(A("YN"), A("YH"), A("OM", 0, 512), OP.add)
+            dma("oyn", T.yn[:, :], ap(A("YN")), 1 << 18, "Y", [A("YN")], [])
 
     for r in range(RO):
         round_(r)
+    if not ORDER: ORDER.extend(schedule(ops))
+    for i in ORDER: ops[i][5]()
     for sem in cnt:
         if known["G"].get(sem, 0) < cnt[sem]: g.wait_ge(T.sem[sem], cnt[sem])

@@ -91,30 +91,40 @@ def schedule(ops):
             s = span(a); acc[a[0]] = [r for r in acc.get(a[0], []) if not (s[0] <= r[0][0] and r[0][1] <= s[1] and s[2] <= r[0][2] and r[0][3] <= s[3])]
         for lst, w in ((reads, False), (writes, True)):
             for a in lst: acc.setdefault(a[0], []).append((span(a), w, i, dmai))
-    succ = [[] for _ in ops]; way = [0.0] * n
-    for i in range(n):
-        for j in deps[i]: succ[j].append(i)
-    for i in range(n - 1, -1, -1): way[i] = max([ops[i][2]] + [deps[k][i] + way[k] for k in succ[i]])
-    left = [len(d) for d in deps]; at = [0.0] * n; ready = {q: [] for q in "VSPGY"}; free = {q: 0.0 for q in ready}; bank = {}; order = []
     banks = [set(a[0] for a in o[3] + o[4] if psum(a)) for o in ops]
+    back = [dict() for _ in ops]
     for i in range(n):
-        if not left[i]: ready[ops[i][0]].append(i)
-    while len(order) < n:
-        best = None
-        for q in ready:
-            for i in ready[q]:
-                t = max([free[q], at[i]] + [bank[b][1] for b in banks[i] if b in bank and bank[b][0] != q])
-                if best is None or (t, -way[i]) < best[:2]: best = (t, -way[i], i)
-        t, _, i = best; q = ops[i][0]
-        ready[q].remove(i); order.append(i); free[q] = t + ops[i][1]
-        for b in banks[i]: bank[b] = (q, t + ops[i][2])
-        for k in succ[i]:
-            at[k] = max(at[k], t + deps[k][i]); left[k] -= 1
-            if not left[k]: ready[ops[k][0]].append(k)
-    return order
+        for j in deps[i]: back[j][i] = deps[i][j] - ops[j][1] + ops[i][1]
+
+    def once(deps, rank):
+        succ = [[] for _ in ops]
+        for i in range(n):
+            for j in deps[i]: succ[j].append(i)
+        left = [len(d) for d in deps]; at = [0.0] * n; ready = {q: [] for q in "VSPGY"}; free = {q: 0.0 for q in ready}; bank = {}; order = []
+        for i in range(n):
+            if not left[i]: ready[ops[i][0]].append(i)
+        while len(order) < n:
+            best = None
+            for q in ready:
+                for i in ready[q]:
+                    t = max([free[q], at[i]] + [bank[b][1] for b in banks[i] if b in bank and bank[b][0] != q])
+                    if best is None or (t, rank[i]) < best[:2]: best = (t, rank[i], i)
+            t, _, i = best; q = ops[i][0]
+            ready[q].remove(i); order.append(i); at[i] = t; free[q] = t + ops[i][1]
+            for b in banks[i]: bank[b] = (q, t + ops[i][1] + LAT)
+            for k in succ[i]:
+                at[k] = max(at[k], t + deps[k][i]); left[k] -= 1
+                if not left[k]: ready[ops[k][0]].append(k)
+        return max(at[i] + ops[i][2] for i in range(n)), order, [-at[i] - ops[i][1] for i in range(n)]
+
+    best = now = once(deps, list(range(n)))
+    for _ in range(PASSES):
+        now = once(deps, once(back, now[2])[2])
+        if now[0] < best[0]: best = now
+    return best[1]
 
 
-ORDER = []
+ORDER, PASSES = [], 4
 
 
 def rank_program(g, core, T, topo):

@@ -6,7 +6,9 @@ SCRATCH, ALIAS, POOL = {}, {}, {}
 REVERSE = True
 ZT_ON = "S"
 V_QUARTERS = {(0, 1), (0, 3), (1, 2)}
-RELU_V = (1, 3, 5, 7)
+N3 = 5
+RELU_V = ((5, 7), (1,))
+SHARE = (2, 0, 2, 2, 0)
 
 
 def _b(names, cols, dtype, where="sbuf"):
@@ -20,13 +22,15 @@ def _s(names, cols, dtype):
         ALIAS[n] = ("pool_" + dtype, o, cols); POOL[dtype] = o + (cols + w - 1) // w * w
 
 
-_b("X", 4112, "bfloat16"); _b("O", 4112, "int32"); _b("OT OM", 1024, "int32"); _b("NB", 512, "int32"); _b("YN YH", 512, "float32")
+_b("X", 4112, "bfloat16"); _b("OF", 4112, "float32"); _s("BM", 16, "float32"); _b("O OT OM", 1024, "int32"); _b("NB", 512, "int32"); _b("YN YH", 512, "float32")
 _b("XG0 XG1 XG2 NR0 NR1 IR", 2048, "bfloat16"); _b("SELC", 2048, "float16"); _b("WA", 2048, "bfloat16")
 _b("PO0 PO1 PO2 PO3", 128, "uint16"); _b("PI0 PI1", 128, "int32"); _b("PF0 PF1 PF2 PF3 SEL0 SEL1 ZT0 ZT1 IOH ID16 NID16", 128, "float16")
-_b("D0 D1 D2 KEY MI EX0 EX1 PEN", 512, "float32", "psum"); _b("NO0 NO1", 128, "bfloat16"); _b("MB ID32 RST KF GF IOT", 128, "float32")
-_b("S1_0 S1_1 S1_2 WG RY", 384, "float32"); _b("SG0 SG1 SG2", 24 * 34, "bfloat16")
-_b("YL0 YL1 YU0 YU1", 24 * 128, "float16"); _b("HOH0 HOH1 HOH2", 24 * 128, "bfloat16")
-_b("IW EXS", 1024, "float32"); _b("C16", 264, "float16"); _b("HT", 256, "bfloat16"); _b("ZR", 512, "float16")
+_b("D0 D1 PN2 KEY MI EX0 EX1 PEN", 512, "float32", "psum"); _b("CB0 CB1 CL0 CL1", 264, "float16"); _b("SG0", 24 * 34, "float16"); _b("NO0 NO1", 128, "bfloat16"); _b("MB RST KF GF TH TH0 TH1", 128, "float32"); _s("TH3", 24, "float32")
+_b("S1_0 S1_1 S1_2 WG RY", 384, "float32"); _b("SG1 SG2", 24 * 34, "bfloat16")
+_b("YL0 YL1 YU0 YU1", 24 * 128, "float16"); _b("HOH1 HOH2", 24 * 128, "bfloat16")
+_b("SEL2", 384, "float16"); _b("EXR EXQ", 1024, "float16"); _b("DM DM4 NDM ONE16", 128, "float16"); _b("R1536", 512, "float16"); _s("WL0B WL1B HP0B HP1B HP2B", 24, "float32")
+_s("WA0 WA1 WB0 WB1", 8, "int32"); _s("LS1_0 LS1_1", 24, "uint16")
+_b("IW", 1024, "float32"); _b("C16", 264, "float16"); _b("HT", 256, "bfloat16"); _b("ZR", 512, "float16")
 _s("VMB1 VMB2 LOB0 LOB1 LOB2 HP0 HP1 HP2 XC0 XC1 WL0 WL1 W0 FA BB BC BD EG EH FC0 FC1 UM0 UM1 UT CF", 24, "float32")
 _s("VL ID_ IC LWI BI EA EB EC PA PB_ PC", 24, "int32"); _s("LW", 24, "uint16"); _s("PB I16 B1", 8, "float32")
 for _r in range(RO):
@@ -51,13 +55,13 @@ for _r in range(RO):
         for _i in range(NCH):
             SEMAPHORES += ["aF%d_%d_%d" % (_r, _j, _i), "aV%d_%d_%d" % (_r, _j, _i), "aZ%d_%d_%d" % (_r, _j, _i)]
         SEMAPHORES += ["aL%d_%d" % (_r, _j)]
-    SEMAPHORES += ["aU%d" % _r, "aM%d" % _r, "aG%d_1" % _r, "aG%d_2a" % _r, "aG%d_2b" % _r]
+    SEMAPHORES += ["aU%d" % _r, "aM%d" % _r, "aC%d" % _r, "aG%d_1" % _r, "aG%d_2a" % _r, "aG%d_2b" % _r]
 
 MAG = 12582912.0
 M4096 = MAG * 4096
 UP, DOWN, EPS = 4097 / 4096, 4095 / 4096, 0.00015
 T0 = 34816.0
-CY, PCY, GCY, LAT, HOP, DMA0, DMAB = 0.83, 0.42, 1.56 * 0.83, 120.0, 2200.0, 1500.0, 190.0
+CY, PCY, GCY, LAT, HOP, DMA0, DMAB = 0.83, 0.42, 1.56 * 0.83, 205.0, 2200.0, 1500.0, 190.0
 
 
 def A(name, c0=0, c1=None, step=1, p0=0, p1=128):
@@ -96,7 +100,7 @@ def schedule(ops):
     for i in range(n):
         for j in deps[i]: back[j][i] = deps[i][j] - ops[j][1] + ops[i][1]
 
-    def once(deps, rank):
+    def once(deps, rank, ahead):
         succ = [[] for _ in ops]
         for i in range(n):
             for j in deps[i]: succ[j].append(i)
@@ -106,9 +110,11 @@ def schedule(ops):
         while len(order) < n:
             best = None
             for q in ready:
-                for i in ready[q]:
-                    t = max([free[q], at[i]] + [bank[b][1] for b in banks[i] if b in bank and bank[b][0] != q])
-                    if best is None or (t, rank[i]) < best[:2]: best = (t, rank[i], i)
+                l = [(max([free[q], at[i]] + [bank[b][1] for b in banks[i] if b in bank and bank[b][0] != q]), rank[i], i) for i in ready[q]]
+                if not l: continue
+                t0 = min(l)[0]; c = min((x for x in l if x[0] <= t0 + ahead), key=lambda x: x[1])
+                c = min((x for x in l if x[0] + ops[x[2]][1] <= c[0] + SLIP), key=lambda x: x[1], default=c)
+                if best is None or c < best: best = c
             t, _, i = best; q = ops[i][0]
             ready[q].remove(i); order.append(i); at[i] = t; free[q] = t + ops[i][1]
             for b in banks[i]: bank[b] = (q, t + ops[i][1] + LAT)
@@ -117,14 +123,16 @@ def schedule(ops):
                 if not left[k]: ready[ops[k][0]].append(k)
         return max(at[i] + ops[i][2] for i in range(n)), order, [-at[i] - ops[i][1] for i in range(n)]
 
-    best = now = once(deps, list(range(n)))
-    for _ in range(PASSES):
-        now = once(deps, once(back, now[2])[2])
-        if now[0] < best[0]: best = now
+    best = once(deps, list(range(n)), 0.0)
+    for ahead in AHEAD:
+        now = best
+        for _ in range(PASSES):
+            now = once(deps, once(back, now[2], ahead)[2], ahead)
+            if now[0] < best[0]: best = now
     return best[1]
 
 
-ORDER, PASSES = [], 4
+ORDER, PASSES, AHEAD, SLIP = [], 4, (0.0, 100.0, 200.0, 300.0, 150.0, 250.0), 30.0
 
 
 def rank_program(g, core, T, topo):
@@ -203,7 +211,7 @@ def rank_program(g, core, T, topo):
             note(q, sem, cnt[sem], reads, writes)
         ops.append((q, 50.0, DMA0 + (after + size) / DMAB, list(reads), list(writes), f))
 
-    def send(step, out, in_, sem):
+    def send(step, out, in_, sem, after=()):
         dst, src = T.cores[(rank + step) % N], T.cores[(rank - step) % N]
         cnt[sem] = len(topo.engines(src, core)); note("R", sem, cnt[sem], [], [out])
 
@@ -212,7 +220,7 @@ def rank_program(g, core, T, topo):
             rid, pid, _ = topo.addr(dst)
             g.remote_dma(ap(out), ap(in_), T.sem[sem], T.sem["ls"], pid, rid, topo.mask(core, dst))
             cnt["ls"] = cnt.get("ls", 0) + len(topo.engines(core, dst))
-        ops.append(("G", 150.0, HOP, [in_], [out], f))
+        ops.append(("G", 150.0, HOP, [in_] + list(after), [out], f))
 
     def col(x):
         return (ap(x), [x]) if isinstance(x, tuple) else (x, [])
@@ -227,8 +235,8 @@ def rank_program(g, core, T, topo):
     def tt(out, a, b, op):
         run("V", CY * max(64, width(out) * (1 if psum(a) or psum(b) else 2)), [a, b], [out], lambda: g.vector.tensor_tensor(ap(out), ap(a), ap(b), op))
 
-    def scan(out, a, b):
-        run("V", vc(width(out), out, a, b), [a, b], [out], lambda: g.vector.tensor_tensor_scan(ap(out), ap(a), ap(b), 0.0, OP.add, OP.max))
+    def scan(out, a, b, op):
+        run("V", vc(width(out), out, a, b), [a, b], [out], lambda: g.vector.tensor_tensor_scan(ap(out), ap(a), ap(b), 0.0, op, OP.max))
 
     def cp(out, a):
         run("V", vc(width(out), out, a), [a], [out], lambda: g.vector.tensor_copy(ap(out), ap(a)))
@@ -255,7 +263,7 @@ def rank_program(g, core, T, topo):
 
     def xcol(b): return b + b // 2048
 
-    ms(A("X", 2048, 2049), 512.0); ms(A("X", 4097, 4112), 512.0); ms(A("O", 2048, 2049), 0); ms(A("O", 4097, 4112), 0)
+    ms(A("X", 2048, 2049), 512.0); ms(A("X", 4097, 4112), 512.0); ms(A("OF", 2048, 2049), 0.0); ms(A("OF", 4097, 4112), 0.0)
     dma("dv", ap(A("VL")), T.v[:, :], 1 << 14, "S", [], [A("VL")])
     dma("dnb", ap(A("NB")), T.nb[:, :], 1 << 18, "Y", [], [A("NB")])
     for i in range(4):
@@ -263,40 +271,48 @@ def rank_program(g, core, T, topo):
         dma("dx%d" % i, ap(a), T.tracks[:, 1024 * i:1024 * i + 1024], 1 << 18, "Y", [], [a], (i + 1) << 18)
     dma("dz", ap(A("Z0_0")), T.z[:, :], 3 << 15, "S", [], [A("Z0_0")], 1 << 18)
     iota(A("CI", 0, 1), [[1, 1]], 0, 1, False); iota(A("IO144"), [[1, 144]], 0, 0); iota(A("I16"), [[16, 8]], 0, 0)
-    iota(A("KB", p1=1), [[0, 8], [1, 16]], 0, 0); iota(A("KF"), [[0, 8], [1, 16]], 0, 0); iota(A("GF"), [[1, 8], [0, 16]], 0, 0)
-    iota(A("IR"), [[1, 128], [0, 16]], 0, 0); iota(A("IW"), [[1, 1024]], 0, 0)
+    iota(A("KF"), [[0, 8], [1, 16]], 0, 0); iota(A("GF"), [[1, 8], [0, 16]], 0, 0)
+    for b in range(4): iota(A("IR", 512 * b, 512 * b + 512), [[1, 32], [0, 16]], 32 * b, 0)
+    for b in range(2): iota(A("IW", 512 * b, 512 * b + 512), [[1, 512]], 512 * b, 0)
     io, part, p16, g16 = A("IO144", 0, 128), A("CF", 0, 1), A("CF", 4, 5), A("CF", 8, 9)
     ms(A("ONE"), 1.0); ms(A("QROW", p1=1), -0.25); ms(A("GROW", p1=1), 512.0); ms(A("PB", 4, 5), 32768.0)
     cp(part, A("CI", 0, 1))
     ts(A("CI", 4, 5), A("CI", 0, 1), 15, OP.bitwise_and); cp(p16, A("CI", 4, 5)); tt(g16, part, p16, OP.subtract)
     ts(A("ID"), io, part, OP.is_equal)
-    ts(A("FI"), A("ID"), 25 / 1024, OP.mult); ts(A("NFI"), A("ID"), -25 / 1024, OP.mult)
+    act(A("FI"), A("ID"), AF.Copy, 0.0, 25 / 1024); act(A("NFI"), A("ID"), AF.Copy, 0.0, -25 / 1024)
     ts(A("CF", 12, 13), g16, 15.0, OP.add); ts(A("CF", 16, 17), p16, 2.0, OP.mult, 1.0, OP.add)
     for b in range(4):
         ts(A("CI", 1, 2), A("CI", 4, 5), b, OP.arith_shift_right, 1, OP.bitwise_and)
         ts(A("PB", 0, 1), A("CI", 1, 2), 2.0 ** -(1 << b) - 1.0, OP.mult, 1.0, OP.add)
         tt(A("PB", 4, 5), A("PB", 4, 5), A("PB", 0, 1), OP.mult)
     ts(A("W8"), A("I16"), g16, OP.is_equal, A("PB", 4, 5), OP.mult)
-    ts(A("KB", p1=1), A("KB", p1=1), 0.5, OP.add, -1 / 16, OP.mult)
+    ts(A("CF", 1, 2), part, 1 / 16, OP.mult, -1 / 16, OP.add); ts(A("CF", 2, 3), part, 65536.0, OP.mult)
+    ts(A("TH0", p1=2), A("KF", p1=2), 0.5, OP.add, A("CF", 1, 2, p1=2), OP.mult); ts(A("TH1", p1=2), A("GF", p1=2), A("CF", 2, 3, p1=2), OP.mult)
+    tt(A("KB", p1=2), A("TH0", p1=2), A("TH1", p1=2), OP.add)
+    ts(A("TH"), A("GF"), 65536.0, OP.mult, T0, OP.add); ms(A("TH0"), 0.0); ms(A("TH1"), 0.0)
+    for i in range(3): act(A("TH3", 8 * i, 8 * i + 8), A("TH", 0, 128, 16), AF.Copy)
     ts(A("RST"), A("KF"), 0.0, OP.is_equal, -4194304.0, OP.mult)
-    ts(A("SELC"), A("IR"), part, OP.is_equal)
+    for b in range(4): ts(A("SELC", 512 * b, 512 * b + 512), A("IR", 512 * b, 512 * b + 512), part, OP.is_equal)
     ts(A("B8"), A("I16"), g16, OP.is_equal); ts(A("B1"), A("I16"), part, OP.is_equal)
     ts(A("DB"), A("IO144"), A("CF", 12, 13), OP.is_equal)
     ts(A("WU"), A("I16"), g16, OP.is_equal, A("CF", 16, 17), OP.mult)
     ts(A("DUB"), A("IO144"), A("CF", 12, 13), OP.is_equal, A("CF", 16, 17), OP.mult)
-    ts(A("HID"), A("ID"), 0.5, OP.mult); ts(A("NID"), A("ID"), -1.0, OP.mult)
-    cp(A("ID16"), A("ID")); cp(A("NID16"), A("NID")); cp(A("ID32"), A("ID")); cp(A("IOH"), io); cp(A("IOB"), io)
+    act(A("HID"), A("ID"), AF.Copy, 0.0, 0.5); act(A("NID"), A("ID"), AF.Copy, 0.0, -1.0); act(A("IOH"), io, AF.Copy); act(A("IOB"), io, AF.Copy)
+    ts(A("CF", 22, 23), part, 1.0, OP.add); ts(A("DM"), io, A("CF", 22, 23), OP.is_equal); tt(A("DM"), A("ID"), A("DM"), OP.subtract)
+    act(A("DM4"), A("DM"), AF.Copy, 0.0, 4096.0); act(A("NDM"), A("DM"), AF.Copy, 0.0, -1.0); act(A("WU"), A("WU"), AF.Copy, 0.0, 1 / 4096)
+    for nm, c in (("R1536", 1536.0), ("ONE16", 1.0), ("ZR", 0.0)): act(A(nm, p1=1), A("IR", 0, width(A(nm)), p1=1), AF.Copy, c, 0.0)
     ts(A("BD16"), A("GF"), 16.0, OP.mult, g16, OP.is_equal)
     ts(A("CI", 2, 3), A("CI", 0, 1), 7, OP.bitwise_and); cp(A("CF", 20, 21), A("CI", 2, 3))
     ts(A("CI", 3, 4), A("CI", 0, 1), 3, OP.arith_shift_right); cp(A("CF", 21, 22), A("CI", 3, 4))
-    ts(A("RP8"), A("GF"), A("CF", 20, 21), OP.is_equal, -45.0, OP.mult)
+    ts(A("RP8"), A("GF"), A("CF", 20, 21), OP.is_equal, -45.0, OP.mult); ts(A("BM"), A("IO144", 0, 16), A("CF", 21, 22), OP.is_equal)
     for a in range(16):
-        ts(A("PB", 1 + a % 2, 2 + a % 2), A("CF", 21, 22), float(a), OP.is_equal)
-        ts(A("WA", 128 * a, 128 * a + 128), A("RP8"), A("PB", 1 + a % 2, 2 + a % 2), OP.mult)
-    ts(A("ZR", p1=1), A("IW", 0, 512, p1=1), 0.0, OP.mult)
+        act(A("WA", 128 * a, 128 * a + 128), A("RP8"), AF.Copy, 0.0, A("BM", a, a + 1))
     ts(A("LWI"), A("VL"), 1023, OP.bitwise_and); cp(A("LW"), A("LWI"))
     ts(A("OT", 0, 512), A("NB"), 4095, OP.bitwise_and); ts(A("OT", 512, 1024), A("NB"), 12, OP.arith_shift_right)
-    ts(A("O", 0, 512), A("OT", 0, 512), UP, OP.mult, EPS, OP.add); ts(A("O", 512, 1024), A("OT", 512, 1024), UP, OP.mult, EPS, OP.add)
+    for h in (0, 512):
+        ts(A("OF", h, h + 512), A("OT", h, h + 512), UP, OP.mult, EPS, OP.add)
+        for a in (1024, 2049, 3073):
+            act(A("OF", a + h, a + h + 512), A("OF", h, h + 512), AF.Copy)
 
     def round_(r):
         last = r == RO - 1
@@ -304,7 +320,7 @@ def rank_program(g, core, T, topo):
 
         def front(n):
             s, i = divmod(n, 3)
-            po = A("PO%d" % (n % 4)); l = A("LV%d_%d" % (r, s), 8 * i, 8 * i + 8) if s else A("LW", 8 * i, 8 * i + 8); w = A("O", 0, 4112 if s else 1024)
+            po = A("PO%d" % (n % 4)); l = A("LV%d_%d" % (r, s), 8 * i, 8 * i + 8) if s else A("LW", 8 * i, 8 * i + 8); w = A("O") if r else A("OF", 0, 4112 if s else 1024)
             if r == 0: gather("V", po, w, l)
             else:
                 pi = A("PI%d" % (n % 2))
@@ -322,43 +338,54 @@ def rank_program(g, core, T, topo):
             if ZT_ON == "S": act(zt, A("KEY", 128, 256), AF.Copy)
             else: cp(zt, A("KEY", 128, 256))
             for b in range(4):
-                d = A("D%d" % ((4 * n + b) % 3))
+                d = A(("D0", "D1", "PN2")[(4 * n + b) % 3] if n < N3 else "D%d" % (b % 2))
                 together(lambda: (mm(d, A("FI"), A("XG%d" % (n % 3), 512 * b, 512 * b + 512), True, False), mm(d, zt, A("SELC", 512 * b, 512 * b + 512), False, True)))
                 ts(A(nr, 512 * b, 512 * b + 512), d, MAG, OP.add, MAG, OP.is_equal)
-            together(lambda: [mm(key, A("ONE", 0, 128, p1=1), A("KB", p1=1), True, False)] +
+            together(lambda: [mm(key, A("ONE", 0, 128, p1=2), A("KB", p1=2), True, False)] +
                      [mm(A("KEY", k, 128, 16), A(nr, k, 2048, 16), A("W8"), False, k == 15) for k in range(16)])
             s1 = A("S1_%d" % s, 128 * i, 128 * i + 128); m = A("S1_%d" % s, 128 * i + 15, 128 * i + 128, 16); no = A("NO%d" % (n % 2))
-            scan(s1, A("RST"), key)
-            go = A("GO%d_%d" % (r, s), *c); fl = A("FL%d_%d" % (r, s), *c) if s else None
-            if s == 0: ts(m, m, T0, OP.max)
-            else: tt(m, m, fl, OP.max)
-            if REVERSE:
-                scan(A("MB", 0, 128, -1), A("RST"), s1[:3] + (-1,) + s1[4:]); tt(no, key, A("MB"), OP.is_ge)
-            else:
-                for q in range(8): ts(A(no[0], 16 * q, 16 * q + 16), A("KEY", 16 * q, 16 * q + 16), A(s1[0], s1[1] + 16 * q + 15, s1[1] + 16 * q + 16), OP.is_ge)
+            go = A("GO%d_%d" % (r, s), *c); fl = A("FL%d_%d" % (r, s), *c) if s else None; th = "TH%d" % (n % 2) if s else "TH"
+            if s: cp(A(th, 0, 128, 16), fl)
+            scan(s1, A(th), key, OP.max)
+            scan(A("MB", 0, 128, -1), A("RST"), s1[:3] + (-1,) + s1[4:], OP.add); tt(no, key, A("MB"), OP.is_ge)
             if s == 2: tt(go, m, fl, OP.is_gt)
             if s < 2:
                 ts(A("F%d_%d" % (r, s), *c), m, 0.5, OP.add)
-                send(1, A("FL%d_%d" % (r, s + 1), *c), A("F%d_%d" % (r, s), *c), "aF%d_%d_%d" % (r, s + 1, i))
-            sl = "SEL%d" % (n % 2); lu = A("LU%d_%d" % (r, s), *c)
+                send(1, A("FL%d_%d" % (r, s + 1), *c), A("F%d_%d" % (r, s), *c), "aF%d_%d_%d" % (r, s + 1, i), [A("UL0")])
+            sl = A("SEL%d" % (n % 2)) if s < 2 else A("SEL2", 128 * i, 128 * i + 128); lu = A("LU%d_%d" % (r, s), *c); vm = A("MI", 160 + c[0], 160 + c[1])
             mm(A("MI", 0, 128), no, A("ID"), True, True)
-            tt(A(sl), A("MI", 0, 128), A("PF%d" % (n % 4)), OP.mult)
-            together(lambda: [mm(A("MI", 128, 136), A("DB", 15 - b, 143 - b), A(sl, b, 128, 16), b == 0, b == 15) for b in range(16)] +
-                     [mm(A("MI", 136, 144), A(sl), A("B8"), True, True)])
-            ts(lu, A("MI", 128, 136), 2048.0, OP.add)
-            act(A(vmb(s), *c), A("MI", 136, 144), AF.Copy)
+            tt(sl, A("MI", 0, 128), A("PF%d" % (n % 4)), OP.mult)
+            mm(vm, sl, A("B8"), True, True)
             if s < 2:
-                send(1, A("LV%d_%d" % (r, s + 1), *c), lu, "aV%d_%d_%d" % (r, s + 1, i))
+                aslist(sl[0], lu)
+                act(A(vmb(s), *c), vm, AF.Copy)
+                if r:
+                    wa, wb = A("WA%d" % (n % 2), 0, 8), A("WB%d" % (n % 2), 0, 8); ls = A("LS%d_%d" % (r, s), *c)
+                    ts(wa, A("MI", 128, 136), 2048.0, OP.add, DOWN, OP.mult); ts(wb, wa, 1023, OP.bitwise_and); cp(ls, wb)
+                send(1, A("LV%d_%d" % (r, s + 1), *c), ls if r else lu, "aV%d_%d_%d" % (r, s + 1, i), [A("UL0")])
                 zo = A("ZO%d_%d" % (r, s), 128 * i, 128 * i + 128)
                 gather("S", zo, A("X"), lu)
                 send(1, A("Z%d_%d" % (r, s + 1), 128 * i, 128 * i + 128), zo, "aZ%d_%d_%d" % (r, s + 1, i))
 
         def vmb(s): return "VMB%d" % s if s else "VMB0_%d" % r
 
+        def aslist(sl, lu):
+            w = width(lu); o = A("MI", 128, 128 + w)
+            together(lambda: [mm(o, A("DB", 15 - b, 143 - b), A(sl, b, 16 * w, 16), b == 0, b == 15) for b in range(16)])
+            ts(lu, o, 2048.0, OP.add)
+
+        def steps(out, io, at, v, c0, c1, share):
+            if share < 4: cp(A(at, c0, c1), v)
+            if share: ts(A(at + "B", c0, c1), v, -256.0, OP.mult, 128.0, OP.add)
+            for j in range(c0, c1):
+                o = A(out, 128 * j, 128 * j + 128)
+                if j % 4 < share: act(o, A("IO144", 0, 128), AF.Sigmoid, A(at + "B", j, j + 1), 256.0)
+                else: ts(o, A(io), A(at, j, j + 1), OP.is_ge)
+
         def codes():
             together(lambda: [mm(A("MI", 256 + 8 * i, 264 + 8 * i), A(z0[0], 128 * i, 128 * i + 128), A("WU"), True, True) for i in range(3)] +
                      [mm(A("MI", 288, 312), A("DUB", 15 - b, 143 - b), A(z0[0], b, 384, 16), b == 0, b == 15) for b in range(16)])
-            ts(A("UT"), A("MI", 256, 280), M4096, OP.add, M4096, OP.subtract); tt(A("U%d" % r), A("MI", 256, 280), A("UT"), OP.subtract)
+            ts(A("UT"), A("MI", 256, 280), MAG, OP.add, MAG, OP.subtract); tt(A("U%d" % r), A("MI", 256, 280), A("UT"), OP.subtract)
             tt(A("ID_"), A("MI", 288, 312), A("VL"), OP.add); ts(A("IC"), A("ID_"), 4095, OP.bitwise_and); cp(A("FA"), A("IC"))
             send(1, A("UL%d" % r), A("U%d" % r), "aU%d" % r)
             gather("S", A("WG"), A("IW"), A("LW"))
@@ -368,8 +395,7 @@ def rank_program(g, core, T, topo):
         def exdig(s):
             if s == 0: cp(A("EA"), A("W0"))
             else: ts(A("EA"), A("ML%d" % r), 2048.0, OP.add, DOWN, OP.mult)
-            ts(A("EB"), A("EA"), 127, OP.bitwise_and); cp(A("WL%d" % s), A("EB"))
-            for j in range(24): ts(A("YL%d" % s, 128 * j, 128 * j + 128), A("IOH"), A("WL%d" % s, j, j + 1), OP.is_equal)
+            ts(A("EB"), A("EA"), 127, OP.bitwise_and); steps("YL%d" % s, "IOH", "WL%d" % s, A("EB"), 0, 24, SHARE[s])
             ts(A("EC"), A("EA"), 7, OP.arith_shift_right, 7, OP.bitwise_and)
             tt(A("EG"), A("F%d_%d" % (r, s)), A("S1_%d" % s, 15, 384, 16), OP.subtract)
             ts(A("EH"), A("EG"), 128.0, OP.mult, -4.0, OP.add); tt(A("XC%d" % s), A("EH"), A("EC"), OP.add)
@@ -383,10 +409,10 @@ def rank_program(g, core, T, topo):
 
         def pendig(s, c0, c1):
             a, b, c = A("PA", c0, c1), A("PB_", c0, c1), A("PC", c0, c1)
-            ts(a, A(vmb(s), c0, c1), 2048.0, OP.add, DOWN, OP.mult)
+            ts(a, A(vmb(s), c0, c1) if s < 2 else A("MI", 160 + c0, 160 + c1), 2048.0, OP.add, DOWN, OP.mult)
             ts(c, a, 7, OP.arith_shift_right); ts(b, a, 127, OP.bitwise_and)
-            ts(A("LOB%d" % s, c0, c1), c, -1.0, OP.mult, -0.5, OP.add); cp(A("HP%d" % s, c0, c1), b)
-            for j in range(c0, c1): ts(A("HOH%d" % s, 128 * j, 128 * j + 128), A("IOB"), A("HP%d" % s, j, j + 1), OP.is_equal)
+            ts(A("LOB%d" % s, c0, c1), c, -1.0, OP.mult, -0.5, OP.add)
+            steps("HOH%d" % s, "IOB", "HP%d" % s, b, c0, c1, SHARE[1 + s + c0 // 16])
 
         def penadd(s, c0, c1, end=False):
             m = "GO%d_%d" % (r, s)
@@ -396,6 +422,17 @@ def rank_program(g, core, T, topo):
                 sg = A("SG%d" % s, 34 * j, 34 * j + 33)
                 act(sg, A("IO144", 0, 33), AF.Sign, A("LOB%d" % s, j, j + 1), A(m, j, j + 1))
                 mm(A("PEN", j % 8, 264, 8), A("HOH%d" % s, 128 * j, 128 * j + 128), sg, False, end and j == c1 - 1, True)
+
+        def penback():
+            ts(A("PC"), A("EA"), 7, OP.arith_shift_right); ts(A("LOB0"), A("PC"), -1.0, OP.mult, -0.5, OP.add)
+            ts(A("HP0"), A("ML%d" % r), 0.0, OP.not_equal); tt(A("FC0"), A("HP0"), A("GO%d_1" % r), OP.subtract)
+            mm(A("PN2", 0, 264), A("ZR", 0, 128, p1=1), A("ZR", 0, 264, p1=1), True, False, True)
+            for j in range(24):
+                sg = A("SG0", 34 * j, 34 * j + 33)
+                act(sg, A("IO144", 0, 33), AF.Sign, A("LOB0", j, j + 1), A("FC0", j, j + 1))
+                mm(A("PN2", j % 8, 264, 8), A("YL1", 128 * j, 128 * j + 128), sg, False, j == 23, True)
+            act(A("CB%d" % r), A("PN2", 0, 264), AF.Copy)
+            send(-1, A("CL%d" % r), A("CB%d" % r), "aC%d" % r)
 
         def settle():
             for j, (l, w) in enumerate((("LU%d_0", 1.0), ("LU%d_1", 1.0), ("LV%d_1", 3.0), ("LV%d_2", 3.0))):
@@ -418,54 +455,52 @@ def rank_program(g, core, T, topo):
             if last: dma("oyz", T.yz[:, :], ap(zn), 3 << 15, "Y", [zn], [])
 
         def passed(s):
-            if s == 0: ts(A("GO%d_0" % r), A("S1_0", 15, 384, 16), T0, OP.is_gt)
-            else: tt(A("GO%d_1" % r), A("S1_1", 15, 384, 16), A("FL%d_1" % r), OP.is_gt)
+            tt(A("GO%d_%d" % (r, s)), A("S1_%d" % s, 15, 384, 16), A("FL%d_1" % r if s else "TH3"), OP.is_gt)
 
         front(0); front(1); front(2)
-        for a in (1024, 2049, 3073):
-            src, d = A("O", 0, 1024), A("O", a, a + 1024)
-            dma("dcp%d" % r, ap(d), ap(src), 1 << 19, "Y", [src, A("X")], [d], (a // 1024 - 1) << 19)
         codes()
         for n in range(9):
             hear(n)
             if n < 6: front(n + 3)
             if n == 2:
                 send(1, A("ML%d" % r), A(vmb(0)), "aM%d" % r)
-                passed(0); own(); exdig(0); pendig(0, 0, 24); boats(A("LU%d_0" % r))
+                passed(0); own(); exdig(0); boats(A("LU%d_0" % r))
             if n == 5:
                 passed(1)
                 send(-1, A("GL%d_1" % r), A("GO%d_1" % r), "aG%d_1" % r); send(-1, A("LL%d_1" % r), A("LU%d_1" % r), "aL%d_1" % r)
-                for h in ("EX0", "EX1"): mm(A(h), A("ZR", 0, 128, p1=1), A("ZR", p1=1), True, False)
+                for h in ("EX0", "EX1"): mm(A(h), A("ONE16", p1=1), A("R1536", p1=1), True, False)
                 mm(A("PEN", 0, 264), A("ZR", 0, 128, p1=1), A("ZR", 0, 264, p1=1), True, False, True)
-                exadd(0, 0, 24); penadd(0, 0, 24); exdig(1); pendig(1, 0, 24); boats(A("LL%d_1" % r))
+                exadd(0, 0, 24); exdig(1); penback(); pendig(1, 0, 24); boats(A("LL%d_1" % r))
                 if not last: settle()
             if n == 7:
                 send(-1, A("GL%d_2" % r, 0, 16), A("GO%d_2" % r, 0, 16), "aG%d_2a" % r)
                 pendig(2, 0, 16); penadd(2, 0, 16); exadd(1, 0, 16); penadd(1, 0, 16)
-        send(-1, A("GL%d_2" % r, 16, 24), A("GO%d_2" % r, 16, 24), "aG%d_2b" % r); send(-2, A("LL%d_2" % r), A("LU%d_2" % r), "aL%d_2" % r)
+        send(-1, A("GL%d_2" % r, 16, 24), A("GO%d_2" % r, 16, 24), "aG%d_2b" % r)
         pendig(2, 16, 24); penadd(2, 16, 24); exadd(1, 16, 24); penadd(1, 16, 24, True)
+        aslist("SEL2", A("LU%d_2" % r)); send(-2, A("LL%d_2" % r), A("LU%d_2" % r), "aL%d_2" % r)
         boats(A("LL%d_2" % r))
         if last: dma("oyv", T.yv[:, :], ap(A("FA")), 1 << 14, "Y", [A("FA")], [])
         else:
             cp(A("VL"), A("FA")); ts(A("LWI"), A("VL"), 1023, OP.bitwise_and); cp(A("LW"), A("LWI"))
             ts(A("FI"), A("ID"), A("FCOL"), OP.mult); ts(A("NFI"), A("ID"), A("FCOL"), OP.mult, -1.0, OP.mult)
-        cp(A("C16"), A("PEN", 0, 264))
+        tt(A("C16"), A("PEN", 0, 264), A("CL%d" % r), OP.add)
         together(lambda: [mm(A("PEN", 128 * h, 128 * h + 128), A("C16", 128 * h + d, 128 * h + d + 128), A(w), d == 8, d == 0, True)
-                          for h in range(2) for d, w in ((8, "ID16"), (0, "NID16"))])
-        ts(A("HT"), A("PEN", 0, 256), 0.0, OP.is_gt)
+                          for h in range(2) for d, w in ((8, "DM"), (0, "NDM"))])
+        act(A("HT"), A("PEN", 0, 256), AF.Sign)
         for c in range(8):
-            d = ("D0", "D1", "D2", "KEY")[c % 4]; x = A("X", xcol(512 * c), xcol(512 * c) + 512)
+            d = ("D0", "D1", "PN2", "KEY")[c % 4]; x = A("X", xcol(512 * c), xcol(512 * c) + 512)
             mm(A(d), A("ID"), x, True, False)
             together(lambda: [mm(A(d, 128 * b, 128 * b + 128), A("WA", 128 * ((4 * c + b) % 16), 128 * ((4 * c + b) % 16) + 128),
                                  A("HT", 128 * (c // 4), 128 * (c // 4) + 128), False, b == 3, True) for b in range(4)])
-            if c in RELU_V: ts(x, A(d), 0.0, OP.max)
+            if c in RELU_V[r]: ts(x, A(d), 0.0, OP.max)
             else: act(x, A(d), AF.Relu)
             if last: dma("oyx", T.yx[:, 512 * c:512 * c + 512], ap(x), 1 << 17, "Y", [x], [], c << 17)
-        for h in range(2): act(A("EXS", 512 * h, 512 * h + 512), A("EX%d" % h), AF.Copy)
+        for h in range(2):
+            c = (512 * h, 512 * h + 512)
+            act(A("EXQ", *c), A("EX%d" % h), AF.Copy); tt(A("EXR", *c), A("EX%d" % h), A("EXQ", *c), OP.subtract)
         for h in range(2):
             e = "EX%d" % h; c = (512 * h, 512 * h + 512)
-            together(lambda: [run("P", 4 * 128 * PCY, [A("EXS", 4 * h + b, 1024, 8), A("ID32")], [A(e, 128 * b, 128 * b + 128)],
-                                  lambda b=b, e=e, h=h: g.tensor.transpose(ap(A(e, 128 * b, 128 * b + 128)), ap(A("EXS", 4 * h + b, 1024, 8)), ap(A("ID32")))) for b in range(4)])
+            together(lambda: [mm(A(e, 128 * b, 128 * b + 128), A("EXR", 4 * h + b, 1024, 8), A("DM4"), True, True) for b in range(4)])
             if not last: tt(A("O", *c), A(e), A("OT", *c), OP.add)
             else:
                 tt(A("OT", *c), A(e), A("O", *c), OP.add); ts(A("OM", *c), A("OT", *c), 4095, OP.bitwise_and)

@@ -7,7 +7,10 @@ REVERSE = True
 ZT_ON = "S"
 V_QUARTERS = {(0, 1), (0, 3), (1, 2)}
 N3 = 5
-RELU_V = ((5, 7), (1,))
+JOIN, ROT, ZTB = (), 0, ("KEY", 128, 256)
+BYDMA, ALT, SFIX, SGV = (), False, 0.0, ()
+VFIX = 15.0
+RELU_V = ((5, 7), (1, 3))
 SHARE = (2, 0, 2, 2, 0)
 
 
@@ -25,10 +28,10 @@ def _s(names, cols, dtype):
 _b("X", 4112, "bfloat16"); _b("OF", 4112, "float32"); _s("BM", 16, "float32"); _b("O OT OM", 1024, "int32"); _b("NB", 512, "int32"); _b("YN YH", 512, "float32")
 _b("XG0 XG1 XG2 NR0 NR1 IR", 2048, "bfloat16"); _b("SELC", 2048, "float16"); _b("WA", 2048, "bfloat16")
 _b("PO0 PO1 PO2 PO3", 128, "uint16"); _b("PI0 PI1", 128, "int32"); _b("PF0 PF1 PF2 PF3 SEL0 SEL1 ZT0 ZT1 IOH ID16 NID16", 128, "float16")
-_b("D0 D1 PN2 KEY MI EX0 EX1 PEN", 512, "float32", "psum"); _b("CB0 CB1 CL0 CL1", 264, "float16"); _b("SG0", 24 * 34, "float16"); _b("NO0 NO1", 128, "bfloat16"); _b("MB RST KF GF TH TH0 TH1", 128, "float32"); _s("TH3", 24, "float32")
+_b("D0 D1 D2 KEY MI EX0 EX1 PEN", 512, "float32", "psum"); _b("CB0 CB1 CL0 CL1", 264, "float16"); _b("SG0", 24 * 34, "float16"); _b("NO0 NO1", 128, "bfloat16"); _b("MB KF GF TH TH0 TH1", 128, "float32"); _b("RST", 128, "bfloat16"); _s("TH3", 24, "float32")
 _b("S1_0 S1_1 S1_2 WG RY", 384, "float32"); _b("SG1 SG2", 24 * 34, "bfloat16")
 _b("YL0 YL1 YU0 YU1", 24 * 128, "float16"); _b("HOH1 HOH2", 24 * 128, "bfloat16")
-_b("SEL2", 384, "float16"); _b("EXR EXQ", 1024, "float16"); _b("DM DM4 NDM ONE16", 128, "float16"); _b("R1536", 512, "float16"); _s("WL0B WL1B HP0B HP1B HP2B", 24, "float32")
+_b("SEL2", 384, "float16"); _b("EXR EXQ", 1024, "float16"); _b("DM DM4 NDM ONE16 BDH DIAG LM0 LM1", 128, "float16"); _b("R1536", 512, "float16"); _s("WL0B WL1B HP0B HP1B HP2B", 24, "float32")
 _s("WA0 WA1 WB0 WB1", 8, "int32"); _s("LS1_0 LS1_1", 24, "uint16")
 _b("IW", 1024, "float32"); _b("C16", 264, "float16"); _b("HT", 256, "bfloat16"); _b("ZR", 512, "float16")
 _s("VMB1 VMB2 LOB0 LOB1 LOB2 HP0 HP1 HP2 XC0 XC1 WL0 WL1 W0 FA BB BC BD EG EH FC0 FC1 UM0 UM1 UT CF", 24, "float32")
@@ -43,7 +46,8 @@ for _r in range(RO):
             _s("GL%d_%d" % (_r, _i), 24, "float32"); _s("FL%d_%d" % (_r, _i), 24, "int32"); _s("LV%d_%d LL%d_%d" % (_r, _i, _r, _i), 24, "uint16")
     _s("U%d UL%d VMB0_%d ML%d" % (_r, _r, _r, _r), 24, "float32")
 _b("RB RD ONE", 384, "bfloat16")
-_b("IOB ID HID NID FI NFI BD16 KB QROW GROW RP8", 128, "bfloat16"); _s("CI", 8, "int32")
+_b("NIH IOH128", 128, "float16"); _s("I128", 33, "float32"); _s("SB", 24, "float32")
+_b("NIB ID HID NID FI NFI BD16 KB QROW GROW RP8", 128, "bfloat16"); _s("CI", 8, "int32")
 _s("W8 WU", 8, "bfloat16"); _s("B8", 8, "float16"); _b("DB", 144, "float16"); _b("DUB", 144, "bfloat16"); _b("IO144", 144, "float32")
 _s("AL", 96, "float32"); _s("AR FCOL", 1, "float32"); _s("AC", 1, "bfloat16"); _s("AI AJ", 1, "int32")
 for _d in POOL:
@@ -61,6 +65,7 @@ MAG = 12582912.0
 M4096 = MAG * 4096
 UP, DOWN, EPS = 4097 / 4096, 4095 / 4096, 0.00015
 T0 = 34816.0
+M128, STEEP, NOBOAT = MAG * 128, 1048576.0, 63.5 - 2048 * DOWN
 CY, PCY, GCY, LAT, HOP, DMA0, DMAB = 0.83, 0.42, 1.56 * 0.83, 205.0, 2200.0, 1500.0, 190.0
 
 
@@ -124,14 +129,16 @@ def schedule(ops):
         return max(at[i] + ops[i][2] for i in range(n)), order, [-at[i] - ops[i][1] for i in range(n)]
 
     best = once(deps, list(range(n)), 0.0)
-    for ahead in AHEAD:
-        now = best
-        for _ in range(PASSES):
-            now = once(deps, once(back, now[2], ahead)[2], ahead)
+    for turn in range(TURNS):
+        now = best; ahead = AHEAD[turn % len(AHEAD)]
+        for k in range(PASSES):
+            rank = [x + (i * 7919 + turn * 104729) % 1009 * BLUR * (turn >= len(AHEAD) and k == 0) for i, x in enumerate(now[2])]
+            now = once(deps, once(back, rank, ahead)[2], ahead)
             if now[0] < best[0]: best = now
     return best[1]
 
 
+TURNS, BLUR = 14, 0.3
 ORDER, PASSES, AHEAD, SLIP = [], 4, (0.0, 100.0, 200.0, 300.0, 150.0, 250.0), 30.0
 
 
@@ -194,6 +201,7 @@ def rank_program(g, core, T, topo):
     group = []
 
     def run(q, cost, reads, writes, call):
+        if q == "V": cost += VFIX
         if group: group[0].append((cost, reads, writes, call))
         else: ops.append((q, cost, cost + LAT, reads, writes, lambda: issue(q, reads, writes, call)))
 
@@ -250,7 +258,7 @@ def rank_program(g, core, T, topo):
 
     def act(out, a, f, bias=0.0, scale=1.0):
         v, r = col(bias); v2, r2 = col(scale)
-        run("S", CY * max(64, width(out)), [a] + r + r2, [out], lambda: g.scalar.activation(ap(out), ap(a), f, bias=v, scale=v2))
+        run("S", SFIX + CY * max(64, width(out)), [a] + r + r2, [out], lambda: g.scalar.activation(ap(out), ap(a), f, bias=v, scale=v2))
 
     def gather(q, out, win, off):
         if q == "V": run("V", 50 + 16 * width(off) * GCY, [win, off], [out], lambda: g.vector.tensor_copy(ap(out), ap(win).indirect(ap(off))))
@@ -275,7 +283,7 @@ def rank_program(g, core, T, topo):
     for b in range(4): iota(A("IR", 512 * b, 512 * b + 512), [[1, 32], [0, 16]], 32 * b, 0)
     for b in range(2): iota(A("IW", 512 * b, 512 * b + 512), [[1, 512]], 512 * b, 0)
     io, part, p16, g16 = A("IO144", 0, 128), A("CF", 0, 1), A("CF", 4, 5), A("CF", 8, 9)
-    ms(A("ONE"), 1.0); ms(A("QROW", p1=1), -0.25); ms(A("GROW", p1=1), 512.0); ms(A("PB", 4, 5), 32768.0)
+    ms(A("ONE"), 1.0); ms(A("QROW", p1=1), -0.25); ms(A("GROW", p1=1), 512.0); ms(A("PB", 4, 5), 32768.0); ms(A("CF", 3, 4), -STEEP / 2)
     cp(part, A("CI", 0, 1))
     ts(A("CI", 4, 5), A("CI", 0, 1), 15, OP.bitwise_and); cp(p16, A("CI", 4, 5)); tt(g16, part, p16, OP.subtract)
     ts(A("ID"), io, part, OP.is_equal)
@@ -291,17 +299,19 @@ def rank_program(g, core, T, topo):
     tt(A("KB", p1=2), A("TH0", p1=2), A("TH1", p1=2), OP.add)
     ts(A("TH"), A("GF"), 65536.0, OP.mult, T0, OP.add); ms(A("TH0"), 0.0); ms(A("TH1"), 0.0)
     for i in range(3): act(A("TH3", 8 * i, 8 * i + 8), A("TH", 0, 128, 16), AF.Copy)
-    ts(A("RST"), A("KF"), 0.0, OP.is_equal, -4194304.0, OP.mult)
+    act(A("RST"), A("KF"), AF.Sigmoid, A("CF", 3, 4), STEEP)
     for b in range(4): ts(A("SELC", 512 * b, 512 * b + 512), A("IR", 512 * b, 512 * b + 512), part, OP.is_equal)
     ts(A("B8"), A("I16"), g16, OP.is_equal); ts(A("B1"), A("I16"), part, OP.is_equal)
     ts(A("DB"), A("IO144"), A("CF", 12, 13), OP.is_equal)
     ts(A("WU"), A("I16"), g16, OP.is_equal, A("CF", 16, 17), OP.mult)
     ts(A("DUB"), A("IO144"), A("CF", 12, 13), OP.is_equal, A("CF", 16, 17), OP.mult)
-    act(A("HID"), A("ID"), AF.Copy, 0.0, 0.5); act(A("NID"), A("ID"), AF.Copy, 0.0, -1.0); act(A("IOH"), io, AF.Copy); act(A("IOB"), io, AF.Copy)
+    act(A("HID"), A("ID"), AF.Copy, 0.0, 0.5); act(A("NID"), A("ID"), AF.Copy, 0.0, -1.0); act(A("IOH"), io, AF.Copy)
+    act(A("NIB"), io, AF.Copy, 63.0, -1.0); act(A("NIH"), io, AF.Copy, 63.0, -1.0); act(A("IOH128"), io, AF.Copy, 0.0, 128.0); act(A("I128"), A("IO144", 0, 33), AF.Copy, -64.0, 128.0)
     ts(A("CF", 22, 23), part, 1.0, OP.add); ts(A("DM"), io, A("CF", 22, 23), OP.is_equal); tt(A("DM"), A("ID"), A("DM"), OP.subtract)
     act(A("DM4"), A("DM"), AF.Copy, 0.0, 4096.0); act(A("NDM"), A("DM"), AF.Copy, 0.0, -1.0); act(A("WU"), A("WU"), AF.Copy, 0.0, 1 / 4096)
     for nm, c in (("R1536", 1536.0), ("ONE16", 1.0), ("ZR", 0.0)): act(A(nm, p1=1), A("IR", 0, width(A(nm)), p1=1), AF.Copy, c, 0.0)
     ts(A("BD16"), A("GF"), 16.0, OP.mult, g16, OP.is_equal)
+    if ALT: act(A("BDH"), A("BD16"), AF.Copy); ts(A("DIAG"), A("KF"), p16, OP.is_equal)
     ts(A("CI", 2, 3), A("CI", 0, 1), 7, OP.bitwise_and); cp(A("CF", 20, 21), A("CI", 2, 3))
     ts(A("CI", 3, 4), A("CI", 0, 1), 3, OP.arith_shift_right); cp(A("CF", 21, 22), A("CI", 3, 4))
     ts(A("RP8"), A("GF"), A("CF", 20, 21), OP.is_equal, -45.0, OP.mult); ts(A("BM"), A("IO144", 0, 16), A("CF", 21, 22), OP.is_equal)
@@ -309,10 +319,15 @@ def rank_program(g, core, T, topo):
         act(A("WA", 128 * a, 128 * a + 128), A("RP8"), AF.Copy, 0.0, A("BM", a, a + 1))
     ts(A("LWI"), A("VL"), 1023, OP.bitwise_and); cp(A("LW"), A("LWI"))
     ts(A("OT", 0, 512), A("NB"), 4095, OP.bitwise_and); ts(A("OT", 512, 1024), A("NB"), 12, OP.arith_shift_right)
-    for h in (0, 512):
-        ts(A("OF", h, h + 512), A("OT", h, h + 512), UP, OP.mult, EPS, OP.add)
-        for a in (1024, 2049, 3073):
-            act(A("OF", a + h, a + h + 512), A("OF", h, h + 512), AF.Copy)
+
+    def columns(o):
+        for h in (0, 512):
+            ts(A("OF", h, h + 512), A(o, h, h + 512), UP, OP.mult, EPS, OP.add)
+            for a in (1024, 2049, 3073):
+                src, d = A("OF", h, h + 512), A("OF", a + h, a + h + 512)
+                if o == "OM" and a in BYDMA: dma("dcp%d" % (h // 512), ap(d), ap(src), 1 << 18, "Y", [src], [d], (BYDMA.index(a) + h // 512 * len(BYDMA)) << 18)
+                else: act(d, src, AF.Copy)
+    columns("OT")
 
     def round_(r):
         last = r == RO - 1
@@ -320,8 +335,8 @@ def rank_program(g, core, T, topo):
 
         def front(n):
             s, i = divmod(n, 3)
-            po = A("PO%d" % (n % 4)); l = A("LV%d_%d" % (r, s), 8 * i, 8 * i + 8) if s else A("LW", 8 * i, 8 * i + 8); w = A("O") if r else A("OF", 0, 4112 if s else 1024)
-            if r == 0: gather("V", po, w, l)
+            po = A("PO%d" % (n % 4)); l = A("LV%d_%d" % (r, s), 8 * i, 8 * i + 8) if s else A("LW", 8 * i, 8 * i + 8); w = A("O") if r and not s else A("OF", 0, 4112 if s else 1024)
+            if r == 0 or s: gather("V", po, w, l)
             else:
                 pi = A("PI%d" % (n % 2))
                 ts(pi, w, 4095, OP.bitwise_and, off=l); ts(po, pi, UP, OP.mult, EPS, OP.add)
@@ -329,25 +344,24 @@ def rank_program(g, core, T, topo):
             b = 0
             while b < 4:
                 q = "V" if (n, b) in V_QUARTERS else "S"; e = b + 1
-                if q == "S" and b % 2 == 0 and (n, e) not in V_QUARTERS: e += 1
+                if q == "S" and b in JOIN and (n, e) not in V_QUARTERS: e += 1
                 gather(q, A("XG%d" % (n % 3), 512 * b, 512 * e), A("X"), A(po[0], 32 * b, 32 * e)); b = e
 
         def hear(n):
-            s, i = divmod(n, 3); c = (8 * i, 8 * i + 8); zt = A("ZT%d" % (n % 2)); nr = "NR%d" % (n % 2); key = A("KEY", 0, 128)
-            mm(A("KEY", 128, 256), A("Z%d_%d" % (r, s), 128 * i, 128 * i + 128), A("NFI"), True, True)
-            if ZT_ON == "S": act(zt, A("KEY", 128, 256), AF.Copy)
-            else: cp(zt, A("KEY", 128, 256))
+            s, i = divmod(n, 3); c = (8 * i, 8 * i + 8); zt = A("ZT%d" % (n % 2)); nr = "NR%d" % (n % 2); ko = ROT * (n % 2); key = A("KEY", ko, ko + 128)
+            mm(A(*ZTB), A("Z%d_%d" % (r, s), 128 * i, 128 * i + 128), A("NFI"), True, True)
+            act(zt, A(*ZTB), AF.Copy)
             for b in range(4):
-                d = A(("D0", "D1", "PN2")[(4 * n + b) % 3] if n < N3 else "D%d" % (b % 2))
+                d = A("D%d" % ((4 * n + b) % 3))
                 together(lambda: (mm(d, A("FI"), A("XG%d" % (n % 3), 512 * b, 512 * b + 512), True, False), mm(d, zt, A("SELC", 512 * b, 512 * b + 512), False, True)))
                 ts(A(nr, 512 * b, 512 * b + 512), d, MAG, OP.add, MAG, OP.is_equal)
             together(lambda: [mm(key, A("ONE", 0, 128, p1=2), A("KB", p1=2), True, False)] +
-                     [mm(A("KEY", k, 128, 16), A(nr, k, 2048, 16), A("W8"), False, k == 15) for k in range(16)])
+                     [mm(A("KEY", ko + k, ko + 128, 16), A(nr, k, 2048, 16), A("W8"), False, k == 15) for k in range(16)])
             s1 = A("S1_%d" % s, 128 * i, 128 * i + 128); m = A("S1_%d" % s, 128 * i + 15, 128 * i + 128, 16); no = A("NO%d" % (n % 2))
             go = A("GO%d_%d" % (r, s), *c); fl = A("FL%d_%d" % (r, s), *c) if s else None; th = "TH%d" % (n % 2) if s else "TH"
             if s: cp(A(th, 0, 128, 16), fl)
             scan(s1, A(th), key, OP.max)
-            scan(A("MB", 0, 128, -1), A("RST"), s1[:3] + (-1,) + s1[4:], OP.add); tt(no, key, A("MB"), OP.is_ge)
+            scan(A("MB", 0, 128, -1), A("RST"), s1[:3] + (-1,) + s1[4:], OP.mult); tt(no, key, A("MB"), OP.is_ge)
             if s == 2: tt(go, m, fl, OP.is_gt)
             if s < 2:
                 ts(A("F%d_%d" % (r, s), *c), m, 0.5, OP.add)
@@ -355,14 +369,16 @@ def rank_program(g, core, T, topo):
             sl = A("SEL%d" % (n % 2)) if s < 2 else A("SEL2", 128 * i, 128 * i + 128); lu = A("LU%d_%d" % (r, s), *c); vm = A("MI", 160 + c[0], 160 + c[1])
             mm(A("MI", 0, 128), no, A("ID"), True, True)
             tt(sl, A("MI", 0, 128), A("PF%d" % (n % 4)), OP.mult)
-            mm(vm, sl, A("B8"), True, True)
+            if s == 2 or not ALT:
+                mm(vm, sl, A("B8"), True, True)
+                if s < 2: aslist(sl[0], lu); act(A(vmb(s), *c), vm, AF.Copy, NOBOAT, -DOWN)
+            else:
+                lm = A("LM%d" % (n % 2))
+                mm(A("MI", 384, 512), sl, A("BDH"), True, True); tt(lm, A("MI", 384, 512), A("DIAG"), OP.mult)
+                act(A(vmb(s), *c), A("MI", 384, 512, 16), AF.Copy, NOBOAT, -DOWN)
+                mm(A("MI", 128, 136), lm, A("B8"), True, True); ts(lu, A("MI", 128, 136), 2048.0, OP.add)
             if s < 2:
-                aslist(sl[0], lu)
-                act(A(vmb(s), *c), vm, AF.Copy)
-                if r:
-                    wa, wb = A("WA%d" % (n % 2), 0, 8), A("WB%d" % (n % 2), 0, 8); ls = A("LS%d_%d" % (r, s), *c)
-                    ts(wa, A("MI", 128, 136), 2048.0, OP.add, DOWN, OP.mult); ts(wb, wa, 1023, OP.bitwise_and); cp(ls, wb)
-                send(1, A("LV%d_%d" % (r, s + 1), *c), ls if r else lu, "aV%d_%d_%d" % (r, s + 1, i), [A("UL0")])
+                send(1, A("LV%d_%d" % (r, s + 1), *c), lu, "aV%d_%d_%d" % (r, s + 1, i), [A("UL0")])
                 zo = A("ZO%d_%d" % (r, s), 128 * i, 128 * i + 128)
                 gather("S", zo, A("X"), lu)
                 send(1, A("Z%d_%d" % (r, s + 1), 128 * i, 128 * i + 128), zo, "aZ%d_%d_%d" % (r, s + 1, i))
@@ -374,13 +390,14 @@ def rank_program(g, core, T, topo):
             together(lambda: [mm(o, A("DB", 15 - b, 143 - b), A(sl, b, 16 * w, 16), b == 0, b == 15) for b in range(16)])
             ts(lu, o, 2048.0, OP.add)
 
-        def steps(out, io, at, v, c0, c1, share):
-            if share < 4: cp(A(at, c0, c1), v)
-            if share: ts(A(at + "B", c0, c1), v, -256.0, OP.mult, 128.0, OP.add)
+        def steps(out, io, an, nj, c0, c1, share):
+            ts(A(nj, c0, c1), A(an, c0, c1), M128, OP.add, M128, OP.subtract)
+            if share:
+                tt(A("SB", c0, c1), A(an, c0, c1), A(nj, c0, c1), OP.subtract); ts(A(nj + "B", c0, c1), A("SB", c0, c1), -63.0, OP.add, STEEP, OP.mult)
             for j in range(c0, c1):
                 o = A(out, 128 * j, 128 * j + 128)
-                if j % 4 < share: act(o, A("IO144", 0, 128), AF.Sigmoid, A(at + "B", j, j + 1), 256.0)
-                else: ts(o, A(io), A(at, j, j + 1), OP.is_ge)
+                if j % 4 < share: act(o, A("IO144", 0, 128), AF.Sigmoid, A(nj + "B", j, j + 1), STEEP)
+                else: ts(o, A(io), A(nj, j, j + 1), OP.add, A(an, j, j + 1), OP.is_lt)
 
         def codes():
             together(lambda: [mm(A("MI", 256 + 8 * i, 264 + 8 * i), A(z0[0], 128 * i, 128 * i + 128), A("WU"), True, True) for i in range(3)] +
@@ -390,29 +407,26 @@ def rank_program(g, core, T, topo):
             send(1, A("UL%d" % r), A("U%d" % r), "aU%d" % r)
             gather("S", A("WG"), A("IW"), A("LW"))
             together(lambda: [mm(A("MI", 320 + 8 * i, 328 + 8 * i), A("WG", 128 * i, 128 * i + 128), A("B1"), True, True) for i in range(3)])
-            act(A("W0"), A("MI", 320, 344), AF.Copy)
+            act(A("W0"), A("MI", 320, 344), AF.Copy, 63.5, -1.0)
 
         def exdig(s):
-            if s == 0: cp(A("EA"), A("W0"))
-            else: ts(A("EA"), A("ML%d" % r), 2048.0, OP.add, DOWN, OP.mult)
-            ts(A("EB"), A("EA"), 127, OP.bitwise_and); steps("YL%d" % s, "IOH", "WL%d" % s, A("EB"), 0, 24, SHARE[s])
-            ts(A("EC"), A("EA"), 7, OP.arith_shift_right, 7, OP.bitwise_and)
+            steps("YL%d" % s, "NIH", "ML%d" % r if s else "W0", "WL%d" % s, 0, 24, SHARE[s])
             tt(A("EG"), A("F%d_%d" % (r, s)), A("S1_%d" % s, 15, 384, 16), OP.subtract)
-            ts(A("EH"), A("EG"), 128.0, OP.mult, -4.0, OP.add); tt(A("XC%d" % s), A("EH"), A("EC"), OP.add)
+            if s == 0: ts(A("EH"), A("EG"), 16384.0, OP.mult, -512.0, OP.add); tt(A("XC0"), A("EH"), A("WL0"), OP.subtract)
+            else:
+                ts(A("EA"), A("ML%d" % r), -1.0, OP.mult, 63.5, OP.add); ts(A("EC"), A("EA"), 7, OP.arith_shift_right, 7, OP.bitwise_and)
+                ts(A("EH"), A("EG"), 128.0, OP.mult, -4.0, OP.add); tt(A("XC1"), A("EH"), A("EC"), OP.add)
 
         def exadd(s, c0, c1):
             tt(A("UM%d" % s, c0, c1), A(("UL%d" if s else "U%d") % r, c0, c1), A("GL%d_%d" % (r, s + 1), c0, c1), OP.mult)
             for j in range(c0, c1):
                 q = j % 8; y = A("YU%d" % s, 128 * j, 128 * j + 128)
-                ts(y, A("IOH"), A("XC%d" % s, j, j + 1), OP.is_equal, A("UM%d" % s, j, j + 1), OP.mult)
+                ts(y, A("IOH" if s else "IOH128"), A("XC%d" % s, j, j + 1), OP.is_equal, A("UM%d" % s, j, j + 1), OP.mult)
                 mm(A("EX%d" % (q // 4), q % 4 * 128, q % 4 * 128 + 128), A("YL%d" % s, 128 * j, 128 * j + 128), y, False, s == 1 and j in (19, 23), True)
 
         def pendig(s, c0, c1):
-            a, b, c = A("PA", c0, c1), A("PB_", c0, c1), A("PC", c0, c1)
-            ts(a, A(vmb(s), c0, c1) if s < 2 else A("MI", 160 + c0, 160 + c1), 2048.0, OP.add, DOWN, OP.mult)
-            ts(c, a, 7, OP.arith_shift_right); ts(b, a, 127, OP.bitwise_and)
-            ts(A("LOB%d" % s, c0, c1), c, -1.0, OP.mult, -0.5, OP.add)
-            steps("HOH%d" % s, "IOB", "HP%d" % s, b, c0, c1, SHARE[1 + s + c0 // 16])
+            if s == 2: act(A(vmb(s), c0, c1), A("MI", 160 + c0, 160 + c1), AF.Copy, NOBOAT, -DOWN)
+            steps("HOH%d" % s, "NIB", vmb(s), "HP%d" % s, c0, c1, SHARE[1 + s + c0 // 16])
 
         def penadd(s, c0, c1, end=False):
             m = "GO%d_%d" % (r, s)
@@ -420,18 +434,18 @@ def rank_program(g, core, T, topo):
                 tt(A("FC%d" % s, c0, c1), A(m, c0, c1), A("GL%d_%d" % (r, s + 1), c0, c1), OP.subtract); m = "FC%d" % s
             for j in range(c0, c1):
                 sg = A("SG%d" % s, 34 * j, 34 * j + 33)
-                act(sg, A("IO144", 0, 33), AF.Sign, A("LOB%d" % s, j, j + 1), A(m, j, j + 1))
+                act(sg, A("I128"), AF.Sign, A("HP%d" % s, j, j + 1), A(m, j, j + 1))
                 mm(A("PEN", j % 8, 264, 8), A("HOH%d" % s, 128 * j, 128 * j + 128), sg, False, end and j == c1 - 1, True)
 
         def penback():
-            ts(A("PC"), A("EA"), 7, OP.arith_shift_right); ts(A("LOB0"), A("PC"), -1.0, OP.mult, -0.5, OP.add)
-            ts(A("HP0"), A("ML%d" % r), 0.0, OP.not_equal); tt(A("FC0"), A("HP0"), A("GO%d_1" % r), OP.subtract)
-            mm(A("PN2", 0, 264), A("ZR", 0, 128, p1=1), A("ZR", 0, 264, p1=1), True, False, True)
+            ts(A("HP0"), A("ML%d" % r), NOBOAT, OP.not_equal); tt(A("FC0"), A("HP0"), A("GO%d_1" % r), OP.subtract)
+            zero = lambda: mm(A("PEN", 0, 264), A("ZR", 0, 128, p1=1), A("ZR", 0, 264, p1=1), True, False, True)
+            zero()
             for j in range(24):
                 sg = A("SG0", 34 * j, 34 * j + 33)
-                act(sg, A("IO144", 0, 33), AF.Sign, A("LOB0", j, j + 1), A("FC0", j, j + 1))
-                mm(A("PN2", j % 8, 264, 8), A("YL1", 128 * j, 128 * j + 128), sg, False, j == 23, True)
-            act(A("CB%d" % r), A("PN2", 0, 264), AF.Copy)
+                act(sg, A("I128"), AF.Sign, A("WL1", j, j + 1), A("FC0", j, j + 1))
+                mm(A("PEN", j % 8, 264, 8), A("YL1", 128 * j, 128 * j + 128), sg, False, j == 23, True)
+            act(A("CB%d" % r), A("PEN", 0, 264), AF.Copy); zero()
             send(-1, A("CL%d" % r), A("CB%d" % r), "aC%d" % r)
 
         def settle():
@@ -458,6 +472,9 @@ def rank_program(g, core, T, topo):
             tt(A("GO%d_%d" % (r, s)), A("S1_%d" % s, 15, 384, 16), A("FL%d_1" % r if s else "TH3"), OP.is_gt)
 
         front(0); front(1); front(2)
+        if r:
+            for h in (0, 512): ts(A("OM", h, h + 512), A("O", h, h + 512), 4095, OP.bitwise_and)
+            columns("OM")
         codes()
         for n in range(9):
             hear(n)
@@ -469,7 +486,6 @@ def rank_program(g, core, T, topo):
                 passed(1)
                 send(-1, A("GL%d_1" % r), A("GO%d_1" % r), "aG%d_1" % r); send(-1, A("LL%d_1" % r), A("LU%d_1" % r), "aL%d_1" % r)
                 for h in ("EX0", "EX1"): mm(A(h), A("ONE16", p1=1), A("R1536", p1=1), True, False)
-                mm(A("PEN", 0, 264), A("ZR", 0, 128, p1=1), A("ZR", 0, 264, p1=1), True, False, True)
                 exadd(0, 0, 24); exdig(1); penback(); pendig(1, 0, 24); boats(A("LL%d_1" % r))
                 if not last: settle()
             if n == 7:
@@ -488,7 +504,7 @@ def rank_program(g, core, T, topo):
                           for h in range(2) for d, w in ((8, "DM"), (0, "NDM"))])
         act(A("HT"), A("PEN", 0, 256), AF.Sign)
         for c in range(8):
-            d = ("D0", "D1", "PN2", "KEY")[c % 4]; x = A("X", xcol(512 * c), xcol(512 * c) + 512)
+            d = ("D0", "D1", "D2", "KEY")[c % 4]; x = A("X", xcol(512 * c), xcol(512 * c) + 512)
             mm(A(d), A("ID"), x, True, False)
             together(lambda: [mm(A(d, 128 * b, 128 * b + 128), A("WA", 128 * ((4 * c + b) % 16), 128 * ((4 * c + b) % 16) + 128),
                                  A("HT", 128 * (c // 4), 128 * (c // 4) + 128), False, b == 3, True) for b in range(4)])

@@ -9,9 +9,9 @@ V_QUARTERS = {(0, 1), (0, 3), (1, 2)}
 N3 = 5
 JOIN, ROT, ZTB = (), 0, ("KEY", 128, 256)
 BYDMA, ALT, SFIX, SGV = (), False, 0.0, ()
-VFIX = 15.0
+VFIX, NARROW = 0.0, True
 RELU_V = ((5, 7), (1, 3))
-SHARE = (2, 0, 2, 2, 0)
+SHARE = (0, 0, 0, 0, 0)
 
 
 def _b(names, cols, dtype, where="sbuf"):
@@ -28,28 +28,29 @@ def _s(names, cols, dtype):
 _b("X", 4112, "bfloat16"); _b("OF", 4112, "float32"); _s("BM", 16, "float32"); _b("O OT OM", 1024, "int32"); _b("NB", 512, "int32"); _b("YN YH", 512, "float32")
 _b("XG0 XG1 XG2 NR0 NR1 IR", 2048, "bfloat16"); _b("SELC", 2048, "float16"); _b("WA", 2048, "bfloat16")
 _b("PO0 PO1 PO2 PO3", 128, "uint16"); _b("PI0 PI1", 128, "int32"); _b("PF0 PF1 PF2 PF3 SEL0 SEL1 ZT0 ZT1 IOH ID16 NID16", 128, "float16")
-_b("D0 D1 D2 KEY MI EX0 EX1 PEN", 512, "float32", "psum"); _b("CB0 CB1 CL0 CL1", 264, "float16"); _b("SG0", 24 * 34, "float16"); _b("NO0 NO1", 128, "bfloat16"); _b("MB KF GF TH TH0 TH1", 128, "float32"); _b("RST", 128, "bfloat16"); _s("TH3", 24, "float32")
+_b("D0 D1 D2 KEY MI EX0 EX1 PEN", 512, "float32", "psum"); _b("CB0 CB1 CL0 CL1", 264, "float16"); _b("SG0", 24 * 34, "float16"); _b("NO0 NO1", 128, "bfloat16"); _b("MB KF GF TH", 128, "float32"); _b("TH1 TH2", 384, "float32"); _s("EF FB", 24, "float32"); _b("RST", 128, "bfloat16"); _s("TH3", 24, "float32")
 _b("S1_0 S1_1 S1_2 WG RY", 384, "float32"); _b("SG1 SG2", 24 * 34, "bfloat16")
 _b("YL0 YL1 YU0 YU1", 24 * 128, "float16"); _b("HOH1 HOH2", 24 * 128, "bfloat16")
 _b("SEL2", 384, "float16"); _b("EXR EXQ", 1024, "float16"); _b("DM DM4 NDM ONE16 BDH DIAG LM0 LM1", 128, "float16"); _b("R1536", 512, "float16"); _s("WL0B WL1B HP0B HP1B HP2B", 24, "float32")
 _s("WA0 WA1 WB0 WB1", 8, "int32"); _s("LS1_0 LS1_1", 24, "uint16")
 _b("IW", 1024, "float32"); _b("C16", 264, "float16"); _b("HT", 256, "bfloat16"); _b("ZR", 512, "float16")
-_s("VMB1 VMB2 LOB0 LOB1 LOB2 HP0 HP1 HP2 XC0 XC1 WL0 WL1 W0 FA BB BC BD EG EH FC0 FC1 UM0 UM1 UT CF", 24, "float32")
+_s("VMB1 VMB2 LOB0 LOB1 LOB2 HP0 HP1 HP2 WL0 WL1 W0 FA BB BC BD EG EH FC0 FC1 UT CF", 24, "float32")
+_s("WL0C WL1C HP1C HP2C", 24, "bfloat16"); _s("XC0 XC1 UM0 UM1", 24, "float16")
 _s("VL ID_ IC LWI BI EA EB EC PA PB_ PC", 24, "int32"); _s("LW", 24, "uint16"); _s("PB I16 B1", 8, "float32")
 for _r in range(RO):
     for _i in range(3):
         _b("Z%d_%d" % (_r, _i), 384, "bfloat16")
         _s("GO%d_%d" % (_r, _i), 24, "float32"); _s("LU%d_%d" % (_r, _i), 24, "uint16")
         if _i < 2:
-            _s("F%d_%d" % (_r, _i), 24, "int32"); _b("ZO%d_%d" % (_r, _i), 384, "bfloat16")
+            _s("F%d_%d" % (_r, _i), 24, "float32"); _b("ZO%d_%d" % (_r, _i), 384, "bfloat16")
         if _i > 0:
-            _s("GL%d_%d" % (_r, _i), 24, "float32"); _s("FL%d_%d" % (_r, _i), 24, "int32"); _s("LV%d_%d LL%d_%d" % (_r, _i, _r, _i), 24, "uint16")
+            _s("GL%d_%d" % (_r, _i), 24, "float32"); _s("FL%d_%d" % (_r, _i), 24, "float32"); _s("LV%d_%d LL%d_%d" % (_r, _i, _r, _i), 24, "uint16")
     _s("U%d UL%d VMB0_%d ML%d" % (_r, _r, _r, _r), 24, "float32")
 _b("RB RD ONE", 384, "bfloat16")
 _b("NIH IOH128", 128, "float16"); _s("I128", 33, "float32"); _s("SB", 24, "float32")
 _b("NIB ID HID NID FI NFI BD16 KB QROW GROW RP8", 128, "bfloat16"); _s("CI", 8, "int32")
 _s("W8 WU", 8, "bfloat16"); _s("B8", 8, "float16"); _b("DB", 144, "float16"); _b("DUB", 144, "bfloat16"); _b("IO144", 144, "float32")
-_s("AL", 96, "float32"); _s("AR FCOL", 1, "float32"); _s("AC", 1, "bfloat16"); _s("AI AJ", 1, "int32")
+_s("AL", 96, "float32"); _s("AR FCOL", 1, "float32"); _s("AC PT", 1, "bfloat16"); _s("AI AJ", 1, "int32")
 for _d in POOL:
     _b("pool_" + _d, POOL[_d], _d)
 
@@ -64,9 +65,9 @@ for _r in range(RO):
 MAG = 12582912.0
 M4096 = MAG * 4096
 UP, DOWN, EPS = 4097 / 4096, 4095 / 4096, 0.00015
-T0 = 34816.0
+T0, WHOLE = 34816.0, 8388608.0
 M128, STEEP, NOBOAT = MAG * 128, 1048576.0, 63.5 - 2048 * DOWN
-CY, PCY, GCY, LAT, HOP, DMA0, DMAB = 0.83, 0.42, 1.56 * 0.83, 205.0, 2200.0, 1500.0, 190.0
+CY, PCY, GCY, LAT, HOP, DMA0, DMAB = 0.83, 0.42, 1.56 * 0.83, 165.0, 2200.0, 1500.0, 330.0
 
 
 def A(name, c0=0, c1=None, step=1, p0=0, p1=128):
@@ -238,7 +239,7 @@ def rank_program(g, core, T, topo):
     def ts(out, in0, s1, op0, s2=None, op1=None, off=None):
         v1, r1 = col(s1); v2, r2 = col(s2); tail = (op0,) if op1 is None else (op0, op1)
         if off: run("V", 50 + 16 * width(off) * GCY, [in0, off], [out], lambda: g.vector.tensor_scalar(ap(out), ap(in0).indirect(ap(off)), v1, v2, *tail))
-        else: run("V", vc(width(out), out, in0), [in0] + r1 + r2, [out], lambda: g.vector.tensor_scalar(ap(out), ap(in0), v1, v2, *tail))
+        else: run("V", vc(width(out), out, in0, *(r1 + r2)), [in0] + r1 + r2, [out], lambda: g.vector.tensor_scalar(ap(out), ap(in0), v1, v2, *tail))
 
     def tt(out, a, b, op):
         run("V", CY * max(64, width(out) * (1 if psum(a) or psum(b) else 2)), [a, b], [out], lambda: g.vector.tensor_tensor(ap(out), ap(a), ap(b), op))
@@ -283,7 +284,7 @@ def rank_program(g, core, T, topo):
     for b in range(4): iota(A("IR", 512 * b, 512 * b + 512), [[1, 32], [0, 16]], 32 * b, 0)
     for b in range(2): iota(A("IW", 512 * b, 512 * b + 512), [[1, 512]], 512 * b, 0)
     io, part, p16, g16 = A("IO144", 0, 128), A("CF", 0, 1), A("CF", 4, 5), A("CF", 8, 9)
-    ms(A("ONE"), 1.0); ms(A("QROW", p1=1), -0.25); ms(A("GROW", p1=1), 512.0); ms(A("PB", 4, 5), 32768.0); ms(A("CF", 3, 4), -STEEP / 2)
+    ms(A("ONE"), 1.0); ms(A("QROW", p1=1), -0.25); ms(A("GROW", p1=1), 512.0); ms(A("PB", 4, 5), 32768.0)
     cp(part, A("CI", 0, 1))
     ts(A("CI", 4, 5), A("CI", 0, 1), 15, OP.bitwise_and); cp(p16, A("CI", 4, 5)); tt(g16, part, p16, OP.subtract)
     ts(A("ID"), io, part, OP.is_equal)
@@ -294,13 +295,14 @@ def rank_program(g, core, T, topo):
         ts(A("PB", 0, 1), A("CI", 1, 2), 2.0 ** -(1 << b) - 1.0, OP.mult, 1.0, OP.add)
         tt(A("PB", 4, 5), A("PB", 4, 5), A("PB", 0, 1), OP.mult)
     ts(A("W8"), A("I16"), g16, OP.is_equal, A("PB", 4, 5), OP.mult)
-    ts(A("CF", 1, 2), part, 1 / 16, OP.mult, -1 / 16, OP.add); ts(A("CF", 2, 3), part, 65536.0, OP.mult)
-    ts(A("TH0", p1=2), A("KF", p1=2), 0.5, OP.add, A("CF", 1, 2, p1=2), OP.mult); ts(A("TH1", p1=2), A("GF", p1=2), A("CF", 2, 3, p1=2), OP.mult)
-    tt(A("KB", p1=2), A("TH0", p1=2), A("TH1", p1=2), OP.add)
-    ts(A("TH"), A("GF"), 65536.0, OP.mult, T0, OP.add); ms(A("TH0"), 0.0); ms(A("TH1"), 0.0)
+    ts(A("CF", 1, 2), part, 1 / 32, OP.mult, -1 / 32, OP.add); ts(A("CF", 2, 3), part, 65536.0, OP.mult)
+    ts(A("MB", p1=2), A("KF", p1=2), -8.0, OP.add, A("CF", 1, 2, p1=2), OP.mult); ts(A("TH", p1=2), A("GF", p1=2), A("CF", 2, 3, p1=2), OP.mult)
+    tt(A("KB", p1=2), A("MB", p1=2), A("TH", p1=2), OP.add)
+    act(A("TH"), A("GF"), AF.Copy, T0 + 0.5, 65536.0)
+    for s in (1, 2): act(A("TH%d" % s), A("ONE"), AF.Copy, 0.0, 0.0)
     for i in range(3): act(A("TH3", 8 * i, 8 * i + 8), A("TH", 0, 128, 16), AF.Copy)
-    act(A("RST"), A("KF"), AF.Sigmoid, A("CF", 3, 4), STEEP)
-    for b in range(4): ts(A("SELC", 512 * b, 512 * b + 512), A("IR", 512 * b, 512 * b + 512), part, OP.is_equal)
+    ts(A("RST"), A("KF"), 0.0, OP.is_gt); cp(A("PT"), A("CI", 0, 1))
+    for b in range(4): ts(A("SELC", 512 * b, 512 * b + 512), A("IR", 512 * b, 512 * b + 512), A("PT"), OP.is_equal)
     ts(A("B8"), A("I16"), g16, OP.is_equal); ts(A("B1"), A("I16"), part, OP.is_equal)
     ts(A("DB"), A("IO144"), A("CF", 12, 13), OP.is_equal)
     ts(A("WU"), A("I16"), g16, OP.is_equal, A("CF", 16, 17), OP.mult)
@@ -358,13 +360,13 @@ def rank_program(g, core, T, topo):
             together(lambda: [mm(key, A("ONE", 0, 128, p1=2), A("KB", p1=2), True, False)] +
                      [mm(A("KEY", ko + k, ko + 128, 16), A(nr, k, 2048, 16), A("W8"), False, k == 15) for k in range(16)])
             s1 = A("S1_%d" % s, 128 * i, 128 * i + 128); m = A("S1_%d" % s, 128 * i + 15, 128 * i + 128, 16); no = A("NO%d" % (n % 2))
-            go = A("GO%d_%d" % (r, s), *c); fl = A("FL%d_%d" % (r, s), *c) if s else None; th = "TH%d" % (n % 2) if s else "TH"
-            if s: cp(A(th, 0, 128, 16), fl)
-            scan(s1, A(th), key, OP.max)
+            go = A("GO%d_%d" % (r, s), *c); th = A("TH%d" % s, 128 * i, 128 * i + 128) if s else A("TH"); fl = th[:3] + (16,) + th[4:]
+            if s: act(fl, A("FL%d_%d" % (r, s), *c), AF.Copy, 0.5 - WHOLE)
+            scan(s1, th, key, OP.max)
             scan(A("MB", 0, 128, -1), A("RST"), s1[:3] + (-1,) + s1[4:], OP.mult); tt(no, key, A("MB"), OP.is_ge)
             if s == 2: tt(go, m, fl, OP.is_gt)
             if s < 2:
-                ts(A("F%d_%d" % (r, s), *c), m, 0.5, OP.add)
+                act(A("F%d_%d" % (r, s), *c), m, AF.Copy, WHOLE)
                 send(1, A("FL%d_%d" % (r, s + 1), *c), A("F%d_%d" % (r, s), *c), "aF%d_%d_%d" % (r, s + 1, i), [A("UL0")])
             sl = A("SEL%d" % (n % 2)) if s < 2 else A("SEL2", 128 * i, 128 * i + 128); lu = A("LU%d_%d" % (r, s), *c); vm = A("MI", 160 + c[0], 160 + c[1])
             mm(A("MI", 0, 128), no, A("ID"), True, True)
@@ -394,16 +396,19 @@ def rank_program(g, core, T, topo):
             ts(A(nj, c0, c1), A(an, c0, c1), M128, OP.add, M128, OP.subtract)
             if share:
                 tt(A("SB", c0, c1), A(an, c0, c1), A(nj, c0, c1), OP.subtract); ts(A(nj + "B", c0, c1), A("SB", c0, c1), -63.0, OP.add, STEEP, OP.mult)
+            if share < 4 and NARROW:
+                ts(A("PA", c0, c1), A(an, c0, c1), -1.0, OP.mult, 63.5, OP.add); tt(A(nj + "C", c0, c1), A("PA", c0, c1), A(nj, c0, c1), OP.add)
             for j in range(c0, c1):
                 o = A(out, 128 * j, 128 * j + 128)
                 if j % 4 < share: act(o, A("IO144", 0, 128), AF.Sigmoid, A(nj + "B", j, j + 1), STEEP)
+                elif NARROW: ts(o, A("IOH"), A(nj + "C", j, j + 1), OP.is_ge)
                 else: ts(o, A(io), A(nj, j, j + 1), OP.add, A(an, j, j + 1), OP.is_lt)
 
         def codes():
             together(lambda: [mm(A("MI", 256 + 8 * i, 264 + 8 * i), A(z0[0], 128 * i, 128 * i + 128), A("WU"), True, True) for i in range(3)] +
                      [mm(A("MI", 288, 312), A("DUB", 15 - b, 143 - b), A(z0[0], b, 384, 16), b == 0, b == 15) for b in range(16)])
             ts(A("UT"), A("MI", 256, 280), MAG, OP.add, MAG, OP.subtract); tt(A("U%d" % r), A("MI", 256, 280), A("UT"), OP.subtract)
-            tt(A("ID_"), A("MI", 288, 312), A("VL"), OP.add); ts(A("IC"), A("ID_"), 4095, OP.bitwise_and); cp(A("FA"), A("IC"))
+            tt(A("ID_"), A("MI", 288, 312), A("VL"), OP.add); ts(A("IC"), A("ID_"), 4095, OP.bitwise_and); ts(A("FA"), A("IC"), -2048.0, OP.add)
             send(1, A("UL%d" % r), A("U%d" % r), "aU%d" % r)
             gather("S", A("WG"), A("IW"), A("LW"))
             together(lambda: [mm(A("MI", 320 + 8 * i, 328 + 8 * i), A("WG", 128 * i, 128 * i + 128), A("B1"), True, True) for i in range(3)])
@@ -411,11 +416,11 @@ def rank_program(g, core, T, topo):
 
         def exdig(s):
             steps("YL%d" % s, "NIH", "ML%d" % r if s else "W0", "WL%d" % s, 0, 24, SHARE[s])
-            tt(A("EG"), A("F%d_%d" % (r, s)), A("S1_%d" % s, 15, 384, 16), OP.subtract)
-            if s == 0: ts(A("EH"), A("EG"), 16384.0, OP.mult, -512.0, OP.add); tt(A("XC0"), A("EH"), A("WL0"), OP.subtract)
+            act(A("EF"), A("F%d_%d" % (r, s)), AF.Copy, -WHOLE); tt(A("EG"), A("EF"), A("S1_%d" % s, 15, 384, 16), OP.subtract)
+            if s == 0: act(A("EH"), A("EG"), AF.Copy, 8192.0, 32768.0); tt(A("XC0"), A("EH"), A("WL0"), OP.subtract)
             else:
                 ts(A("EA"), A("ML%d" % r), -1.0, OP.mult, 63.5, OP.add); ts(A("EC"), A("EA"), 7, OP.arith_shift_right, 7, OP.bitwise_and)
-                ts(A("EH"), A("EG"), 128.0, OP.mult, -4.0, OP.add); tt(A("XC1"), A("EH"), A("EC"), OP.add)
+                act(A("EH"), A("EG"), AF.Copy, 64.0, 256.0); tt(A("XC1"), A("EH"), A("EC"), OP.add)
 
         def exadd(s, c0, c1):
             tt(A("UM%d" % s, c0, c1), A(("UL%d" if s else "U%d") % r, c0, c1), A("GL%d_%d" % (r, s + 1), c0, c1), OP.mult)
@@ -457,8 +462,8 @@ def rank_program(g, core, T, topo):
             ts(A("FCOL"), A("AJ"), -1 / 1024, OP.mult, 25 / 1024, OP.add)
 
         def boats(lu):
-            ts(A("BI"), lu, DOWN, OP.mult); ts(A("BB"), lu, 2048.0, OP.is_equal); tt(A("BC"), A("FA"), A("BI"), OP.subtract)
-            tt(A("BD"), A("BC"), A("BB"), OP.mult); tt(A("FA"), A("BD"), A("BI"), OP.add)
+            ts(A("BI"), lu, DOWN, OP.mult, -2048.0, OP.add); ts(A("BB"), lu, 2048.0, OP.is_equal)
+            tt(A("BD"), A("FA"), A("BB"), OP.mult); tt(A("FA"), A("BD"), A("BI"), OP.add)
 
         def own():
             z1, zn, y = A("ZO%d_0" % r), A("RD" if last else "Z%d_0" % (r + 1)), A("PEN", 0, 384); one = A("ONE", p1=1)
@@ -469,7 +474,7 @@ def rank_program(g, core, T, topo):
             if last: dma("oyz", T.yz[:, :], ap(zn), 3 << 15, "Y", [zn], [])
 
         def passed(s):
-            tt(A("GO%d_%d" % (r, s)), A("S1_%d" % s, 15, 384, 16), A("FL%d_1" % r if s else "TH3"), OP.is_gt)
+            tt(A("GO%d_%d" % (r, s)), A("S1_%d" % s, 15, 384, 16), A("TH1", 0, 384, 16) if s else A("TH3"), OP.is_gt)
 
         front(0); front(1); front(2)
         if r:
@@ -495,10 +500,10 @@ def rank_program(g, core, T, topo):
         pendig(2, 16, 24); penadd(2, 16, 24); exadd(1, 16, 24); penadd(1, 16, 24, True)
         aslist("SEL2", A("LU%d_2" % r)); send(-2, A("LL%d_2" % r), A("LU%d_2" % r), "aL%d_2" % r)
         boats(A("LL%d_2" % r))
-        if last: dma("oyv", T.yv[:, :], ap(A("FA")), 1 << 14, "Y", [A("FA")], [])
+        if last: act(A("FB"), A("FA"), AF.Copy, 2048.0); dma("oyv", T.yv[:, :], ap(A("FB")), 1 << 14, "Y", [A("FB")], [])
         else:
-            cp(A("VL"), A("FA")); ts(A("LWI"), A("VL"), 1023, OP.bitwise_and); cp(A("LW"), A("LWI"))
-            ts(A("FI"), A("ID"), A("FCOL"), OP.mult); ts(A("NFI"), A("ID"), A("FCOL"), OP.mult, -1.0, OP.mult)
+            ts(A("VL"), A("FA"), 2048.0, OP.add); ts(A("LWI"), A("VL"), 1023, OP.bitwise_and); cp(A("LW"), A("LWI"))
+            act(A("FI"), A("ID"), AF.Copy, 0.0, A("FCOL")); act(A("NFI"), A("NID"), AF.Copy, 0.0, A("FCOL"))
         tt(A("C16"), A("PEN", 0, 264), A("CL%d" % r), OP.add)
         together(lambda: [mm(A("PEN", 128 * h, 128 * h + 128), A("C16", 128 * h + d, 128 * h + d + 128), A(w), d == 8, d == 0, True)
                           for h in range(2) for d, w in ((8, "DM"), (0, "NDM"))])

@@ -1,17 +1,26 @@
+from concourse.bass import DstId, RemoteDMATransfer
 from concourse.mybir import dt, AluOpType as OP, ActivationFunctionType as AF, AxisListType
 
 RO, ST, NCH = 2, 3, 3
 BS = {"float32": 4, "int32": 4, "bfloat16": 2, "float16": 2, "uint16": 2}
 SCRATCH, ALIAS, POOL = {}, {}, {}
-REVERSE = True
-ZT_ON = "S"
-V_QUARTERS = {(0, 1), (0, 3), (1, 2)}
-N3 = 5
-JOIN, ROT, ZTB = (), 0, ("KEY", 128, 256)
-BYDMA, ALT, SFIX, SGV = (), False, 0.0, ()
-VFIX, NARROW = 0.0, True
-RELU_V = ((5, 7), (1, 3))
-SHARE = (0, 0, 0, 0, 0)
+V_QUARTERS = ({(0, 1), (0, 3)},) * 2
+S_PO = ((3, 6), (3, 6))
+S_ABS = ((), ())
+RELU_V = ((1, 3, 5, 7), (1, 3, 5))
+PARTS = (((0, 8), (8, 16), (16, 24)), ((0, 16), (16, 24)), ((0, 16), (16, 24)), ((0, 24),), ((0, 24),))
+STORES = (1, 1, 2, 2, 2)
+PO_SPLIT, HALVES, KEY_SPLIT, ZO_V = ((), ()), ((), ()), ((), ()), ((0, 1),) * 2
+ON_V = ("CW", "C")
+PARTS2, JOIN, NOJOIN = ((0, 24),), (1,), ()
+BY_SCAN, ZFIRST = (range(6), range(6)), 1
+S_ROWS = (((), range(4, 16)),) * 2
+SPREAD, IW_S = ("SGG", "GGY"), True
+ROOM, FUSE, NZT, CUT, TH_LAST, DIRECT = {}, False, 3, 384, 0, (1, 2)
+HOME = (((0, 16), (16, 24)), ((0, 24),))
+MARKS = ""
+V_STEPS, HT_APART, Z_LAST = (((), range(20, 24)),) * 2, True, True
+OWN_V, OF_V = False, ()
 
 
 def _b(names, cols, dtype, where="sbuf"):
@@ -25,49 +34,46 @@ def _s(names, cols, dtype):
         ALIAS[n] = ("pool_" + dtype, o, cols); POOL[dtype] = o + (cols + w - 1) // w * w
 
 
-_b("X", 4112, "bfloat16"); _b("OF", 4112, "float32"); _s("BM", 16, "float32"); _b("O OT OM", 1024, "int32"); _b("NB", 512, "int32"); _b("YN YH", 512, "float32")
-_b("XG0 XG1 XG2 NR0 NR1 IR", 2048, "bfloat16"); _b("SELC", 2048, "float16"); _b("WA", 2048, "bfloat16")
-_b("PO0 PO1 PO2 PO3", 128, "uint16"); _b("PI0 PI1", 128, "int32"); _b("PF0 PF1 PF2 PF3 SEL0 SEL1 ZT0 ZT1 IOH ID16 NID16", 128, "float16")
-_b("D0 D1 D2 KEY MI EX0 EX1 PEN", 512, "float32", "psum"); _b("CB0 CB1 CL0 CL1", 264, "float16"); _b("SG0", 24 * 34, "float16"); _b("NO0 NO1", 128, "bfloat16"); _b("MB KF GF TH", 128, "float32"); _b("TH1 TH2", 384, "float32"); _s("EF FB", 24, "float32"); _b("RST", 128, "bfloat16"); _s("TH3", 24, "float32")
-_b("S1_0 S1_1 S1_2 WG RY", 384, "float32"); _b("SG1 SG2", 24 * 34, "bfloat16")
-_b("YL0 YL1 YU0 YU1", 24 * 128, "float16"); _b("HOH1 HOH2", 24 * 128, "bfloat16")
-_b("SEL2", 384, "float16"); _b("EXR EXQ", 1024, "float16"); _b("DM DM4 NDM ONE16 BDH DIAG LM0 LM1", 128, "float16"); _b("R1536", 512, "float16"); _s("WL0B WL1B HP0B HP1B HP2B", 24, "float32")
-_s("WA0 WA1 WB0 WB1", 8, "int32"); _s("LS1_0 LS1_1", 24, "uint16")
-_b("IW", 1024, "float32"); _b("C16", 264, "float16"); _b("HT", 256, "bfloat16"); _b("ZR", 512, "float16")
-_s("VMB1 VMB2 LOB0 LOB1 LOB2 HP0 HP1 HP2 WL0 WL1 W0 FA BB BC BD EG EH FC0 FC1 UT CF", 24, "float32")
-_s("WL0C WL1C HP1C HP2C", 24, "bfloat16"); _s("XC0 XC1 UM0 UM1", 24, "float16")
-_s("VL ID_ IC LWI BI EA EB EC PA PB_ PC", 24, "int32"); _s("LW", 24, "uint16"); _s("PB I16 B1", 8, "float32")
+_b("X", 4112, "bfloat16"); _b("OT", 4112, "int32"); _b("OF", 4112, "float32"); _b("NB", 512, "int32"); _b("YN", 512, "float32")
+_b("O16 EXQ EXR", 1024, "float16"); _b("IW", 1024, "float32")
+_b("XG0 XG1 XG2 NR0 NR1", 2048, "bfloat16"); _b("AB0 AB1 SELC WA", 512, "float16"); _b("IR ONE", 512, "bfloat16")
+_b("PO0 PO1 PO2 PO3", 128, "uint16"); _b("PF0 PF1 PF2 PF3 SEL0 SEL1 ZT0 ZT1 ZT2 IOL IOS IOH ID16 TRI DM NDM D4 BDH", 128, "float16")
+_b("D0 D1 D2 KEY MI EX0 EX1 PEN", 512, "float32", "psum")
+_b("NO0 NO1 RST ID NID FI NFI N6 BD16 KL KV OFFD IH", 128, "bfloat16"); _b("MB2 KF GF TH0 LS", 128, "float32"); _b("S1 WG TH", 384, "float32"); _b("RY", 384, "float16")
+_b("LO0 LO1 LO2 LO3 HI0 HI1", 24 * 128, "float16"); _b("HI2", 3 * 264, "float16"); _b("SG1 SG2", 24 * 34, "float16")
+_b("SEL2", 384, "float16"); _b("HT", 256, "float16"); _b("BG C16 CB0 CB1 CL0 CL1", 264, "float16"); _b("G2 CG", 264, "bfloat16"); _b("KB RB RD", 384, "bfloat16")
+_b("DB", 144, "float16"); _b("DUB", 144, "bfloat16"); _b("IO", 144, "float32")
+_s("K1536 K0 K2048 KM4096 K512 KM", 128, "bfloat16"); _s("I128 J128", 33, "float32"); _s("HALF", 1, "float32")
+_s("VM1 VM2 W0 FA BB BI BD UT FB CF RR FR EH ES NJ0 NJ1 NJ2 NJ3", 24, "float32"); _s("BB2 BI2", 48, "float32")
+_s("XC0 XC1 VA0 VA1", 24, "float16"); _s("LD0 LD1 LD2 LD3", 24, "bfloat16")
+_s("VL LWI EA EC", 24, "int32"); _s("LW", 24, "uint16"); _s("B1", 8, "float32"); _s("H16 PW MK", 16, "float32")
 for _r in range(RO):
+    _s("LH%d" % _r, 48, "uint16")
     for _i in range(3):
         _b("Z%d_%d" % (_r, _i), 384, "bfloat16")
-        _s("GO%d_%d" % (_r, _i), 24, "float32"); _s("LU%d_%d" % (_r, _i), 24, "uint16")
         if _i < 2:
-            _s("F%d_%d" % (_r, _i), 24, "float32"); _b("ZO%d_%d" % (_r, _i), 384, "bfloat16")
+            _b("MB%d_%d" % (_r, _i), 384, "float32"); _b("ZO%d_%d" % (_r, _i), 384, "bfloat16")
         if _i > 0:
-            _s("GL%d_%d" % (_r, _i), 24, "float32"); _s("FL%d_%d" % (_r, _i), 24, "float32"); _s("LV%d_%d LL%d_%d" % (_r, _i, _r, _i), 24, "uint16")
-    _s("U%d UL%d VMB0_%d ML%d" % (_r, _r, _r, _r), 24, "float32")
-_b("RB RD ONE", 384, "bfloat16")
-_b("NIH IOH128", 128, "float16"); _s("I128", 33, "float32"); _s("SB", 24, "float32")
-_b("NIB ID HID NID FI NFI BD16 KB QROW GROW RP8", 128, "bfloat16"); _s("CI", 8, "int32")
-_s("W8 WU", 8, "bfloat16"); _s("B8", 8, "float16"); _b("DB", 144, "float16"); _b("DUB", 144, "bfloat16"); _b("IO144", 144, "float32")
-_s("AL", 96, "float32"); _s("AR FCOL", 1, "float32"); _s("AC PT", 1, "bfloat16"); _s("AI AJ", 1, "int32")
+            _b("TH%d_%d" % (_r, _i), 384, "float32"); _s("GO%d_%d GL%d_%d FL%d_%d F%d_%d" % (_r, _i, _r, _i, _r, _i, _r, _i - 1), 24, "float32"); _s("LV%d_%d LU%d_%d" % (_r, _i, _r, _i), 24, "uint16")
+    _s("VM0_%d ML%d" % (_r, _r), 24, "float32"); _s("U%d UL%d" % (_r, _r), 24, "float16"); _s("LL%d" % _r, 24, "uint16")
+_s("CI", 8, "int32"); _s("W8 WU", 8, "bfloat16"); _s("B8", 8, "float16")
+_s("AL", 96, "bfloat16"); _s("AR FCOL", 1, "float32"); _s("AC PT", 1, "bfloat16"); _s("AI AJ", 1, "int32")
 for _d in POOL:
     _b("pool_" + _d, POOL[_d], _d)
 
-SEMAPHORES = ["V", "S", "P", "G", "ls", "dnb", "dv", "dz", "dx0", "dx1", "dx2", "dx3", "dcp0", "dcp1", "oyx", "oyn", "oyv", "oyz"]
+SEMAPHORES = ["V", "S", "P", "G", "ls", "dnb", "dv", "dz", "dx", "dcp0", "dcp1", "oyx", "oyn", "oyv", "oyz"]
 for _r in range(RO):
     for _j in (1, 2):
         for _i in range(NCH):
-            SEMAPHORES += ["aF%d_%d_%d" % (_r, _j, _i), "aV%d_%d_%d" % (_r, _j, _i), "aZ%d_%d_%d" % (_r, _j, _i)]
+            SEMAPHORES += ["a%s%d_%d_%d" % (_k, _r, _j, _i) for _k in "FVZG"]
         SEMAPHORES += ["aL%d_%d" % (_r, _j)]
-    SEMAPHORES += ["aU%d" % _r, "aM%d" % _r, "aC%d" % _r, "aG%d_1" % _r, "aG%d_2a" % _r, "aG%d_2b" % _r]
+    SEMAPHORES += ["aU%d" % _r, "aC%d" % _r, "aL%d_3" % _r, "aL%d_4" % _r] + ["aM%d_%d" % (_r, _i) for _i in range(NCH)]
 
 MAG = 12582912.0
-M4096 = MAG * 4096
-UP, DOWN, EPS = 4097 / 4096, 4095 / 4096, 0.00015
-T0, WHOLE = 34816.0, 8388608.0
-M128, STEEP, NOBOAT = MAG * 128, 1048576.0, 63.5 - 2048 * DOWN
-CY, PCY, GCY, LAT, HOP, DMA0, DMAB = 0.83, 0.42, 1.56 * 0.83, 165.0, 2200.0, 1500.0, 330.0
+M128 = MAG * 128
+T0, NOBOAT, SUMK = 34816.0, 4096.0, 15 * 2048.0 - 2048.0
+TIE = (48.0, 31.0, 15.0)
+CY, PCY, GCY, HOP, DMA0, DMAB = 0.83, 0.42, 1.56 * 0.83, 2100.0, 1500.0, 330.0
 
 
 def A(name, c0=0, c1=None, step=1, p0=0, p1=128):
@@ -87,60 +93,153 @@ def meet(s, t, b):
     return s[0] < t[1] and t[0] < s[1] and s[2] // b * b < -(-t[3] // b) * b and t[2] // b * b < -(-s[3] // b) * b
 
 
-def schedule(ops):
+def schedule(ops, walk):
     n = len(ops); deps = [dict() for _ in ops]; acc = {}
-    for i, (q, c, d, reads, writes, _) in enumerate(ops):
-        dmai = q in "YG" and d > c + LAT
-        for lst, w in ((reads, False), (writes, True)):
+    for i, (q, c, d, reads, writes, _, sums, _) in enumerate(ops):
+        dmai = d > 0
+        for lst, w in ((reads, 0), (writes, 1), (sums, 2)):
             for a in lst:
                 s = span(a)
                 for (t, ow, j, dmaj) in acc.get(a[0], []):
-                    if j != i and (ow or w) and meet(s, t, 16 if ow and w and dmai != dmaj else 1):
-                        deps[i][j] = ops[j][1] if ops[j][0] == q == "P" and psum(a) and j not in deps[i] else ops[j][2]
+                    if j != i and (ow != w or w == 1) and meet(s, t, 16 if ow and w and dmai != dmaj else 1):
+                        deps[i][j] = deps[i].get(j, False) or not (ops[j][0] == q == "P" and psum(a))
         for a in writes:
             s = span(a); acc[a[0]] = [r for r in acc.get(a[0], []) if not (s[0] <= r[0][0] and r[0][1] <= s[1] and s[2] <= r[0][2] and r[0][3] <= s[3])]
-        for lst, w in ((reads, False), (writes, True)):
+        for lst, w in ((reads, 0), (writes, 1), (sums, 2)):
             for a in lst: acc.setdefault(a[0], []).append((span(a), w, i, dmai))
-    banks = [set(a[0] for a in o[3] + o[4] if psum(a)) for o in ops]
-    back = [dict() for _ in ops]
-    for i in range(n):
-        for j in deps[i]: back[j][i] = deps[i][j] - ops[j][1] + ops[i][1]
+    deps = [{j: f for j, f in d.items() if not (ops[j][2] == 0 and any(j in deps[k] and d[k] for k in d))} for d in deps]
+    banks = [sorted(set(a[0] for a in o[3] + o[4] + o[6] if psum(a))) for o in ops]; qs = [o[0] for o in ops]; cases = []
+    for slow, jump, lat, hop, _, call, link, *fix in CASES:
+        cs = [o[1] + (call + link * o[7]) * (o[0] == "G") if o[2] else slow * (o[1] + (jump - 1) * o[7]) + sum(fix) * (o[0] in "VS" and bool(b)) for o, b in zip(ops, banks)]
+        ds = [o[2] + (hop + link * o[7]) * (o[0] == "G") if o[2] else c + lat for o, c in zip(ops, cs)]
+        ways = []
+        for turned in (False, True):
+            before, after = [[] for _ in ops], [[] for _ in ops]
+            for i in range(n):
+                for j, full in deps[i].items():
+                    d = ds[j] if full else cs[j]
+                    if turned: before[j].append((i, d - cs[j] + cs[i])); after[i].append((j, d - cs[j] + cs[i]))
+                    else: before[i].append((j, d)); after[j].append((i, d))
+            ways.append((before, after))
+        cases.append((cs, ds, lat, ways[0], ways[1]))
 
-    def once(deps, rank, ahead):
-        succ = [[] for _ in ops]
+    def once(case, way, rank, ahead):
+        cs, ds, lat = case[:3]; before, after = case[way]
+        left = [len(d) for d in before]; at = [0.0] * n; ready = {q: [] for q in "VSPGY"}; free = {q: 0.0 for q in ready}; bank = {}; order = []; pick = {}
         for i in range(n):
-            for j in deps[i]: succ[j].append(i)
-        left = [len(d) for d in deps]; at = [0.0] * n; ready = {q: [] for q in "VSPGY"}; free = {q: 0.0 for q in ready}; bank = {}; order = []
-        for i in range(n):
-            if not left[i]: ready[ops[i][0]].append(i)
+            if not left[i]: ready[qs[i]].append(i)
         while len(order) < n:
-            best = None
             for q in ready:
-                l = [(max([free[q], at[i]] + [bank[b][1] for b in banks[i] if b in bank and bank[b][0] != q]), rank[i], i) for i in ready[q]]
-                if not l: continue
-                t0 = min(l)[0]; c = min((x for x in l if x[0] <= t0 + ahead), key=lambda x: x[1])
-                c = min((x for x in l if x[0] + ops[x[2]][1] <= c[0] + SLIP), key=lambda x: x[1], default=c)
-                if best is None or c < best: best = c
-            t, _, i = best; q = ops[i][0]
-            ready[q].remove(i); order.append(i); at[i] = t; free[q] = t + ops[i][1]
-            for b in banks[i]: bank[b] = (q, t + ops[i][1] + LAT)
-            for k in succ[i]:
-                at[k] = max(at[k], t + deps[k][i]); left[k] -= 1
-                if not left[k]: ready[ops[k][0]].append(k)
-        return max(at[i] + ops[i][2] for i in range(n)), order, [-at[i] - ops[i][1] for i in range(n)]
+                if q in pick or not ready[q]: continue
+                f = free[q]; l = []
+                for i in ready[q]:
+                    t = at[i] if at[i] > f else f
+                    for b in banks[i]:
+                        x = bank.get(b)
+                        if x and x[0] != q and x[1] > t: t = x[1]
+                    l.append((t, rank[i], i))
+                t0 = min(l)[0] + ahead; c = min((x for x in l if x[0] <= t0), key=lambda x: x[1])
+                t0 = c[0] + SLIP; pick[q] = min((x for x in l if x[0] + cs[x[2]] <= t0), key=lambda x: x[1], default=c)
+            t, _, i = min(pick.values()); q = qs[i]
+            ready[q].remove(i); order.append(i); at[i] = t; free[q] = t + cs[i]; del pick[q]
+            for b in banks[i]:
+                bank[b] = (q, t + cs[i] + lat)
+                for x in "VSP": pick.pop(x, None)
+            for k, d in after[i]:
+                if t + d > at[k]: at[k] = t + d
+                left[k] -= 1
+                if not left[k]: ready[qs[k]].append(k); pick.pop(qs[k], None)
+        return max(at[i] + ds[i] for i in range(n)), order, [-at[i] - cs[i] for i in range(n)]
 
-    best = once(deps, list(range(n)), 0.0)
+    def times(case, order, old=None, a=0):
+        cs, ds, lat, deps, _ = case; a = a // 64 if old else 0
+        at, why, (free, bank), kept = (old[1][:], old[2][:], old[4][a], old[4][:a]) if old else ([0.0] * n, [-1] * n, ({}, {}), [])
+        free, bank = dict(free), dict(bank)
+        for k in range(64 * a, n):
+            if not k & 63: kept.append((dict(free), dict(bank)))
+            i = order[k]; t = 0.0; w = -1; q = qs[i]
+            for j, d in deps[0][i]:
+                if at[j] + d > t: t = at[j] + d; w = j
+            j = free.get(q)
+            if j is not None and at[j] + cs[j] >= t: t = at[j] + cs[j]; w = j
+            for b in banks[i]:
+                j = bank.get(b)
+                if j is not None and qs[j] != q and at[j] + cs[j] + lat > t: t = at[j] + cs[j] + lat; w = j
+                bank[b] = i
+            at[i] = t; why[i] = w; free[q] = i
+        e = max(ends, key=lambda i: at[i] + ds[i])
+        return at[e] + ds[e], at, why, e, kept
+
+    ends = [i for i in range(n) if not cases[0][3][1][i]]
+
+    start = {p: once(cases[p], 3, list(range(n)), 0.0) for p in PLANS}; best = None; base = None; pool = []
     for turn in range(TURNS):
-        now = best; ahead = AHEAD[turn % len(AHEAD)]
+        p = PLANS[turn % len(PLANS)]; case = cases[p]; now = start[p]; k0 = turn // len(PLANS); ahead = AHEAD[k0 % len(AHEAD)]
         for k in range(PASSES):
-            rank = [x + (i * 7919 + turn * 104729) % 1009 * BLUR * (turn >= len(AHEAD) and k == 0) for i, x in enumerate(now[2])]
-            now = once(deps, once(back, rank, ahead)[2], ahead)
-            if now[0] < best[0]: best = now
+            rank = [x + (i * 7919 + turn * 104729) % 1009 * BLUR * (k0 >= len(AHEAD) // 2 and k == 0) for i, x in enumerate(now[2])]
+            first = FIRST[(turn // len(PLANS) + k // 2) % len(FIRST)]
+            rank = once(case, 4, [x + BACK * first * w for x, w in zip(rank, walk)], ahead)[2]
+            now = once(case, 3, [x - first * w for x, w in zip(rank, walk)], ahead)
+            if now[0] < start[p][0]: start[p] = now
+            t = [times(c, now[1])[0] for c in cases]; base = base or t
+            worth = sum(a / b * c[4] for a, b, c in zip(t, base, CASES))
+            if best is None or worth < best[0]: best = (worth, now[1], t)
+            pool.append((worth, now[1], p))
+    seed = 1
+    for turn in range(MIXES):
+        pool.sort(key=lambda x: x[0]); del pool[KEEP:]
+        seed = (seed * 1103515245 + 12345) % 2147483648; a = pool[(seed >> 8) % len(pool)]; b = pool[(seed >> 16) % len(pool)]
+        seed = (seed * 1103515245 + 12345) % 2147483648; cut = (seed >> 8) % n; p = (a, b)[seed >> 5 & 1][2]; case = cases[p]
+        head = set(a[1][:cut]); order = a[1][:cut] + [i for i in b[1] if i not in head]; kind = seed >> 6 & 7; ahead = AHEAD[(seed >> 20) % len(AHEAD)]
+        if kind >= SHAKE:
+            a = pool[(seed >> 10) % 3 % len(pool)]; rank = times(case, a[1])[1]; far = (200.0, 500.0, 1000.0)[(seed >> 13) % 3]
+            for k, i in enumerate(a[1][cut:cut + 120]): rank[i] += ((i * 7919 + seed) % 1009 / 1009 - 0.5 - walk[i]) * far
+            order = once(case, 3, rank, ahead)[1]
+        elif kind & 3:
+            rank = times(case, order)[1]
+            if kind & 1: rank = once(case, 4, [-x - c for x, c in zip(rank, case[0])], ahead)[2]
+            order = once(case, 3, rank, ahead)[1]
+        t = [times(c, order)[0] for c in cases[:2]]
+        if sum(t) > 1.012 * sum(best[2][:2]): continue
+        t += [times(c, order)[0] for c in cases[2:]]; worth = sum(a / b * c[4] for a, b, c in zip(t, base, CASES))
+        if worth < best[0]: best = (worth, order, t)
+        if all(abs(worth - x[0]) > 1e-5 for x in pool): pool.append((worth, order, p))
+    worth, order, t = best; ways = {}; now = [times(c, order) for c in cases]
+    for step in range(SWAPS):
+        seed = (seed * 1103515245 + 12345) % 2147483648; p = (seed >> 12) % len(cases)
+        if p not in ways:
+            why, i = now[p][2:4]; arcs = []
+            while why[i] >= 0:
+                if why[i] not in deps[i]: arcs.append((why[i], i))
+                i = why[i]
+            ways[p] = arcs; pos = {i: k for k, i in enumerate(order)}
+        seed = (seed * 1103515245 + 12345) % 2147483648; j, i = ways[p][(seed >> 8) % len(ways[p])]; a, b = pos[j], pos[i]
+        if seed >> 4 & 1:
+            a = max(0, a - (seed >> 5 & 1) * (seed >> 20 & 15)); mv = {i}
+            for k in reversed(order[a:b]):
+                if any(k in deps[x] for x in mv): mv.add(k)
+            if j in mv: continue
+            new = order[:a] + [k for k in order[a:b + 1] if k in mv] + [k for k in order[a:b + 1] if k not in mv] + order[b + 1:]
+        else:
+            b = min(n - 1, b + (seed >> 5 & 3) * (seed >> 20 & 15)); mv = {j}
+            for k in order[a + 1:b + 1]:
+                if any(x in mv for x in deps[k]): mv.add(k)
+            if i in mv: continue
+            new = order[:a] + [k for k in order[a:b + 1] if k not in mv] + [k for k in order[a:b + 1] if k in mv] + order[b + 1:]
+        tp = times(cases[p], new, now[p], a)
+        if tp[0] > now[p][0]: continue
+        t2 = [tp if k == p else times(c, new, now[k], a) for k, c in enumerate(cases)]; w2 = sum(x[0] / b * c[4] for x, b, c in zip(t2, base, CASES))
+        if w2 <= worth: worth, order, now, ways = w2, new, t2, {}
+    best = (worth, order, [x[0] for x in now])
+    SPAN[:] = [best[2], best[0], now[0][:4], ops]
     return best[1]
 
 
-TURNS, BLUR = 14, 0.3
-ORDER, PASSES, AHEAD, SLIP = [], 4, (0.0, 100.0, 200.0, 300.0, 150.0, 250.0), 30.0
+CASES = ((1.3, 1.0, 240.0, 450.0, 1.0, 0.0, 0.0), (1.25, 1.0, 240.0, 700.0, 1.0, 0.0, 0.0), (1.0, 1.0, 220.0, 0.0, 1.0, 0.0, 0.0), (1.25, 1.0, 240.0, 0.0, 1.5, 0.0, 0.0),
+         (1.4, 1.2, 240.0, 300.0, 0.7, 0.0, 0.0), (1.4, 0.8, 240.0, 300.0, 0.7, 0.0, 0.0))
+PLANS = (0, 1)
+TURNS, BLUR, FIRST, BACK, BIG, MIXES, KEEP, SHAKE, SWAPS = 12, 0.3, (0.0, 0.0, 1000.0), 0.0, 0.5, 500, 20, 5, 6000
+ORDER, SPAN, PASSES, AHEAD, SLIP = [], [], 4, (0.0, 150.0, 250.0, 350.0, 200.0, 300.0), 30.0
 
 
 def rank_program(g, core, T, topo):
@@ -148,7 +247,6 @@ def rank_program(g, core, T, topo):
     if rank is None:
         return
     N = len(T.cores)
-    nxt, prv = T.cores[(rank + 1) % N], T.cores[(rank - 1) % N]
     eng = {"V": g.vector, "S": g.scalar, "P": g.tensor, "G": g, "Y": g.sync}
     cnt, snap, acc, known = {}, {}, {}, {q: {} for q in eng}
     ops = []
@@ -201,15 +299,15 @@ def rank_program(g, core, T, topo):
 
     group = []
 
-    def run(q, cost, reads, writes, call):
-        if q == "V": cost += VFIX
-        if group: group[0].append((cost, reads, writes, call))
-        else: ops.append((q, cost, cost + LAT, reads, writes, lambda: issue(q, reads, writes, call)))
+    def run(q, cost, reads, writes, call, sums=(), jumps=0.0):
+        if group: group[0].append((cost, reads, writes, call, list(sums)))
+        else: ops.append((q, cost + jumps, 0.0, reads, writes, lambda: issue(q, reads, writes + list(sums), call), list(sums), jumps))
 
     def together(f):
         group.append([]); f(); l = group.pop()
         c = sum(x[0] for x in l)
-        ops.append(("P", c, c + LAT, [a for x in l for a in x[1]], [a for x in l for a in x[2]], lambda: [issue("P", x[1], x[2], x[3]) for x in l]))
+        ops.append(("P", c, 0.0, [a for x in l for a in x[1]], [a for x in l for a in x[2]], lambda: [issue("P", x[1], x[2] + x[4], x[3]) for x in l],
+                    [a for x in l for a in x[4]], 0.0))
 
     def dma(sem, out, in_, size, q="Y", reads=(), writes=(), after=0.0):
         def f():
@@ -218,7 +316,7 @@ def rank_program(g, core, T, topo):
             cnt[sem] = cnt.get(sem, 0) + 16
             snap[(sem, cnt[sem])] = dict(known[q])
             note(q, sem, cnt[sem], reads, writes)
-        ops.append((q, 50.0, DMA0 + (after + size) / DMAB, list(reads), list(writes), f))
+        ops.append((q, size / DMAB if q == "Y" else 50.0, DMA0 + (after + size) / DMAB, list(reads), list(writes), f, [], 0.0))
 
     def send(step, out, in_, sem, after=()):
         dst, src = T.cores[(rank + step) % N], T.cores[(rank - step) % N]
@@ -229,7 +327,20 @@ def rank_program(g, core, T, topo):
             rid, pid, _ = topo.addr(dst)
             g.remote_dma(ap(out), ap(in_), T.sem[sem], T.sem["ls"], pid, rid, topo.mask(core, dst))
             cnt["ls"] = cnt.get("ls", 0) + len(topo.engines(core, dst))
-        ops.append(("G", 150.0, HOP, [in_] + list(after), [out], f))
+        ops.append(("G", 150.0 + ROOM.get(sem, 0.0), HOP + ROOM.get(sem, 0.0) + 128 * (span(out)[3] - span(out)[2]) / DMAB, [in_] + list(after), [out], f, [], 128 * (span(out)[3] - span(out)[2]) / DMAB))
+
+    def sends(l):
+        for step, out, in_, sem, share in l: cnt[sem] = cnt.get(sem, 0) + len(topo.engines(T.cores[(rank - step) % N], core)) // share
+        for step, out, in_, sem, share in l: note("R", sem, cnt[sem], [], [out])
+
+        def f():
+            hazards("G", "ls", [x[2] for x in l], []); at = 0; tr = []
+            for step, out, in_, sem, share in l:
+                dst = T.cores[(rank + step) % N]; rid, pid, _ = topo.addr(dst); e = topo.engines(core, dst); k = len(e) // share
+                tr.append(RemoteDMATransfer(dst_ids=[DstId(rid=rid, pnc=pid)], dma_engine_mask=sum(1 << j for j in e[at:at + k]), remote_sem=T.sem[sem], src=ap(in_), dst=ap(out)))
+                at += k
+            g.remote_dma_fused(tr, local_sem=T.sem["ls"]); cnt["ls"] = cnt.get("ls", 0) + at
+        ops.append(("G", 150.0, HOP + 300.0 + 128 * (span(l[0][1])[3] - span(l[0][1])[2]) * 4 / DMAB, [x[2] for x in l], [x[1] for x in l], f, [], 0.0))
 
     def col(x):
         return (ap(x), [x]) if isinstance(x, tuple) else (x, [])
@@ -238,14 +349,17 @@ def rank_program(g, core, T, topo):
 
     def ts(out, in0, s1, op0, s2=None, op1=None, off=None):
         v1, r1 = col(s1); v2, r2 = col(s2); tail = (op0,) if op1 is None else (op0, op1)
-        if off: run("V", 50 + 16 * width(off) * GCY, [in0, off], [out], lambda: g.vector.tensor_scalar(ap(out), ap(in0).indirect(ap(off)), v1, v2, *tail))
+        if off: run("V", 50, [in0, off], [out], lambda: g.vector.tensor_scalar(ap(out), ap(in0).indirect(ap(off)), v1, v2, *tail), (), 16 * width(off) * GCY)
         else: run("V", vc(width(out), out, in0, *(r1 + r2)), [in0] + r1 + r2, [out], lambda: g.vector.tensor_scalar(ap(out), ap(in0), v1, v2, *tail))
 
     def tt(out, a, b, op):
         run("V", CY * max(64, width(out) * (1 if psum(a) or psum(b) else 2)), [a, b], [out], lambda: g.vector.tensor_tensor(ap(out), ap(a), ap(b), op))
 
-    def scan(out, a, b, op):
-        run("V", vc(width(out), out, a, b), [a, b], [out], lambda: g.vector.tensor_tensor_scan(ap(out), ap(a), ap(b), 0.0, op, OP.max))
+    def scan(out, a, b, first, op):
+        run("V", vc(width(out), out, a, b), [a, b], [out], lambda: g.vector.tensor_tensor_scan(ap(out), ap(a), ap(b), first, op, OP.max))
+
+    def reduce(out, a):
+        run("V", CY * max(64, width(a)), [a], [out], lambda: g.vector.tensor_reduce(ap(out), ap(a), AxisListType.X, OP.add))
 
     def cp(out, a):
         run("V", vc(width(out), out, a), [a], [out], lambda: g.vector.tensor_copy(ap(out), ap(a)))
@@ -253,285 +367,350 @@ def rank_program(g, core, T, topo):
     def ms(out, c):
         run("V", vc(width(out), out), [], [out], lambda: g.vector.memset(ap(out), c))
 
+    def pc(l, r): return PCY * max(min(64, width(l)), width(r)) * (4 if SCRATCH[l[0]][2] == "float32" else 1)
+
     def mm(out, l, r, start, stop, whole=False):
-        c = PCY * max(min(64, width(l)), width(r)) * (4 if SCRATCH[l[0]][2] == "float32" else 1)
-        run("P", c, [l, r], [A(out[0]) if whole else out], lambda: g.tensor.matmul(ap(out), ap(l), ap(r), start, stop))
+        run("P", pc(l, r), [l, r], [A(out[0]) if whole else out], lambda: g.tensor.matmul(ap(out), ap(l), ap(r), start, stop))
+
+    open_ = {}
+
+    def begin(out, c):
+        mm(out, A(c, p1=1), A("ONE", 0, width(out), p1=1), True, False, True); open_[out[0]] = [0]
+
+    def add(out, l, r, part=None):
+        left = open_[out[0]]; left[0] += 1
+
+        def f():
+            left[0] -= 1
+            return g.tensor.matmul(ap(out), ap(l), ap(r), False, left[0] == 0)
+        run("P", pc(l, r), [l, r], [], f, [part or A(out[0])])
 
     def act(out, a, f, bias=0.0, scale=1.0):
         v, r = col(bias); v2, r2 = col(scale)
-        run("S", SFIX + CY * max(64, width(out)), [a] + r + r2, [out], lambda: g.scalar.activation(ap(out), ap(a), f, bias=v, scale=v2))
+        run("S", CY * max(64, width(out)), [a] + r + r2, [out], lambda: g.scalar.activation(ap(out), ap(a), f, bias=v, scale=v2))
 
-    def gather(q, out, win, off):
-        if q == "V": run("V", 50 + 16 * width(off) * GCY, [win, off], [out], lambda: g.vector.tensor_copy(ap(out), ap(win).indirect(ap(off))))
-        else: run("S", 65 + 16 * width(off) * GCY, [win, off], [out], lambda: g.scalar.activation(ap(out), ap(win).indirect(ap(off)), AF.Copy))
+    def gather(q, out, win, off, bias=0.0, f=AF.Copy):
+        if q == "V": ts(out, win, 0.0, OP.max, off=off)
+        else: run("S", 65, [win, off], [out], lambda: g.scalar.activation(ap(out), ap(win).indirect(ap(off)), f, bias=bias), (), 16 * width(off) * GCY)
 
     def iota(out, pat, base, cm, flag=True):
         c = 130 + 2 * CY * width(out)
         if flag: run("G", c, [], [out], lambda: g.iota(ap(out), pat, base, cm, allow_small_or_imprecise_dtypes=True))
         else: run("G", c, [], [out], lambda: g.iota(ap(out), pat, base, cm))
 
-    def xcol(b): return b + b // 2048
+    def spread(o, r):
+        for j in (1, 2, 3):
+            src, d = A(o, 0, 1024), A(o, 1024 * j, 1024 * j + 1024)
+            q = SPREAD[r][j - 1]
+            if q == "Y": dma("dcp%d" % r, ap(d), ap(src), 1 << 19, "Y", [src], [d])
+            for h in (0, 512) if q != "Y" else ():
+                s, e = A(o, h, h + 512), A(o, 1024 * j + h, 1024 * j + h + 512)
+                if q == "S": act(e, s, AF.Copy)
+                elif q == "V": cp(e, s)
+                else: keep(e, s)
 
-    ms(A("X", 2048, 2049), 512.0); ms(A("X", 4097, 4112), 512.0); ms(A("OF", 2048, 2049), 0.0); ms(A("OF", 4097, 4112), 0.0)
+    def keep(out, a):
+        run("G", 170 + 2 * CY * width(out), [a], [out], lambda: g.affine_select(ap(out), ap(a), [[0, width(out)]], OP.is_ge, 0.0, 0, 0))
+
+    ms(A("X", 4096, 4112), 512.0); ms(A("OT", 4096, 4112), 0); ms(A("OF", 4096, 4112), 0.0)
     dma("dv", ap(A("VL")), T.v[:, :], 1 << 14, "S", [], [A("VL")])
     dma("dnb", ap(A("NB")), T.nb[:, :], 1 << 18, "Y", [], [A("NB")])
-    for i in range(4):
-        a = A("X", xcol(1024 * i), xcol(1024 * i) + 1024)
-        dma("dx%d" % i, ap(a), T.tracks[:, 1024 * i:1024 * i + 1024], 1 << 18, "Y", [], [a], (i + 1) << 18)
-    dma("dz", ap(A("Z0_0")), T.z[:, :], 3 << 15, "S", [], [A("Z0_0")], 1 << 18)
-    iota(A("CI", 0, 1), [[1, 1]], 0, 1, False); iota(A("IO144"), [[1, 144]], 0, 0); iota(A("I16"), [[16, 8]], 0, 0)
-    iota(A("KF"), [[0, 8], [1, 16]], 0, 0); iota(A("GF"), [[1, 8], [0, 16]], 0, 0)
-    for b in range(4): iota(A("IR", 512 * b, 512 * b + 512), [[1, 32], [0, 16]], 32 * b, 0)
-    for b in range(2): iota(A("IW", 512 * b, 512 * b + 512), [[1, 512]], 512 * b, 0)
-    io, part, p16, g16 = A("IO144", 0, 128), A("CF", 0, 1), A("CF", 4, 5), A("CF", 8, 9)
-    ms(A("ONE"), 1.0); ms(A("QROW", p1=1), -0.25); ms(A("GROW", p1=1), 512.0); ms(A("PB", 4, 5), 32768.0)
+    dma("dx", ap(A("X", 0, 4096)), T.tracks[:, :], 1 << 20, "Y", [], [A("X", 0, 4096)])
+    if Z_LAST: dma("dz", ap(A("Z0_0")), T.z[:, :], 3 << 15, "Y", [], [A("Z0_0")])
+    else: dma("dz", ap(A("Z0_0")), T.z[:, :], 3 << 15, "S", [], [A("Z0_0")], 1 << 18)
+    iota(A("CI", 0, 1), [[1, 1]], 0, 1, False); iota(A("IO"), [[1, 144]], 0, 0)
+    iota(A("KF"), [[0, 8], [1, 16]], 0, 0); iota(A("GF"), [[1, 8], [0, 16]], 0, 0); iota(A("IR"), [[1, 32], [0, 16]], 0, 0)
+    iota(A("G2"), [[1, 8], [0, 33]], 0, 0); iota(A("CG", p1=1), [[0, 8], [1, 33]], int(SUMK) // 128, 0)
+    if IW_S:
+        iota(A("IW", 0, 256), [[1, 256]], 0, 0)
+        for b in (1, 2, 3): act(A("IW", 256 * b, 256 * b + 256), A("IW", 0, 256), AF.Copy, 256.0 * b)
+    else:
+        for b in range(2): iota(A("IW", 512 * b, 512 * b + 512), [[1, 512]], 512 * b, 0)
+    io, part, p16, pg, at15, odd, two15 = (A("IO", 0, 128),) + tuple(A("CF", j, j + 1) for j in (0, 4, 8, 12, 16, 20))
+    ms(A("ONE", p1=33), 1.0)
+    if DIRECT: ms(A("KV", p1=32), 0.0); ms(A("KV", p1=1), -SUMK); ms(A("KV", p0=32, p1=33), -63.5)
+    for nm, c in (("K1536", 1536.0), ("K0", 0.0), ("K2048", 2048.0), ("KM4096", -4096.0), ("K512", 512.0), ("KM", -128.0)): ms(A(nm, p1=1), c)
+    ms(A("KL", p1=32), 0.0); ms(A("KL", p1=1), 65536.0); ms(A("KL", p0=32, p1=33), 1 / 64)
+    ms(A("HALF"), 0.5)
+    if MARKS: ms(A("TH"), -1048576.0)
+    for s in range(3):
+        act(A("KB", 128 * s, 128 * s + 128, p1=32), A("GF", p1=32), AF.Copy, -4.0); act(A("KB", 128 * s, 128 * s + 128, p0=32, p1=33), A("KF", p0=32, p1=33), AF.Copy, TIE[s], -1.0)
     cp(part, A("CI", 0, 1))
-    ts(A("CI", 4, 5), A("CI", 0, 1), 15, OP.bitwise_and); cp(p16, A("CI", 4, 5)); tt(g16, part, p16, OP.subtract)
+    for j, (c, s, op) in enumerate(((p16, 15, OP.bitwise_and), (pg, 4, OP.arith_shift_right), (A("PT"), 31, OP.bitwise_and))):
+        ts(A("CI", j + 1, j + 2), A("CI", 0, 1), s, op); cp(c, A("CI", j + 1, j + 2))
     ts(A("ID"), io, part, OP.is_equal)
-    act(A("FI"), A("ID"), AF.Copy, 0.0, 25 / 1024); act(A("NFI"), A("ID"), AF.Copy, 0.0, -25 / 1024)
-    ts(A("CF", 12, 13), g16, 15.0, OP.add); ts(A("CF", 16, 17), p16, 2.0, OP.mult, 1.0, OP.add)
-    for b in range(4):
-        ts(A("CI", 1, 2), A("CI", 4, 5), b, OP.arith_shift_right, 1, OP.bitwise_and)
-        ts(A("PB", 0, 1), A("CI", 1, 2), 2.0 ** -(1 << b) - 1.0, OP.mult, 1.0, OP.add)
-        tt(A("PB", 4, 5), A("PB", 4, 5), A("PB", 0, 1), OP.mult)
-    ts(A("W8"), A("I16"), g16, OP.is_equal, A("PB", 4, 5), OP.mult)
-    ts(A("CF", 1, 2), part, 1 / 32, OP.mult, -1 / 32, OP.add); ts(A("CF", 2, 3), part, 65536.0, OP.mult)
-    ts(A("MB", p1=2), A("KF", p1=2), -8.0, OP.add, A("CF", 1, 2, p1=2), OP.mult); ts(A("TH", p1=2), A("GF", p1=2), A("CF", 2, 3, p1=2), OP.mult)
-    tt(A("KB", p1=2), A("MB", p1=2), A("TH", p1=2), OP.add)
-    act(A("TH"), A("GF"), AF.Copy, T0 + 0.5, 65536.0)
-    for s in (1, 2): act(A("TH%d" % s), A("ONE"), AF.Copy, 0.0, 0.0)
-    for i in range(3): act(A("TH3", 8 * i, 8 * i + 8), A("TH", 0, 128, 16), AF.Copy)
-    ts(A("RST"), A("KF"), 0.0, OP.is_gt); cp(A("PT"), A("CI", 0, 1))
-    for b in range(4): ts(A("SELC", 512 * b, 512 * b + 512), A("IR", 512 * b, 512 * b + 512), A("PT"), OP.is_equal)
-    ts(A("B8"), A("I16"), g16, OP.is_equal); ts(A("B1"), A("I16"), part, OP.is_equal)
-    ts(A("DB"), A("IO144"), A("CF", 12, 13), OP.is_equal)
-    ts(A("WU"), A("I16"), g16, OP.is_equal, A("CF", 16, 17), OP.mult)
-    ts(A("DUB"), A("IO144"), A("CF", 12, 13), OP.is_equal, A("CF", 16, 17), OP.mult)
-    act(A("HID"), A("ID"), AF.Copy, 0.0, 0.5); act(A("NID"), A("ID"), AF.Copy, 0.0, -1.0); act(A("IOH"), io, AF.Copy)
-    act(A("NIB"), io, AF.Copy, 63.0, -1.0); act(A("NIH"), io, AF.Copy, 63.0, -1.0); act(A("IOH128"), io, AF.Copy, 0.0, 128.0); act(A("I128"), A("IO144", 0, 33), AF.Copy, -64.0, 128.0)
-    ts(A("CF", 22, 23), part, 1.0, OP.add); ts(A("DM"), io, A("CF", 22, 23), OP.is_equal); tt(A("DM"), A("ID"), A("DM"), OP.subtract)
-    act(A("DM4"), A("DM"), AF.Copy, 0.0, 4096.0); act(A("NDM"), A("DM"), AF.Copy, 0.0, -1.0); act(A("WU"), A("WU"), AF.Copy, 0.0, 1 / 4096)
-    for nm, c in (("R1536", 1536.0), ("ONE16", 1.0), ("ZR", 0.0)): act(A(nm, p1=1), A("IR", 0, width(A(nm)), p1=1), AF.Copy, c, 0.0)
-    ts(A("BD16"), A("GF"), 16.0, OP.mult, g16, OP.is_equal)
-    if ALT: act(A("BDH"), A("BD16"), AF.Copy); ts(A("DIAG"), A("KF"), p16, OP.is_equal)
-    ts(A("CI", 2, 3), A("CI", 0, 1), 7, OP.bitwise_and); cp(A("CF", 20, 21), A("CI", 2, 3))
-    ts(A("CI", 3, 4), A("CI", 0, 1), 3, OP.arith_shift_right); cp(A("CF", 21, 22), A("CI", 3, 4))
-    ts(A("RP8"), A("GF"), A("CF", 20, 21), OP.is_equal, -45.0, OP.mult); ts(A("BM"), A("IO144", 0, 16), A("CF", 21, 22), OP.is_equal)
-    for a in range(16):
-        act(A("WA", 128 * a, 128 * a + 128), A("RP8"), AF.Copy, 0.0, A("BM", a, a + 1))
+    for nm, c in (("FI", 25 / 1024), ("NFI", -25 / 1024), ("NID", -1.0), ("N6", -6144.0), ("ID16", 1.0), ("D4", 4096.0)): act(A(nm), A("ID"), AF.Copy, 0.0, c)
+    ts(at15, pg, 16.0, OP.mult, 15.0, OP.add); ts(odd, p16, 2.0, OP.mult, 1.0, OP.add)
+    ms(A("H16"), 0.5); scan(A("PW"), A("H16"), A("H16"), 65536.0, OP.mult)
+    ts(A("MK"), A("IO", 0, 16), p16, OP.is_equal); tt(A("MK"), A("MK"), A("PW"), OP.mult); reduce(two15, A("MK"))
+    ts(A("W8"), A("IO", 0, 8), pg, OP.is_equal, two15, OP.mult)
+    act(A("TH0"), A("GF"), AF.Copy, T0 + 63 / 64 - 4 * 65536.0, 65536.0)
+    ts(A("RST"), A("KF"), 0.0, OP.is_equal, -1048576.0, OP.mult)
+    ts(A("SELC"), A("IR"), A("PT"), OP.is_equal)
+    ts(A("B8"), A("IO", 0, 8), pg, OP.is_equal); ts(A("B1"), A("IO", 0, 128, 16), part, OP.is_equal); ts(A("BG"), A("G2"), pg, OP.is_equal)
+    ts(A("DB"), A("IO", 0, 144), at15, OP.is_equal); ts(A("DUB"), A("IO", 0, 144), at15, OP.is_equal, odd, OP.mult)
+    ts(A("WU"), A("IO", 0, 8), pg, OP.is_equal, odd, OP.mult); act(A("WU"), A("WU"), AF.Copy, 0.0, 1 / 4096)
+    act(A("IOL"), io, AF.Copy, 63.5, -1.0); act(A("IOS"), io, AF.Copy, -63.0); ts(A("TRI"), io, part, OP.is_ge, 0.5, OP.subtract)
+    ts(A("CI", 4, 5), A("CI", 0, 1), 1.0, OP.add); ts(A("CI", 5, 6), A("CI", 4, 5), 127, OP.bitwise_and); cp(A("CF", 1, 2), A("CI", 5, 6))
+    ts(A("CF", 2, 3), part, 126.5, OP.is_lt, -0.5, OP.add); ts(A("NDM"), io, A("CF", 1, 2), OP.is_equal, A("CF", 2, 3), OP.mult)
+    act(A("NDM"), A("NDM"), AF.Copy, 0.0, 2.0); tt(A("DM"), A("ID16"), A("NDM"), OP.subtract); act(A("NDM"), A("DM"), AF.Copy, 0.0, -1.0)
+    iota(A("IH"), [[4, 2], [8, 16], [1, 4]], 0, 0); act(A("IOH"), A("IH"), AF.Copy, 0.0, 1 / 256)
+    act(A("I128"), A("IO", 0, 33), AF.Copy, 64.0, -128.0); act(A("J128"), A("IO", 0, 33), AF.Copy, 0.0, 128.0)
+    act(A("WA"), A("SELC"), AF.Copy, 0.0, -45.0)
+    ts(A("BD16"), A("GF"), pg, OP.is_equal)
+    if any(BY_SCAN): act(A("BDH"), A("BD16"), AF.Copy); ts(A("OFFD"), A("KF"), p16, OP.not_equal, -65536.0, OP.mult)
     ts(A("LWI"), A("VL"), 1023, OP.bitwise_and); cp(A("LW"), A("LWI"))
     ts(A("OT", 0, 512), A("NB"), 4095, OP.bitwise_and); ts(A("OT", 512, 1024), A("NB"), 12, OP.arith_shift_right)
+    for h in (0, 512): act(A("O16", h, h + 512), A("OT", h, h + 512), AF.Copy, -0.5, 1 / 4096)
+    spread("OT", 0)
 
-    def columns(o):
-        for h in (0, 512):
-            ts(A("OF", h, h + 512), A(o, h, h + 512), UP, OP.mult, EPS, OP.add)
-            for a in (1024, 2049, 3073):
-                src, d = A("OF", h, h + 512), A("OF", a + h, a + h + 512)
-                if o == "OM" and a in BYDMA: dma("dcp%d" % (h // 512), ap(d), ap(src), 1 << 18, "Y", [src], [d], (BYDMA.index(a) + h // 512 * len(BYDMA)) << 18)
-                else: act(d, src, AF.Copy)
-    columns("OT")
+    turn, walk = [0], set()
 
     def round_(r):
         last = r == RO - 1
         z0 = A("Z%d_0" % r)
+        def lu_(s, *c): return A("LU%d_%d" % (r, s), *c) if s else A("LH%d" % r, *(c or (0, 24)))
+        def vm_(s, *c): return A("VM%d" % s if s else "VM0_%d" % r, *c)
 
         def front(n):
             s, i = divmod(n, 3)
-            po = A("PO%d" % (n % 4)); l = A("LV%d_%d" % (r, s), 8 * i, 8 * i + 8) if s else A("LW", 8 * i, 8 * i + 8); w = A("O") if r and not s else A("OF", 0, 4112 if s else 1024)
-            if r == 0 or s: gather("V", po, w, l)
+            po, pf = A("PO%d" % (n % 4)), A("PF%d" % (n % 4)); l = A("LV%d_%d" % (r, s) if s else "LW", 8 * i, 8 * i + 8); w = A("OF" if r else "OT", 0, 4112 if s else 1024)
+            if n in S_PO[r]: gather("S", pf, w, l, 0.0 if r else -2048.0); ts(po, pf, 2048.0, OP.add)
             else:
-                pi = A("PI%d" % (n % 2))
-                ts(pi, w, 4095, OP.bitwise_and, off=l); ts(po, pi, UP, OP.mult, EPS, OP.add)
-            ts(A("PF%d" % (n % 4)), po, -2048.0, OP.add)
-            b = 0
-            while b < 4:
-                q = "V" if (n, b) in V_QUARTERS else "S"; e = b + 1
-                if q == "S" and b in JOIN and (n, e) not in V_QUARTERS: e += 1
-                gather(q, A("XG%d" % (n % 3), 512 * b, 512 * e), A("X"), A(po[0], 32 * b, 32 * e)); b = e
+                for a, b in ((0, 2), (2, 8)) if n in PO_SPLIT[r] else ((0, 8),):
+                    ts(A(po[0], 16 * a, 16 * b), w, 2048.0 if r else 0.0, OP.add, off=(l[0], l[1] + a, l[1] + b) + l[3:])
+                ts(pf, po, -2048.0, OP.add)
+            start = None
+            for b, c0, c1 in pieces(n):
+                start = c0 if start is None else start; q = "V" if (n, b) in V_QUARTERS[r] else "S"
+                if q == "S" and b in JOIN and n not in NOJOIN and (n, b + 1) not in V_QUARTERS[r]: continue
+                gather(q, A("XG%d" % (n % 3), start, c1), A("X"), A(po[0], start // 16, c1 // 16), f=AF.Relu); start = None
+
+        def pieces(n): return [(b, 512 * b + c, 512 * b + c + w) for b in range(4) for c, w in (((0, CUT), (CUT, 512 - CUT)) if (n, b) in HALVES[r] else ((0, 512),))]
 
         def hear(n):
-            s, i = divmod(n, 3); c = (8 * i, 8 * i + 8); zt = A("ZT%d" % (n % 2)); nr = "NR%d" % (n % 2); ko = ROT * (n % 2); key = A("KEY", ko, ko + 128)
-            mm(A(*ZTB), A("Z%d_%d" % (r, s), 128 * i, 128 * i + 128), A("NFI"), True, True)
-            act(zt, A(*ZTB), AF.Copy)
-            for b in range(4):
-                d = A("D%d" % ((4 * n + b) % 3))
-                together(lambda: (mm(d, A("FI"), A("XG%d" % (n % 3), 512 * b, 512 * b + 512), True, False), mm(d, zt, A("SELC", 512 * b, 512 * b + 512), False, True)))
-                ts(A(nr, 512 * b, 512 * b + 512), d, MAG, OP.add, MAG, OP.is_equal)
-            together(lambda: [mm(key, A("ONE", 0, 128, p1=2), A("KB", p1=2), True, False)] +
-                     [mm(A("KEY", ko + k, ko + 128, 16), A(nr, k, 2048, 16), A("W8"), False, k == 15) for k in range(16)])
-            s1 = A("S1_%d" % s, 128 * i, 128 * i + 128); m = A("S1_%d" % s, 128 * i + 15, 128 * i + 128, 16); no = A("NO%d" % (n % 2))
-            go = A("GO%d_%d" % (r, s), *c); th = A("TH%d" % s, 128 * i, 128 * i + 128) if s else A("TH"); fl = th[:3] + (16,) + th[4:]
-            if s: act(fl, A("FL%d_%d" % (r, s), *c), AF.Copy, 0.5 - WHOLE)
-            scan(s1, th, key, OP.max)
-            scan(A("MB", 0, 128, -1), A("RST"), s1[:3] + (-1,) + s1[4:], OP.mult); tt(no, key, A("MB"), OP.is_ge)
-            if s == 2: tt(go, m, fl, OP.is_gt)
+            s, i = divmod(n, 3); c = (8 * i, 8 * i + 8); h = (128 * i, 128 * i + 128); zt = "ZT%d" % (n % NZT); nr = "NR%d" % (n % 2); key = A("KEY", 0, 128)
+            mm(A("KEY", 128, 256), A("Z%d_%d" % (r, s), *h), A("NFI"), True, True)
+            act(A(zt), A("KEY", 128, 256), AF.Copy)
+            for b, c0, c1 in pieces(n):
+                turn[0] += 1; d = A("D%d" % (turn[0] % 3), 0, c1 - c0); p = dict(p0=32 * b, p1=32 * b + 32); o = A(nr, c0, c1); ab = A("AB%d" % (turn[0] % 2), 0, c1 - c0)
+                zx = [(A(zt, **p), A("SELC", c0 - 512 * b, c1 - 512 * b, **p)), (A("FI"), A("XG%d" % (n % 3), c0, c1))]
+                if ZFIRST == 2: together(lambda: (mm(d, *zx[1], True, False), mm(d, *zx[0], False, True)))
+                else: mm(d, *zx[1 - ZFIRST], True, False); mm(d, *zx[ZFIRST], False, True)
+                if (n, b) in S_ABS[r]: act(ab, d, AF.Abs); ts(o, ab, 0.5, OP.is_lt)
+                else: ts(o, d, MAG, OP.add, MAG, OP.is_equal)
+            for p0, p1 in ((0, 96), (96, 128)) if n in KEY_SPLIT[r] else ((0, 128),):
+                together(lambda: [mm(A("KEY", 0, 128, p0=p0, p1=p1), A("KL", p0, p1, p1=33), A("KB", 128 * s, 128 * s + 128, p1=33), True, False)] +
+                         [mm(A("KEY", k, 128, 16, p0, p1), A(nr, 16 * p0 + k, 16 * p1, 16), A("W8"), False, k == 15) for k in range(16)])
+            s1 = A("S1", *h); mb = A("MB%d_%d" % (r, s), *h) if s < 2 else A("MB2"); th = A("TH0") if MARKS or not s else A("TH%d_%d" % (r, s), *h); no = A("NO%d" % (n % 2))
+            if s and MARKS:
+                th = A("TH", *h); move(MARKS[1], A("TH", h[0], h[1], 16), A("FL%d_%d" % (r, s), *c))
+            scan(s1, th, key, -1048576.0, OP.max)
+            if s < 2 and MARKS:
+                f = A("F%d_%d" % (r, s), *c); move(MARKS[0], f, A("S1", h[0] + 15, h[1], 16)); out = (A("FL%d_%d" % (r, s + 1), *c), f, "aF%d_%d_%d" % (r, s + 1, i))
+                if s and c in PARTS[0]: bits(1, *c); sends([(1,) + out + (2,), (-1, A("GL%d_1" % r, *c), A("GO%d_1" % r, *c), "aG%d_1_%d" % (r, i), 2)])
+                else: send(1, *out)
+            scan(mb[:3] + (-1,) + mb[4:], A("RST"), s1[:3] + (-1,) + s1[4:], 0.0, OP.add); tt(no, key, mb, OP.is_ge)
+            if s < 2 and not FUSE and not TH_LAST and not MARKS: send(1, A("TH%d_%d" % (r, s + 1), *h), mb, "aF%d_%d_%d" % (r, s + 1, i))
+            sl = A("SEL%d" % (n % 2)) if s < 2 else A("SEL2", *h)
+            together(lambda: (mm(A("MI", 0, 128), A("K2048", p1=1), A("ONE", 0, 128, p1=1), True, False), mm(A("MI", 0, 128), no, A("N6"), False, True)))
+            tt(sl, A("MI", 0, 128), A("PF%d" % (n % 4)), OP.max)
+            vm = A("MI", 160 + c[0], 160 + c[1])
+            if s in DIRECT: together(lambda: (mm(vm, A("KV", p1=33), A("ONE", 0, 8, p1=33), True, False), mm(vm, sl, A("B8"), False, True)))
+            else: mm(vm, sl, A("B8"), True, True)
             if s < 2:
-                act(A("F%d_%d" % (r, s), *c), m, AF.Copy, WHOLE)
-                send(1, A("FL%d_%d" % (r, s + 1), *c), A("F%d_%d" % (r, s), *c), "aF%d_%d_%d" % (r, s + 1, i), [A("UL0")])
-            sl = A("SEL%d" % (n % 2)) if s < 2 else A("SEL2", 128 * i, 128 * i + 128); lu = A("LU%d_%d" % (r, s), *c); vm = A("MI", 160 + c[0], 160 + c[1])
-            mm(A("MI", 0, 128), no, A("ID"), True, True)
-            tt(sl, A("MI", 0, 128), A("PF%d" % (n % 4)), OP.mult)
-            if s == 2 or not ALT:
-                mm(vm, sl, A("B8"), True, True)
-                if s < 2: aslist(sl[0], lu); act(A(vmb(s), *c), vm, AF.Copy, NOBOAT, -DOWN)
+                if n in BY_SCAN[r]:
+                    y = A("MI", 384, 512)
+                    together(lambda: (mm(y, A("ID"), A("OFFD"), True, False), mm(y, A("BDH"), sl, False, True)))
+                    scan(A("LS"), A("RST"), y, 0.0, OP.add); ts(lu_(s, *c), A("LS", 15, 128, 16), -SUMK, OP.add)
+                else: aslist(sl[0], lu_(s, *c))
+                send(1, A("LV%d_%d" % (r, s + 1), *c), lu_(s, *c), "aV%d_%d_%d" % (r, s + 1, i), [A("UL0")])
+                zo = A("ZO%d_%d" % (r, s), *h)
+                gather("V" if n in ZO_V[r] else "S", zo, A("X"), lu_(s, *c), f=AF.Relu)
+                if FUSE:
+                    marks = [(A("TH%d_%d" % (r, s + 1), h[0] + j, h[0] + j + 64), A(mb[0], h[0] + j, h[0] + j + 64), "aF%d_%d_%d" % (r, s + 1, i), 4) for j in (0, 64)]
+                    sends([(1, A("Z%d_%d" % (r, s + 1), *h), zo, "aZ%d_%d_%d" % (r, s + 1, i), 2)] + [(1,) + x for x in marks])
+                else: send(1, A("Z%d_%d" % (r, s + 1), *h), zo, "aZ%d_%d_%d" % (r, s + 1, i))
+                if TH_LAST: send(1, A("TH%d_%d" % (r, s + 1), *h), mb, "aF%d_%d_%d" % (r, s + 1, i), [zo if TH_LAST == 2 else lu_(s, *c)])
             else:
-                lm = A("LM%d" % (n % 2))
-                mm(A("MI", 384, 512), sl, A("BDH"), True, True); tt(lm, A("MI", 384, 512), A("DIAG"), OP.mult)
-                act(A(vmb(s), *c), A("MI", 384, 512, 16), AF.Copy, NOBOAT, -DOWN)
-                mm(A("MI", 128, 136), lm, A("B8"), True, True); ts(lu, A("MI", 128, 136), 2048.0, OP.add)
-            if s < 2:
-                send(1, A("LV%d_%d" % (r, s + 1), *c), lu, "aV%d_%d_%d" % (r, s + 1, i), [A("UL0")])
-                zo = A("ZO%d_%d" % (r, s), 128 * i, 128 * i + 128)
-                gather("S", zo, A("X"), lu)
-                send(1, A("Z%d_%d" % (r, s + 1), 128 * i, 128 * i + 128), zo, "aZ%d_%d_%d" % (r, s + 1, i))
+                y = A("MI", 240, 504)
+                together(lambda: (mm(y, sl, A("BG"), True, False), mm(y, A("KM", p1=1), A("CG", p1=1), False, True)))
+                act(A("HI2", 264 * i, 264 * i + 264), y, AF.Sign, A("HALF"))
 
-        def vmb(s): return "VMB%d" % s if s else "VMB0_%d" % r
-
-        def aslist(sl, lu):
+        def aslist(sl, lu, h0=0):
             w = width(lu); o = A("MI", 128, 128 + w)
-            together(lambda: [mm(o, A("DB", 15 - b, 143 - b), A(sl, b, 16 * w, 16), b == 0, b == 15) for b in range(16)])
-            ts(lu, o, 2048.0, OP.add)
-
-        def steps(out, io, an, nj, c0, c1, share):
-            ts(A(nj, c0, c1), A(an, c0, c1), M128, OP.add, M128, OP.subtract)
-            if share:
-                tt(A("SB", c0, c1), A(an, c0, c1), A(nj, c0, c1), OP.subtract); ts(A(nj + "B", c0, c1), A("SB", c0, c1), -63.0, OP.add, STEEP, OP.mult)
-            if share < 4 and NARROW:
-                ts(A("PA", c0, c1), A(an, c0, c1), -1.0, OP.mult, 63.5, OP.add); tt(A(nj + "C", c0, c1), A("PA", c0, c1), A(nj, c0, c1), OP.add)
-            for j in range(c0, c1):
-                o = A(out, 128 * j, 128 * j + 128)
-                if j % 4 < share: act(o, A("IO144", 0, 128), AF.Sigmoid, A(nj + "B", j, j + 1), STEEP)
-                elif NARROW: ts(o, A("IOH"), A(nj + "C", j, j + 1), OP.is_ge)
-                else: ts(o, A(io), A(nj, j, j + 1), OP.add, A(an, j, j + 1), OP.is_lt)
+            together(lambda: [mm(o, A("DB", 15 - b, 143 - b), A(sl, h0 + b, h0 + 16 * w, 16), b == 0, b == 15) for b in range(16)])
+            ts(lu, o, -SUMK, OP.add)
 
         def codes():
             together(lambda: [mm(A("MI", 256 + 8 * i, 264 + 8 * i), A(z0[0], 128 * i, 128 * i + 128), A("WU"), True, True) for i in range(3)] +
-                     [mm(A("MI", 288, 312), A("DUB", 15 - b, 143 - b), A(z0[0], b, 384, 16), b == 0, b == 15) for b in range(16)])
+                     [mm(A("MI", 288, 312), A("KM4096", p1=1), A("ONE", 0, 24, p1=1), True, False)] +
+                     [mm(A("MI", 288, 312), A("DUB", 15 - b, 143 - b), A(z0[0], b, 384, 16), False, b == 15) for b in range(16)])
             ts(A("UT"), A("MI", 256, 280), MAG, OP.add, MAG, OP.subtract); tt(A("U%d" % r), A("MI", 256, 280), A("UT"), OP.subtract)
-            tt(A("ID_"), A("MI", 288, 312), A("VL"), OP.add); ts(A("IC"), A("ID_"), 4095, OP.bitwise_and); ts(A("FA"), A("IC"), -2048.0, OP.add)
+            tt(A("FA"), A("MI", 288, 312), A("VL"), OP.add)
             send(1, A("UL%d" % r), A("U%d" % r), "aU%d" % r)
-            gather("S", A("WG"), A("IW"), A("LW"))
+            gather("V" if "W" in ON_V[r] else "S", A("WG"), A("IW"), A("LW"))
             together(lambda: [mm(A("MI", 320 + 8 * i, 328 + 8 * i), A("WG", 128 * i, 128 * i + 128), A("B1"), True, True) for i in range(3)])
-            act(A("W0"), A("MI", 320, 344), AF.Copy, 63.5, -1.0)
+            act(A("W0"), A("MI", 320, 344), AF.Copy, -63.5); rows(0, A("W0"))
 
-        def exdig(s):
-            steps("YL%d" % s, "NIH", "ML%d" % r if s else "W0", "WL%d" % s, 0, 24, SHARE[s])
-            act(A("EF"), A("F%d_%d" % (r, s)), AF.Copy, -WHOLE); tt(A("EG"), A("EF"), A("S1_%d" % s, 15, 384, 16), OP.subtract)
-            if s == 0: act(A("EH"), A("EG"), AF.Copy, 8192.0, 32768.0); tt(A("XC0"), A("EH"), A("WL0"), OP.subtract)
-            else:
-                ts(A("EA"), A("ML%d" % r), -1.0, OP.mult, 63.5, OP.add); ts(A("EC"), A("EA"), 7, OP.arith_shift_right, 7, OP.bitwise_and)
-                act(A("EH"), A("EG"), AF.Copy, 64.0, 256.0); tt(A("XC1"), A("EH"), A("EC"), OP.add)
+        def bits(s, c0, c1):
+            tt(A("GO%d_%d" % (r, s), c0, c1), A("S1", 16 * c0 + 15, 16 * c1, 16), A("FL%d_%d" % (r, s), c0, c1) if MARKS else A("TH%d_%d" % (r, s), 16 * c0, 16 * c1, 16), OP.is_le)
 
-        def exadd(s, c0, c1):
-            tt(A("UM%d" % s, c0, c1), A(("UL%d" if s else "U%d") % r, c0, c1), A("GL%d_%d" % (r, s + 1), c0, c1), OP.mult)
-            for j in range(c0, c1):
-                q = j % 8; y = A("YU%d" % s, 128 * j, 128 * j + 128)
-                ts(y, A("IOH" if s else "IOH128"), A("XC%d" % s, j, j + 1), OP.is_equal, A("UM%d" % s, j, j + 1), OP.mult)
-                mm(A("EX%d" % (q // 4), q % 4 * 128, q % 4 * 128 + 128), A("YL%d" % s, 128 * j, 128 * j + 128), y, False, s == 1 and j in (19, 23), True)
+        def move(q, out, a):
+            if q == "S": act(out, a, AF.Copy)
+            elif q == "V": cp(out, a)
+            else: keep(out, a)
 
-        def pendig(s, c0, c1):
-            if s == 2: act(A(vmb(s), c0, c1), A("MI", 160 + c0, 160 + c1), AF.Copy, NOBOAT, -DOWN)
-            steps("HOH%d" % s, "NIB", vmb(s), "HP%d" % s, c0, c1, SHARE[1 + s + c0 // 16])
+        def passed(s, c0, c1):
+            if s == 1 and MARKS and c1 - c0 == 8: return
+            bits(s, c0, c1)
+            send(-1, A("GL%d_%d" % (r, s), c0, c1), A("GO%d_%d" % (r, s), c0, c1), "aG%d_%d_%d" % (r, s, c0 // 8))
 
-        def penadd(s, c0, c1, end=False):
-            m = "GO%d_%d" % (r, s)
-            if s < 2:
-                tt(A("FC%d" % s, c0, c1), A(m, c0, c1), A("GL%d_%d" % (r, s + 1), c0, c1), OP.subtract); m = "FC%d" % s
-            for j in range(c0, c1):
-                sg = A("SG%d" % s, 34 * j, 34 * j + 33)
-                act(sg, A("I128"), AF.Sign, A("HP%d" % s, j, j + 1), A(m, j, j + 1))
-                mm(A("PEN", j % 8, 264, 8), A("HOH%d" % s, 128 * j, 128 * j + 128), sg, False, end and j == c1 - 1, True)
+        def named(s, c0, c1):
+            if s in DIRECT: return A("MI", 160 + c0, 160 + c1)
+            act(vm_(s, c0, c1), A("MI", 160 + c0, 160 + c1), AF.Copy, -63.5 - SUMK); return vm_(s, c0, c1)
 
-        def penback():
-            ts(A("HP0"), A("ML%d" % r), NOBOAT, OP.not_equal); tt(A("FC0"), A("HP0"), A("GO%d_1" % r), OP.subtract)
-            zero = lambda: mm(A("PEN", 0, 264), A("ZR", 0, 128, p1=1), A("ZR", 0, 264, p1=1), True, False, True)
-            zero()
-            for j in range(24):
-                sg = A("SG0", 34 * j, 34 * j + 33)
-                act(sg, A("I128"), AF.Sign, A("WL1", j, j + 1), A("FC0", j, j + 1))
-                mm(A("PEN", j % 8, 264, 8), A("YL1", 128 * j, 128 * j + 128), sg, False, j == 23, True)
-            act(A("CB%d" % r), A("PEN", 0, 264), AF.Copy); zero()
-            send(-1, A("CL%d" % r), A("CB%d" % r), "aC%d" % r)
+        def rows(j, an, c0=0, c1=24):
+            ts(A("NJ%d" % j, c0, c1), an, M128, OP.add, M128, OP.subtract); tt(A("LD%d" % j, c0, c1), A("NJ%d" % j, c0, c1), an, OP.subtract)
+            for c in range(c0, c1):
+                ld = A("LD%d" % j, c, c + 1)
+                if j < 2: ts(low(j, c), A("IOL"), ld, OP.is_equal)
+                elif c in S_ROWS[r][j - 2]: act(low(j, c), A("IOS"), AF.Sign, ld)
+                else: ts(low(j, c), A("IOL"), ld, OP.is_le, 0.5, OP.subtract)
+
+        def low(j, c): return A("LO%d" % j, 128 * c, 128 * c + 128)
+        def pen(c): return A("PEN", c % 8, 264, 8)
+
+        def entry(s):
+            m = A("F%d_%d" % (r, s)) if MARKS else A("MB%d_%d" % (r, s), 0, 384, 16)
+            ts(A("RR"), m, MAG, OP.add, MAG, OP.subtract); tt(A("FR"), m, A("RR"), OP.subtract)
+            act(A("EH"), A("FR"), AF.Copy, (TIE[s] - 64 * (s == 0)) / 32, -2.0)
+            if s: ts(A("EA"), A("ML%d" % r), 63.5, OP.add); ts(A("EC"), A("EA"), 896, OP.bitwise_and)
+            act(A("ES"), A("EC" if s else "NJ0"), AF.Copy, 0.0, 1 / 32768); tt(A("XC%d" % s), A("EH"), A("ES"), OP.add)
+
+        def give(s, c0, c1):
+            tt(A("VA%d" % s, c0, c1), A("XC%d" % s, c0, c1), A("GL%d_%d" % (r, s + 1), c0, c1), OP.add)
+            for c in range(c0, c1):
+                y = A("HI%d" % s, 128 * c, 128 * c + 128)
+                ts(y, A("IOH"), A("VA%d" % s, c, c + 1), OP.is_equal, A(("UL%d" if s else "U%d") % r, c, c + 1), OP.mult)
+                together(lambda: [add(A("EX%d" % h, c % 8 * 64, c % 8 * 64 + 64), low(s, c), A(y[0], y[1] + 64 * h, y[1] + 64 * h + 64)) for h in range(2)])
+
+        def name(j, go, c0, c1):
+            for c in range(c0, c1):
+                sg, nj, ng = A("SG%d" % j, 34 * c, 34 * c + 33), A("NJ%d" % j, c, c + 1), (go[0], go[1] + c - c0, go[1] + c - c0 + 1) + go[3:]
+                if c in V_STEPS[r][j - 1]: ts(sg, A("J128"), nj, OP.is_le, ng, OP.mult)
+                else: act(sg, A("I128"), AF.Sign, nj, ng)
+                add(pen(c), low(j, c), sg)
+
+        def third(c0, c1):
+            rows(3, named(2, c0, c1), c0, c1)
+            for c in range(c0, c1): add(pen(c), low(3, c), A("HI2", 33 * c, 33 * c + 33))
+
+        def sums():
+            begin(A("PEN", 0, 264), "K0")
+            for h in range(2):
+                e = "EX%d" % h; begin(A(e), "K1536")
+                if r: add(A(e), A("ID16"), A("EXR", 512 * h, 512 * h + 512))
+                else: together(lambda: [add(A(e, b, 512, 4), A("O16", 512 * h + 128 * b, 512 * h + 128 * b + 128), A("ID16")) for b in range(4)])
+
+        def copy(name, out, a, bias=0.0):
+            if name in ON_V[r]: ts(out, a, bias, OP.add)
+            else: act(out, a, AF.Copy, bias)
 
         def settle():
-            for j, (l, w) in enumerate((("LU%d_0", 1.0), ("LU%d_1", 1.0), ("LV%d_1", 3.0), ("LV%d_2", 3.0))):
-                ts(A("AL", 24 * j, 24 * j + 24), A(l % r), 2048.0, OP.is_equal, w, OP.mult)
-            run("V", 96 * CY, [A("AL")], [A("AR")], lambda: g.vector.tensor_reduce(ap(A("AR")), ap(A("AL")), AxisListType.X, OP.add))
-            cp(A("AC"), A("AR")); mm(A("MI", 352, 353), A("BD16"), A("AC"), True, True)
-            cp(A("AI"), A("MI", 352, 353)); ts(A("AJ"), A("AI"), 3, OP.bitwise_and)
+            for j, (l, w) in enumerate(((lu_(0), 1.0), (lu_(1), 1.0), (A("LV%d_1" % r), 3.0), (A("LV%d_2" % r), 3.0))):
+                ts(A("AL", 24 * j, 24 * j + 24), l, NOBOAT, OP.is_equal, w, OP.mult)
+            mm(A("KEY", 256, 352), A("BD16"), A("AL"), True, True); reduce(A("AR"), A("KEY", 256, 352))
+            cp(A("AI"), A("AR")); ts(A("AJ"), A("AI"), 3, OP.bitwise_and)
             ts(A("FCOL"), A("AJ"), -1 / 1024, OP.mult, 25 / 1024, OP.add)
 
-        def boats(lu):
-            ts(A("BI"), lu, DOWN, OP.mult, -2048.0, OP.add); ts(A("BB"), lu, 2048.0, OP.is_equal)
-            tt(A("BD"), A("FA"), A("BB"), OP.mult); tt(A("FA"), A("BD"), A("BI"), OP.add)
+        def boats():
+            ts(A("BI2"), A("LH%d" % r), -NOBOAT, OP.add); ts(A("BB2"), A("LH%d" % r), NOBOAT, OP.is_equal)
+            for c in (0, 24): tt(A("BD"), A("FA"), A("BB2", c, c + 24), OP.mult); tt(A("FA"), A("BD"), A("BI2", c, c + 24), OP.add)
 
         def own():
-            z1, zn, y = A("ZO%d_0" % r), A("RD" if last else "Z%d_0" % (r + 1)), A("PEN", 0, 384); one = A("ONE", p1=1)
-            together(lambda: (mm(y, A("HID"), z0, True, False), mm(y, A("HID"), z1, False, False), mm(y, A("QROW", p1=1), one, False, True)))
-            act(A("RY"), y, AF.Copy, MAG); act(A("RB"), A("RY"), AF.Copy, -MAG)
-            together(lambda: (mm(y, A("ID"), z0, True, False), mm(y, A("NID"), z1, False, False), mm(y, A("GROW", p1=1), one, False, True)))
+            z1, zn, y = A("ZO%d_0" % r), A("RD" if last else "Z%d_0" % (r + 1)), A("PEN", 0, 384); one = A("ONE", 0, 384, p1=1)
+            mm(y, A("ID"), z0, True, False); mm(y, A("ID"), z1, False, True)
+            act(A("RY"), y, AF.Copy, 1024.0, 0.4995); ts(A("RB"), A("RY"), -1024.0, OP.add)
+            mm(y, A("ID"), z0, True, False); mm(y, A("NID"), z1, False, False); mm(y, A("K512", p1=1), one, False, True)
             tt(zn, y, A("RB"), OP.min)
             if last: dma("oyz", T.yz[:, :], ap(zn), 3 << 15, "Y", [zn], [])
 
-        def passed(s):
-            tt(A("GO%d_%d" % (r, s)), A("S1_%d" % s, 15, 384, 16), A("TH1", 0, 384, 16) if s else A("TH3"), OP.is_gt)
-
-        front(0); front(1); front(2)
-        if r:
-            for h in (0, 512): ts(A("OM", h, h + 512), A("O", h, h + 512), 4095, OP.bitwise_and)
-            columns("OM")
+        def ahead(f, n): a = len(ops); f(n); walk.update(range(a, len(ops)))
+        for n in range(3): ahead(front, n)
+        if r: spread("OF", r)
         codes()
         for n in range(9):
-            hear(n)
-            if n < 6: front(n + 3)
-            if n == 2:
-                send(1, A("ML%d" % r), A(vmb(0)), "aM%d" % r)
-                passed(0); own(); exdig(0); boats(A("LU%d_0" % r))
+            ahead(hear, n)
+            s, i = divmod(n, 3)
+            def ending(parts): return [c for c in parts if c[1] == 8 * i + 8]
+            for c in ending(PARTS[s - 1]) if s else (): passed(s, *c)
+            if n < 6: ahead(front, n + 3)
+            for c in ending(PARTS[3]) if s == 0 else ():
+                named(0, *c); send(1, A("ML%d" % r, *c), vm_(0, *c), "aM%d_%d" % (r, i)); rows(1, A("ML%d" % r, *c), *c)
+            if n == 2: own(); sums(); entry(0)
+            for c in ending(PARTS[0]) if s == 1 else ():
+                name(1, A("GO%d_1" % r, *c), *c); give(0, *c)
+            for c in ending(PARTS[4]) if s == 1 else (): rows(2, named(1, *c), *c)
             if n == 5:
-                passed(1)
-                send(-1, A("GL%d_1" % r), A("GO%d_1" % r), "aG%d_1" % r); send(-1, A("LL%d_1" % r), A("LU%d_1" % r), "aL%d_1" % r)
-                for h in ("EX0", "EX1"): mm(A(h), A("ONE16", p1=1), A("R1536", p1=1), True, False)
-                exadd(0, 0, 24); exdig(1); penback(); pendig(1, 0, 24); boats(A("LL%d_1" % r))
+                copy("B", A("CB%d" % r), A("PEN", 0, 264)); begin(A("PEN", 0, 264), "K0"); send(-1, A("CL%d" % r), A("CB%d" % r), "aC%d" % r)
+                send(-1, A("LH%d" % r, 24, 48), lu_(1), "aL%d_1" % r)
+                entry(1); boats()
                 if not last: settle()
-            if n == 7:
-                send(-1, A("GL%d_2" % r, 0, 16), A("GO%d_2" % r, 0, 16), "aG%d_2a" % r)
-                pendig(2, 0, 16); penadd(2, 0, 16); exadd(1, 0, 16); penadd(1, 0, 16)
-        send(-1, A("GL%d_2" % r, 16, 24), A("GO%d_2" % r, 16, 24), "aG%d_2b" % r)
-        pendig(2, 16, 24); penadd(2, 16, 24); exadd(1, 16, 24); penadd(1, 16, 24, True)
-        aslist("SEL2", A("LU%d_2" % r)); send(-2, A("LL%d_2" % r), A("LU%d_2" % r), "aL%d_2" % r)
-        boats(A("LL%d_2" % r))
-        if last: act(A("FB"), A("FA"), AF.Copy, 2048.0); dma("oyv", T.yv[:, :], ap(A("FB")), 1 << 14, "Y", [A("FB")], [])
+            for c in ending(PARTS[1]) if s == 2 else (): name(2, A("GL%d_2" % r, *c), *c); give(1, *c)
+            for c in ending(PARTS[2]) if s == 2 else (): third(*c)
+        for c in HOME[r]:
+            aslist("SEL2", lu_(2, *c), 16 * c[0]); send(-2, A("LL%d" % r, *c), lu_(2, *c), "aL%d_%d" % (r, 2 + c[0] // 8))
+            ts(A("BI", *c), A("LL%d" % r, *c), 0.0, OP.add); ts(A("BB", *c), A("LL%d" % r, *c), NOBOAT, OP.is_equal)
+            tt(A("BD", *c), A("FA", *c), A("BB", *c), OP.mult); tt(A("VL", *c), A("BD", *c), A("BI", *c), OP.add)
+            ts(A("LWI", *c), A("VL", *c), 4095 if last else 1023, OP.bitwise_and); cp(A("FB" if last else "LW", *c), A("LWI", *c))
+        if last: dma("oyv", T.yv[:, :], ap(A("FB")), 1 << 14, "Y", [A("FB")], [])
         else:
-            ts(A("VL"), A("FA"), 2048.0, OP.add); ts(A("LWI"), A("VL"), 1023, OP.bitwise_and); cp(A("LW"), A("LWI"))
             act(A("FI"), A("ID"), AF.Copy, 0.0, A("FCOL")); act(A("NFI"), A("NID"), AF.Copy, 0.0, A("FCOL"))
-        tt(A("C16"), A("PEN", 0, 264), A("CL%d" % r), OP.add)
-        together(lambda: [mm(A("PEN", 128 * h, 128 * h + 128), A("C16", 128 * h + d, 128 * h + d + 128), A(w), d == 8, d == 0, True)
-                          for h in range(2) for d, w in ((8, "DM"), (0, "NDM"))])
-        act(A("HT"), A("PEN", 0, 256), AF.Sign)
+        add(A("PEN", 0, 264), A("TRI"), A("CL%d" % r))
+        copy("C", A("C16"), A("PEN", 0, 264))
+        for h in range(2):
+            y = A("PEN", 128 * h, 128 * h + 128) if h or not HT_APART else A("MI", 0, 128)
+            together(lambda: [mm(y, A("C16", 128 * h + d, 128 * h + d + 128), A(w), d == 0, d == 8, True) for d, w in ((0, "DM"), (8, "NDM"))])
+            if HT_APART:
+                if "HI"[h] in ON_V[r]: ts(A("HT", 128 * h, 128 * h + 128), y, 0.0, OP.is_gt)
+                else: act(A("HT", 128 * h, 128 * h + 128), y, AF.Sign)
+        if not HT_APART:
+            if "H" in ON_V[r]: ts(A("HT"), A("PEN", 0, 256), 0.0, OP.is_gt)
+            else: act(A("HT"), A("PEN", 0, 256), AF.Sign)
+        ends = [sum(STORES[:j + 1]) for j in range(len(STORES))]
         for c in range(8):
-            d = ("D0", "D1", "D2", "KEY")[c % 4]; x = A("X", xcol(512 * c), xcol(512 * c) + 512)
-            mm(A(d), A("ID"), x, True, False)
-            together(lambda: [mm(A(d, 128 * b, 128 * b + 128), A("WA", 128 * ((4 * c + b) % 16), 128 * ((4 * c + b) % 16) + 128),
-                                 A("HT", 128 * (c // 4), 128 * (c // 4) + 128), False, b == 3, True) for b in range(4)])
-            if c in RELU_V[r]: ts(x, A(d), 0.0, OP.max)
+            x = A("X", 512 * c, 512 * c + 512); p = dict(p0=32 * (c % 4), p1=32 * (c % 4) + 32)
+            bare = c in RELU_V[r] and not last
+            banks = ("MI", "PEN") if bare else ("D0", "D1", "D2", "KEY") + ("MI",) * last
+            d = banks[len([j for j in range(c) if (j in RELU_V[r] and not last) == bare]) % len(banks)]
+            if not bare: mm(A(d), A("ID"), x, True, False)
+            together(lambda: [mm(A(d, 128 * b, 128 * b + 128), A("WA", 128 * b, 128 * b + 128, **p), A("HT", 128 * (c // 4), 128 * (c // 4) + 128, **p), bare, bare or b == 3, True)
+                              for b in range(4)])
+            if bare: tt(x, x, A(d), OP.add)
+            elif c in RELU_V[r]: ts(x, A(d), 0.0, OP.max)
             else: act(x, A(d), AF.Relu)
-            if last: dma("oyx", T.yx[:, 512 * c:512 * c + 512], ap(x), 1 << 17, "Y", [x], [], c << 17)
+            if last and c + 1 in ends:
+                c0 = 512 * (c + 1 - STORES[ends.index(c + 1)]); x = A("X", c0, 512 * c + 512)
+                dma("oyx", T.yx[:, c0:512 * c + 512], ap(x), 256 * width(x), "Y", [x], [])
         for h in range(2):
             c = (512 * h, 512 * h + 512)
-            act(A("EXQ", *c), A("EX%d" % h), AF.Copy); tt(A("EXR", *c), A("EX%d" % h), A("EXQ", *c), OP.subtract)
-        for h in range(2):
-            e = "EX%d" % h; c = (512 * h, 512 * h + 512)
-            together(lambda: [mm(A(e, 128 * b, 128 * b + 128), A("EXR", 4 * h + b, 1024, 8), A("DM4"), True, True) for b in range(4)])
-            if not last: tt(A("O", *c), A(e), A("OT", *c), OP.add)
-            else:
-                tt(A("OT", *c), A(e), A("O", *c), OP.add); ts(A("OM", *c), A("OT", *c), 4095, OP.bitwise_and)
+            copy("QR"[h], A("EXQ", *c), A("EX%d" % h), 1 / 8192); tt(A("EXR", *c), A("EX%d" % h), A("EXQ", *c), OP.subtract)
+        def ex(h, b): return A("EXR", 512 * h + b, 512 * h + 512, 4)
         if last:
-            ts(A("YH"), A("OM", 512, 1024), 4096.0, OP.mult); tt(A("YN"), A("YH"), A("OM", 0, 512), OP.add)
+            together(lambda: [mm(A("EX0", 128 * b, 128 * b + 128), ex(h, b), A("D4" if h else "ID16"), h == 0, h == 1) for b in range(4) for h in range(2)])
+            if "Y" in ON_V[r]: ts(A("YN"), A("EX0"), 4096.0, OP.mult, 2048.0 * 4097, OP.add)
+            else: act(A("YN"), A("EX0"), AF.Copy, 2048.0 * 4097, 4096.0)
             dma("oyn", T.yn[:, :], ap(A("YN")), 1 << 18, "Y", [A("YN")], [])
+        else:
+            for h in range(2):
+                e = "EX%d" % h
+                together(lambda: [mm(A(e, 128 * b, 128 * b + 128), ex(h, b), A("D4"), True, True) for b in range(4)])
+                copy("OP"[h], A("OF", 512 * h, 512 * h + 512), A(e))
 
     for r in range(RO):
         round_(r)
-    if not ORDER: ORDER.extend(schedule(ops))
+    if not ORDER: ORDER.extend(schedule(ops, [(i in walk) * (BIG if o[1] > 400 and o[0] in "VS" or o[3][-1][0] in ("SELC", "XG0", "XG1", "XG2") else 1.0) if o[3] else 0.0 for i, o in enumerate(ops)]))
     for i in ORDER: ops[i][5]()
     for sem in cnt:
         if known["G"].get(sem, 0) < cnt[sem]: g.wait_ge(T.sem[sem], cnt[sem])

from concourse.bass import DstId, RemoteDMATransfer
from concourse.mybir import dt, AluOpType as OP, ActivationFunctionType as AF, AxisListType

RO, ST, NCH = 2, 3, 3
BS = {"float32": 4, "int32": 4, "bfloat16": 2, "float16": 2, "uint16": 2}
SCRATCH, ALIAS, POOL = {}, {}, {}
V_QUARTERS = ({(0, 1), (0, 3)},) * 2
S_PO = ((3, 6), (3, 6))
S_ABS = ((), ())
RELU_V = ((1, 3, 5, 7), (1, 3, 5))
PARTS = (((0, 8), (8, 16), (16, 24)), ((0, 16), (16, 24)), ((0, 16), (16, 24)), ((0, 24),), ((0, 24),))
STORES = (1, 1, 2, 2, 2)
PO_SPLIT, HALVES, KEY_SPLIT, ZO_V = ((), ()), ((), ()), ((), ()), ((0, 1),) * 2
ON_V = ("CW", "C")
PARTS2, JOIN, NOJOIN = ((0, 24),), (1,), ()
BY_SCAN, ZFIRST = (range(6), range(6)), 1
S_ROWS = (((), range(4, 16)),) * 2
SPREAD, IW_S = ("SGG", "GGY"), True
ROOM, FUSE, NZT, CUT, TH_LAST, DIRECT = {}, False, 3, 384, 0, (1, 2)
HOME = (((0, 16), (16, 24)), ((0, 24),))
MARKS = ""
V_STEPS, HT_APART, Z_LAST = (((), range(20, 24)),) * 2, True, True
OWN_V, OF_V = False, ()


def _b(names, cols, dtype, where="sbuf"):
    for n in names.split():
        SCRATCH[n] = (where, [128, cols], dtype)


def _s(names, cols, dtype):
    for n in names.split():
        w = 32 // BS[dtype]; o = POOL.get(dtype, 0)
        ALIAS[n] = ("pool_" + dtype, o, cols); POOL[dtype] = o + (cols + w - 1) // w * w


_b("X", 4112, "bfloat16"); _b("OT", 4112, "int32"); _b("OF", 4112, "float32"); _b("NB", 512, "int32"); _b("YN", 512, "float32")
_b("O16 EXQ EXR", 1024, "float16"); _b("IW", 1024, "float32")
_b("XG0 XG1 XG2 NR0 NR1", 2048, "bfloat16"); _b("AB0 AB1 SELC WA", 512, "float16"); _b("IR ONE", 512, "bfloat16")
_b("PO0 PO1 PO2 PO3", 128, "uint16"); _b("PF0 PF1 PF2 PF3 SEL0 SEL1 ZT0 ZT1 ZT2 IOL IOS IOH ID16 TRI DM NDM D4 BDH", 128, "float16")
_b("D0 D1 D2 KEY MI EX0 EX1 PEN", 512, "float32", "psum")
_b("NO0 NO1 RST ID NID FI NFI N6 BD16 KL KV OFFD IH", 128, "bfloat16"); _b("MB2 KF GF TH0 LS", 128, "float32"); _b("S1 WG TH", 384, "float32"); _b("RY", 384, "float16")
_b("LO0 LO1 LO2 LO3 HI0 HI1", 24 * 128, "float16"); _b("HI2", 3 * 264, "float16"); _b("SG1 SG2", 24 * 34, "float16")
_b("SEL2", 384, "float16"); _b("HT", 256, "float16"); _b("BG C16 CB0 CB1 CL0 CL1", 264, "float16"); _b("G2 CG", 264, "bfloat16"); _b("KB RB RD", 384, "bfloat16")
_b("DB", 144, "float16"); _b("DUB", 144, "bfloat16"); _b("IO", 144, "float32")
_s("K1536 K0 K2048 KM4096 K512 KM", 128, "bfloat16"); _s("I128 J128", 33, "float32"); _s("HALF", 1, "float32")
_s("VM1 VM2 W0 FA BB BI BD UT FB CF RR FR EH ES NJ0 NJ1 NJ2 NJ3", 24, "float32"); _s("BB2 BI2", 48, "float32")
_s("XC0 XC1 VA0 VA1", 24, "float16"); _s("LD0 LD1 LD2 LD3", 24, "bfloat16")
_s("VL LWI EA EC", 24, "int32"); _s("LW", 24, "uint16"); _s("B1", 8, "float32"); _s("H16 PW MK", 16, "float32")
for _r in range(RO):
    _s("LH%d" % _r, 48, "uint16")
    for _i in range(3):
        _b("Z%d_%d" % (_r, _i), 384, "bfloat16")
        if _i < 2:
            _b("MB%d_%d" % (_r, _i), 384, "float32"); _b("ZO%d_%d" % (_r, _i), 384, "bfloat16")
        if _i > 0:
            _b("TH%d_%d" % (_r, _i), 384, "float32"); _s("GO%d_%d GL%d_%d FL%d_%d F%d_%d" % (_r, _i, _r, _i, _r, _i, _r, _i - 1), 24, "float32"); _s("LV%d_%d LU%d_%d" % (_r, _i, _r, _i), 24, "uint16")
    _s("VM0_%d ML%d" % (_r, _r), 24, "float32"); _s("U%d UL%d" % (_r, _r), 24, "float16"); _s("LL%d" % _r, 24, "uint16")
_s("CI", 8, "int32"); _s("W8 WU", 8, "bfloat16"); _s("B8", 8, "float16")
_s("AL", 96, "bfloat16"); _s("AR FCOL", 1, "float32"); _s("AC PT", 1, "bfloat16"); _s("AI AJ", 1, "int32")
for _d in POOL:
    _b("pool_" + _d, POOL[_d], _d)

SEMAPHORES = ["V", "S", "P", "G", "ls", "dnb", "dv", "dz", "dx", "dcp0", "dcp1", "oyx", "oyn", "oyv", "oyz"]
for _r in range(RO):
    for _j in (1, 2):
        for _i in range(NCH):
            SEMAPHORES += ["a%s%d_%d_%d" % (_k, _r, _j, _i) for _k in "FVZG"]
        SEMAPHORES += ["aL%d_%d" % (_r, _j)]
    SEMAPHORES += ["aU%d" % _r, "aC%d" % _r, "aL%d_3" % _r, "aL%d_4" % _r] + ["aM%d_%d" % (_r, _i) for _i in range(NCH)]

MAG = 12582912.0
M128 = MAG * 128
T0, NOBOAT, SUMK = 34816.0, 4096.0, 15 * 2048.0 - 2048.0
TIE = (48.0, 31.0, 15.0)
CY, PCY, GCY, HOP, DMA0, DMAB = 0.83, 0.42, 1.56 * 0.83, 2100.0, 1500.0, 330.0


def A(name, c0=0, c1=None, step=1, p0=0, p1=128):
    if name in ALIAS:
        n, o, w = ALIAS[name]
        return (n, o + c0, o + (w if c1 is None else c1), step, p0, p1)
    return (name, c0, SCRATCH[name][1][1] if c1 is None else c1, step, p0, p1)


def psum(a): return SCRATCH[a[0]][0] == "psum"
def width(a): return len(range(a[1], a[2], abs(a[3])))
def two(*l): return all(BS[SCRATCH[a[0]][2]] == 2 for a in l)
def span(a): w = BS[SCRATCH[a[0]][2]]; return (a[4], a[5], a[1] * w, a[2] * w)


def meet(s, t, b):
    return s[0] < t[1] and t[0] < s[1] and s[2] // b * b < -(-t[3] // b) * b and t[2] // b * b < -(-s[3] // b) * b


def schedule(ops, walk):
    n = len(ops); deps = [dict() for _ in ops]; acc = {}
    for i, (q, c, d, reads, writes, _, sums, _) in enumerate(ops):
        dmai = d > 0
        for lst, w in ((reads, 0), (writes, 1), (sums, 2)):
            for a in lst:
                s = span(a)
                for (t, ow, j, dmaj) in acc.get(a[0], []):
                    if j != i and (ow != w or w == 1) and meet(s, t, 16 if ow and w and dmai != dmaj else 1):
                        deps[i][j] = deps[i].get(j, False) or not (ops[j][0] == q == "P" and psum(a))
        for a in writes:
            s = span(a); acc[a[0]] = [r for r in acc.get(a[0], []) if not (s[0] <= r[0][0] and r[0][1] <= s[1] and s[2] <= r[0][2] and r[0][3] <= s[3])]
        for lst, w in ((reads, 0), (writes, 1), (sums, 2)):
            for a in lst: acc.setdefault(a[0], []).append((span(a), w, i, dmai))
    deps = [{j: f for j, f in d.items() if not (ops[j][2] == 0 and any(j in deps[k] and d[k] for k in d))} for d in deps]
    banks = [sorted(set(a[0] for a in o[3] + o[4] + o[6] if psum(a))) for o in ops]; qs = [o[0] for o in ops]; cases = []
    for slow, jump, lat, hop, _, call, link, *fix in CASES:
        cs = [o[1] + (call + link * o[7]) * (o[0] == "G") if o[2] else slow * (o[1] + (jump - 1) * o[7]) + sum(fix) * (o[0] in "VS" and bool(b)) for o, b in zip(ops, banks)]
        ds = [o[2] + (hop + link * o[7]) * (o[0] == "G") if o[2] else c + lat for o, c in zip(ops, cs)]
        ways = []
        for turned in (False, True):
            before, after = [[] for _ in ops], [[] for _ in ops]
            for i in range(n):
                for j, full in deps[i].items():
                    d = ds[j] if full else cs[j]
                    if turned: before[j].append((i, d - cs[j] + cs[i])); after[i].append((j, d - cs[j] + cs[i]))
                    else: before[i].append((j, d)); after[j].append((i, d))
            ways.append((before, after))
        cases.append((cs, ds, lat, ways[0], ways[1]))

    def once(case, way, rank, ahead):
        cs, ds, lat = case[:3]; before, after = case[way]
        left = [len(d) for d in before]; at = [0.0] * n; ready = {q: [] for q in "VSPGY"}; free = {q: 0.0 for q in ready}; bank = {}; order = []; pick = {}
        for i in range(n):
            if not left[i]: ready[qs[i]].append(i)
        while len(order) < n:
            for q in ready:
                if q in pick or not ready[q]: continue
                f = free[q]; l = []
                for i in ready[q]:
                    t = at[i] if at[i] > f else f
                    for b in banks[i]:
                        x = bank.get(b)
                        if x and x[0] != q and x[1] > t: t = x[1]
                    l.append((t, rank[i], i))
                t0 = min(l)[0] + ahead; c = min((x for x in l if x[0] <= t0), key=lambda x: x[1])
                t0 = c[0] + SLIP; pick[q] = min((x for x in l if x[0] + cs[x[2]] <= t0), key=lambda x: x[1], default=c)
            t, _, i = min(pick.values()); q = qs[i]
            ready[q].remove(i); order.append(i); at[i] = t; free[q] = t + cs[i]; del pick[q]
            for b in banks[i]:
                bank[b] = (q, t + cs[i] + lat)
                for x in "VSP": pick.pop(x, None)
            for k, d in after[i]:
                if t + d > at[k]: at[k] = t + d
                left[k] -= 1
                if not left[k]: ready[qs[k]].append(k); pick.pop(qs[k], None)
        return max(at[i] + ds[i] for i in range(n)), order, [-at[i] - cs[i] for i in range(n)]

    def times(case, order, old=None, a=0):
        cs, ds, lat, deps, _ = case; a = a // 64 if old else 0
        at, why, (free, bank), kept = (old[1][:], old[2][:], old[4][a], old[4][:a]) if old else ([0.0] * n, [-1] * n, ({}, {}), [])
        free, bank = dict(free), dict(bank)
        for k in range(64 * a, n):
            if not k & 63: kept.append((dict(free), dict(bank)))
            i = order[k]; t = 0.0; w = -1; q = qs[i]
            for j, d in deps[0][i]:
                if at[j] + d > t: t = at[j] + d; w = j
            j = free.get(q)
            if j is not None and at[j] + cs[j] >= t: t = at[j] + cs[j]; w = j
            for b in banks[i]:
                j = bank.get(b)
                if j is not None and qs[j] != q and at[j] + cs[j] + lat > t: t = at[j] + cs[j] + lat; w = j
                bank[b] = i
            at[i] = t; why[i] = w; free[q] = i
        e = max(ends, key=lambda i: at[i] + ds[i])
        return at[e] + ds[e], at, why, e, kept

    ends = [i for i in range(n) if not cases[0][3][1][i]]

    start = {p: once(cases[p], 3, list(range(n)), 0.0) for p in PLANS}; best = None; base = None; pool = []
    for turn in range(TURNS):
        p = PLANS[turn % len(PLANS)]; case = cases[p]; now = start[p]; k0 = turn // len(PLANS); ahead = AHEAD[k0 % len(AHEAD)]
        for k in range(PASSES):
            rank = [x + (i * 7919 + turn * 104729) % 1009 * BLUR * (k0 >= len(AHEAD) // 2 and k == 0) for i, x in enumerate(now[2])]
            first = FIRST[(turn // len(PLANS) + k // 2) % len(FIRST)]
            rank = once(case, 4, [x + BACK * first * w for x, w in zip(rank, walk)], ahead)[2]
            now = once(case, 3, [x - first * w for x, w in zip(rank, walk)], ahead)
            if now[0] < start[p][0]: start[p] = now
            t = [times(c, now[1])[0] for c in cases]; base = base or t
            worth = sum(a / b * c[4] for a, b, c in zip(t, base, CASES))
            if best is None or worth < best[0]: best = (worth, now[1], t)
            pool.append((worth, now[1], p))
    seed = 1
    for turn in range(MIXES):
        pool.sort(key=lambda x: x[0]); del pool[KEEP:]
        seed = (seed * 1103515245 + 12345) % 2147483648; a = pool[(seed >> 8) % len(pool)]; b = pool[(seed >> 16) % len(pool)]
        seed = (seed * 1103515245 + 12345) % 2147483648; cut = (seed >> 8) % n; p = (a, b)[seed >> 5 & 1][2]; case = cases[p]
        head = set(a[1][:cut]); order = a[1][:cut] + [i for i in b[1] if i not in head]; kind = seed >> 6 & 7; ahead = AHEAD[(seed >> 20) % len(AHEAD)]
        if kind >= SHAKE:
            a = pool[(seed >> 10) % 3 % len(pool)]; rank = times(case, a[1])[1]; far = (200.0, 500.0, 1000.0)[(seed >> 13) % 3]
            for k, i in enumerate(a[1][cut:cut + 120]): rank[i] += ((i * 7919 + seed) % 1009 / 1009 - 0.5 - walk[i]) * far
            order = once(case, 3, rank, ahead)[1]
        elif kind & 3:
            rank = times(case, order)[1]
            if kind & 1: rank = once(case, 4, [-x - c for x, c in zip(rank, case[0])], ahead)[2]
            order = once(case, 3, rank, ahead)[1]
        t = [times(c, order)[0] for c in cases[:2]]
        if sum(t) > 1.012 * sum(best[2][:2]): continue
        t += [times(c, order)[0] for c in cases[2:]]; worth = sum(a / b * c[4] for a, b, c in zip(t, base, CASES))
        if worth < best[0]: best = (worth, order, t)
        if all(abs(worth - x[0]) > 1e-5 for x in pool): pool.append((worth, order, p))
    worth, order, t = best; ways = {}; now = [times(c, order) for c in cases]
    for step in range(SWAPS):
        seed = (seed * 1103515245 + 12345) % 2147483648; p = (seed >> 12) % len(cases)
        if p not in ways:
            why, i = now[p][2:4]; arcs = []
            while why[i] >= 0:
                if why[i] not in deps[i]: arcs.append((why[i], i))
                i = why[i]
            ways[p] = arcs; pos = {i: k for k, i in enumerate(order)}
        seed = (seed * 1103515245 + 12345) % 2147483648; j, i = ways[p][(seed >> 8) % len(ways[p])]; a, b = pos[j], pos[i]
        if seed >> 4 & 1:
            a = max(0, a - (seed >> 5 & 1) * (seed >> 20 & 15)); mv = {i}
            for k in reversed(order[a:b]):
                if any(k in deps[x] for x in mv): mv.add(k)
            if j in mv: continue
            new = order[:a] + [k for k in order[a:b + 1] if k in mv] + [k for k in order[a:b + 1] if k not in mv] + order[b + 1:]
        else:
            b = min(n - 1, b + (seed >> 5 & 3) * (seed >> 20 & 15)); mv = {j}
            for k in order[a + 1:b + 1]:
                if any(x in mv for x in deps[k]): mv.add(k)
            if i in mv: continue
            new = order[:a] + [k for k in order[a:b + 1] if k not in mv] + [k for k in order[a:b + 1] if k in mv] + order[b + 1:]
        tp = times(cases[p], new, now[p], a)
        if tp[0] > now[p][0]: continue
        t2 = [tp if k == p else times(c, new, now[k], a) for k, c in enumerate(cases)]; w2 = sum(x[0] / b * c[4] for x, b, c in zip(t2, base, CASES))
        if w2 <= worth: worth, order, now, ways = w2, new, t2, {}
    best = (worth, order, [x[0] for x in now])
    SPAN[:] = [best[2], best[0], now[0][:4], ops]
    return best[1]


CASES = ((1.3, 1.0, 240.0, 450.0, 1.0, 0.0, 0.0), (1.25, 1.0, 240.0, 700.0, 1.0, 0.0, 0.0), (1.0, 1.0, 220.0, 0.0, 1.0, 0.0, 0.0), (1.25, 1.0, 240.0, 0.0, 1.5, 0.0, 0.0),
         (1.4, 1.2, 240.0, 300.0, 0.7, 0.0, 0.0), (1.4, 0.8, 240.0, 300.0, 0.7, 0.0, 0.0))
PLANS = (0, 1)
TURNS, BLUR, FIRST, BACK, BIG, MIXES, KEEP, SHAKE, SWAPS = 12, 0.3, (0.0, 0.0, 1000.0), 0.0, 0.5, 500, 20, 5, 6000
ORDER, SPAN, PASSES, AHEAD, SLIP = [], [], 4, (0.0, 150.0, 250.0, 350.0, 200.0, 300.0), 30.0


def rank_program(g, core, T, topo):
    rank = T.rank_of(core)
    if rank is None:
        return
    N = len(T.cores)
    eng = {"V": g.vector, "S": g.scalar, "P": g.tensor, "G": g, "Y": g.sync}
    cnt, snap, acc, known = {}, {}, {}, {q: {} for q in eng}
    ops = []

    def ap(a):
        t = T[a[0]]
        if a[3] < 0: return t[a[4]:a[5], a[2] - 1:(a[1] - 1 if a[1] else None):a[3]]
        return t[a[4]:a[5], a[1]:a[2]] if a[3] == 1 else t[a[4]:a[5], a[1]:a[2]:a[3]]

    def bankspan(a): return (0, 128, 0, 2048) if psum(a) else span(a)

    def learn(q, comp, n):
        k = known[q]
        if k.get(comp, 0) >= n: return
        k[comp] = n
        for c2, n2 in snap.get((comp, n), {}).items():
            if k.get(c2, 0) < n2: k[c2] = n2

    def hazards(q, comp, reads, writes):
        need = {}
        for lst, w in ((reads, False), (writes, True)):
            for a in lst:
                ps = psum(a); s = bankspan(a)
                for (t, ow, oc, on, oq) in acc.get(a[0], []):
                    if not meet(s, t, 16 if ow and w and (oc in eng) != (comp in eng) else 1): continue
                    if ps:
                        if oq == q and oc == comp and (q == "P" or not (ow or w)): continue
                    elif not (ow or w): continue
                    if oc[0] in "do" and known[q].get(oc, 0) < on: on = cnt[oc]
                    if need.get(oc, 0) < on: need[oc] = on
        for oc in sorted(need, key=lambda c: -need[c]):
            if known[q].get(oc, 0) < need[oc]:
                eng[q].wait_ge(T.sem[oc], need[oc]); learn(q, oc, need[oc])

    def note(q, comp, n, reads, writes):
        for a in writes:
            s = bankspan(a)
            if not psum(a): acc[a[0]] = [r for r in acc.get(a[0], []) if not (s[0] <= r[0][0] and r[0][1] <= s[1] and s[2] <= r[0][2] and r[0][3] <= s[3])]
        for lst, w in ((reads, False), (writes, True)):
            for a in lst:
                s = bankspan(a)
                acc[a[0]] = [r for r in acc.get(a[0], []) if not (r[0] == s and r[1] == w and r[2] == comp and r[4] == q)] + [(s, w, comp, n, q)]

    def issue(q, reads, writes, call):
        hazards(q, q, reads, writes)
        i = call(); cnt[q] = cnt.get(q, 0) + 1
        i.then_inc(T.sem[q], 1)
        snap[(q, cnt[q])] = dict(known[q])
        note(q, q, cnt[q], reads, writes)

    group = []

    def run(q, cost, reads, writes, call, sums=(), jumps=0.0):
        if group: group[0].append((cost, reads, writes, call, list(sums)))
        else: ops.append((q, cost + jumps, 0.0, reads, writes, lambda: issue(q, reads, writes + list(sums), call), list(sums), jumps))

    def together(f):
        group.append([]); f(); l = group.pop()
        c = sum(x[0] for x in l)
        ops.append(("P", c, 0.0, [a for x in l for a in x[1]], [a for x in l for a in x[2]], lambda: [issue("P", x[1], x[2] + x[4], x[3]) for x in l],
                    [a for x in l for a in x[4]], 0.0))

    def dma(sem, out, in_, size, q="Y", reads=(), writes=(), after=0.0):
        def f():
            hazards(q, sem, reads, writes)
            eng[q].dma_start(out, in_).then_inc(T.sem[sem], 16)
            cnt[sem] = cnt.get(sem, 0) + 16
            snap[(sem, cnt[sem])] = dict(known[q])
            note(q, sem, cnt[sem], reads, writes)
        ops.append((q, size / DMAB if q == "Y" else 50.0, DMA0 + (after + size) / DMAB, list(reads), list(writes), f, [], 0.0))

    def send(step, out, in_, sem, after=()):
        dst, src = T.cores[(rank + step) % N], T.cores[(rank - step) % N]
        cnt[sem] = len(topo.engines(src, core)); note("R", sem, cnt[sem], [], [out])

        def f():
            hazards("G", "ls", [in_], [])
            rid, pid, _ = topo.addr(dst)
            g.remote_dma(ap(out), ap(in_), T.sem[sem], T.sem["ls"], pid, rid, topo.mask(core, dst))
            cnt["ls"] = cnt.get("ls", 0) + len(topo.engines(core, dst))
        ops.append(("G", 150.0 + ROOM.get(sem, 0.0), HOP + ROOM.get(sem, 0.0) + 128 * (span(out)[3] - span(out)[2]) / DMAB, [in_] + list(after), [out], f, [], 128 * (span(out)[3] - span(out)[2]) / DMAB))

    def sends(l):
        for step, out, in_, sem, share in l: cnt[sem] = cnt.get(sem, 0) + len(topo.engines(T.cores[(rank - step) % N], core)) // share
        for step, out, in_, sem, share in l: note("R", sem, cnt[sem], [], [out])

        def f():
            hazards("G", "ls", [x[2] for x in l], []); at = 0; tr = []
            for step, out, in_, sem, share in l:
                dst = T.cores[(rank + step) % N]; rid, pid, _ = topo.addr(dst); e = topo.engines(core, dst); k = len(e) // share
                tr.append(RemoteDMATransfer(dst_ids=[DstId(rid=rid, pnc=pid)], dma_engine_mask=sum(1 << j for j in e[at:at + k]), remote_sem=T.sem[sem], src=ap(in_), dst=ap(out)))
                at += k
            g.remote_dma_fused(tr, local_sem=T.sem["ls"]); cnt["ls"] = cnt.get("ls", 0) + at
        ops.append(("G", 150.0, HOP + 300.0 + 128 * (span(l[0][1])[3] - span(l[0][1])[2]) * 4 / DMAB, [x[2] for x in l], [x[1] for x in l], f, [], 0.0))

    def col(x):
        return (ap(x), [x]) if isinstance(x, tuple) else (x, [])

    def vc(n, *sides): return CY * max(64, n / 2 if two(*sides) else n)

    def ts(out, in0, s1, op0, s2=None, op1=None, off=None):
        v1, r1 = col(s1); v2, r2 = col(s2); tail = (op0,) if op1 is None else (op0, op1)
        if off: run("V", 50, [in0, off], [out], lambda: g.vector.tensor_scalar(ap(out), ap(in0).indirect(ap(off)), v1, v2, *tail), (), 16 * width(off) * GCY)
        else: run("V", vc(width(out), out, in0, *(r1 + r2)), [in0] + r1 + r2, [out], lambda: g.vector.tensor_scalar(ap(out), ap(in0), v1, v2, *tail))

    def tt(out, a, b, op):
        run("V", CY * max(64, width(out) * (1 if psum(a) or psum(b) else 2)), [a, b], [out], lambda: g.vector.tensor_tensor(ap(out), ap(a), ap(b), op))

    def scan(out, a, b, first, op):
        run("V", vc(width(out), out, a, b), [a, b], [out], lambda: g.vector.tensor_tensor_scan(ap(out), ap(a), ap(b), first, op, OP.max))

    def reduce(out, a):
        run("V", CY * max(64, width(a)), [a], [out], lambda: g.vector.tensor_reduce(ap(out), ap(a), AxisListType.X, OP.add))

    def cp(out, a):
        run("V", vc(width(out), out, a), [a], [out], lambda: g.vector.tensor_copy(ap(out), ap(a)))

    def ms(out, c):
        run("V", vc(width(out), out), [], [out], lambda: g.vector.memset(ap(out), c))

    def pc(l, r): return PCY * max(min(64, width(l)), width(r)) * (4 if SCRATCH[l[0]][2] == "float32" else 1)

    def mm(out, l, r, start, stop, whole=False):
        run("P", pc(l, r), [l, r], [A(out[0]) if whole else out], lambda: g.tensor.matmul(ap(out), ap(l), ap(r), start, stop))

    open_ = {}

    def begin(out, c):
        mm(out, A(c, p1=1), A("ONE", 0, width(out), p1=1), True, False, True); open_[out[0]] = [0]

    def add(out, l, r, part=None):
        left = open_[out[0]]; left[0] += 1

        def f():
            left[0] -= 1
            return g.tensor.matmul(ap(out), ap(l), ap(r), False, left[0] == 0)
        run("P", pc(l, r), [l, r], [], f, [part or A(out[0])])

    def act(out, a, f, bias=0.0, scale=1.0):
        v, r = col(bias); v2, r2 = col(scale)
        run("S", CY * max(64, width(out)), [a] + r + r2, [out], lambda: g.scalar.activation(ap(out), ap(a), f, bias=v, scale=v2))

    def gather(q, out, win, off, bias=0.0, f=AF.Copy):
        if q == "V": ts(out, win, 0.0, OP.max, off=off)
        else: run("S", 65, [win, off], [out], lambda: g.scalar.activation(ap(out), ap(win).indirect(ap(off)), f, bias=bias), (), 16 * width(off) * GCY)

    def iota(out, pat, base, cm, flag=True):
        c = 130 + 2 * CY * width(out)
        if flag: run("G", c, [], [out], lambda: g.iota(ap(out), pat, base, cm, allow_small_or_imprecise_dtypes=True))
        else: run("G", c, [], [out], lambda: g.iota(ap(out), pat, base, cm))

    def spread(o, r):
        for j in (1, 2, 3):
            src, d = A(o, 0, 1024), A(o, 1024 * j, 1024 * j + 1024)
            q = SPREAD[r][j - 1]
            if q == "Y": dma("dcp%d" % r, ap(d), ap(src), 1 << 19, "Y", [src], [d])
            for h in (0, 512) if q != "Y" else ():
                s, e = A(o, h, h + 512), A(o, 1024 * j + h, 1024 * j + h + 512)
                if q == "S": act(e, s, AF.Copy)
                elif q == "V": cp(e, s)
                else: keep(e, s)

    def keep(out, a):
        run("G", 170 + 2 * CY * width(out), [a], [out], lambda: g.affine_select(ap(out), ap(a), [[0, width(out)]], OP.is_ge, 0.0, 0, 0))

    ms(A("X", 4096, 4112), 512.0); ms(A("OT", 4096, 4112), 0); ms(A("OF", 4096, 4112), 0.0)
    dma("dv", ap(A("VL")), T.v[:, :], 1 << 14, "S", [], [A("VL")])
    dma("dnb", ap(A("NB")), T.nb[:, :], 1 << 18, "Y", [], [A("NB")])
    dma("dx", ap(A("X", 0, 4096)), T.tracks[:, :], 1 << 20, "Y", [], [A("X", 0, 4096)])
    if Z_LAST: dma("dz", ap(A("Z0_0")), T.z[:, :], 3 << 15, "Y", [], [A("Z0_0")])
    else: dma("dz", ap(A("Z0_0")), T.z[:, :], 3 << 15, "S", [], [A("Z0_0")], 1 << 18)
    iota(A("CI", 0, 1), [[1, 1]], 0, 1, False); iota(A("IO"), [[1, 144]], 0, 0)
    iota(A("KF"), [[0, 8], [1, 16]], 0, 0); iota(A("GF"), [[1, 8], [0, 16]], 0, 0); iota(A("IR"), [[1, 32], [0, 16]], 0, 0)
    iota(A("G2"), [[1, 8], [0, 33]], 0, 0); iota(A("CG", p1=1), [[0, 8], [1, 33]], int(SUMK) // 128, 0)
    if IW_S:
        iota(A("IW", 0, 256), [[1, 256]], 0, 0)
        for b in (1, 2, 3): act(A("IW", 256 * b, 256 * b + 256), A("IW", 0, 256), AF.Copy, 256.0 * b)
    else:
        for b in range(2): iota(A("IW", 512 * b, 512 * b + 512), [[1, 512]], 512 * b, 0)
    io, part, p16, pg, at15, odd, two15 = (A("IO", 0, 128),) + tuple(A("CF", j, j + 1) for j in (0, 4, 8, 12, 16, 20))
    ms(A("ONE", p1=33), 1.0)
    if DIRECT: ms(A("KV", p1=32), 0.0); ms(A("KV", p1=1), -SUMK); ms(A("KV", p0=32, p1=33), -63.5)
    for nm, c in (("K1536", 1536.0), ("K0", 0.0), ("K2048", 2048.0), ("KM4096", -4096.0), ("K512", 512.0), ("KM", -128.0)): ms(A(nm, p1=1), c)
    ms(A("KL", p1=32), 0.0); ms(A("KL", p1=1), 65536.0); ms(A("KL", p0=32, p1=33), 1 / 64)
    ms(A("HALF"), 0.5)
    if MARKS: ms(A("TH"), -1048576.0)
    for s in range(3):
        act(A("KB", 128 * s, 128 * s + 128, p1=32), A("GF", p1=32), AF.Copy, -4.0); act(A("KB", 128 * s, 128 * s + 128, p0=32, p1=33), A("KF", p0=32, p1=33), AF.Copy, TIE[s], -1.0)
    cp(part, A("CI", 0, 1))
    for j, (c, s, op) in enumerate(((p16, 15, OP.bitwise_and), (pg, 4, OP.arith_shift_right), (A("PT"), 31, OP.bitwise_and))):
        ts(A("CI", j + 1, j + 2), A("CI", 0, 1), s, op); cp(c, A("CI", j + 1, j + 2))
    ts(A("ID"), io, part, OP.is_equal)
    for nm, c in (("FI", 25 / 1024), ("NFI", -25 / 1024), ("NID", -1.0), ("N6", -6144.0), ("ID16", 1.0), ("D4", 4096.0)): act(A(nm), A("ID"), AF.Copy, 0.0, c)
    ts(at15, pg, 16.0, OP.mult, 15.0, OP.add); ts(odd, p16, 2.0, OP.mult, 1.0, OP.add)
    ms(A("H16"), 0.5); scan(A("PW"), A("H16"), A("H16"), 65536.0, OP.mult)
    ts(A("MK"), A("IO", 0, 16), p16, OP.is_equal); tt(A("MK"), A("MK"), A("PW"), OP.mult); reduce(two15, A("MK"))
    ts(A("W8"), A("IO", 0, 8), pg, OP.is_equal, two15, OP.mult)
    act(A("TH0"), A("GF"), AF.Copy, T0 + 63 / 64 - 4 * 65536.0, 65536.0)
    ts(A("RST"), A("KF"), 0.0, OP.is_equal, -1048576.0, OP.mult)
    ts(A("SELC"), A("IR"), A("PT"), OP.is_equal)
    ts(A("B8"), A("IO", 0, 8), pg, OP.is_equal); ts(A("B1"), A("IO", 0, 128, 16), part, OP.is_equal); ts(A("BG"), A("G2"), pg, OP.is_equal)
    ts(A("DB"), A("IO", 0, 144), at15, OP.is_equal); ts(A("DUB"), A("IO", 0, 144), at15, OP.is_equal, odd, OP.mult)
    ts(A("WU"), A("IO", 0, 8), pg, OP.is_equal, odd, OP.mult); act(A("WU"), A("WU"), AF.Copy, 0.0, 1 / 4096)
    act(A("IOL"), io, AF.Copy, 63.5, -1.0); act(A("IOS"), io, AF.Copy, -63.0); ts(A("TRI"), io, part, OP.is_ge, 0.5, OP.subtract)
    ts(A("CI", 4, 5), A("CI", 0, 1), 1.0, OP.add); ts(A("CI", 5, 6), A("CI", 4, 5), 127, OP.bitwise_and); cp(A("CF", 1, 2), A("CI", 5, 6))
    ts(A("CF", 2, 3), part, 126.5, OP.is_lt, -0.5, OP.add); ts(A("NDM"), io, A("CF", 1, 2), OP.is_equal, A("CF", 2, 3), OP.mult)
    act(A("NDM"), A("NDM"), AF.Copy, 0.0, 2.0); tt(A("DM"), A("ID16"), A("NDM"), OP.subtract); act(A("NDM"), A("DM"), AF.Copy, 0.0, -1.0)
    iota(A("IH"), [[4, 2], [8, 16], [1, 4]], 0, 0); act(A("IOH"), A("IH"), AF.Copy, 0.0, 1 / 256)
    act(A("I128"), A("IO", 0, 33), AF.Copy, 64.0, -128.0); act(A("J128"), A("IO", 0, 33), AF.Copy, 0.0, 128.0)
    act(A("WA"), A("SELC"), AF.Copy, 0.0, -45.0)
    ts(A("BD16"), A("GF"), pg, OP.is_equal)
    if any(BY_SCAN): act(A("BDH"), A("BD16"), AF.Copy); ts(A("OFFD"), A("KF"), p16, OP.not_equal, -65536.0, OP.mult)
    ts(A("LWI"), A("VL"), 1023, OP.bitwise_and); cp(A("LW"), A("LWI"))
    ts(A("OT", 0, 512), A("NB"), 4095, OP.bitwise_and); ts(A("OT", 512, 1024), A("NB"), 12, OP.arith_shift_right)
    for h in (0, 512): act(A("O16", h, h + 512), A("OT", h, h + 512), AF.Copy, -0.5, 1 / 4096)
    spread("OT", 0)

    turn, walk = [0], set()

    def round_(r):
        last = r == RO - 1
        z0 = A("Z%d_0" % r)
        def lu_(s, *c): return A("LU%d_%d" % (r, s), *c) if s else A("LH%d" % r, *(c or (0, 24)))
        def vm_(s, *c): return A("VM%d" % s if s else "VM0_%d" % r, *c)

        def front(n):
            s, i = divmod(n, 3)
            po, pf = A("PO%d" % (n % 4)), A("PF%d" % (n % 4)); l = A("LV%d_%d" % (r, s) if s else "LW", 8 * i, 8 * i + 8); w = A("OF" if r else "OT", 0, 4112 if s else 1024)
            if n in S_PO[r]: gather("S", pf, w, l, 0.0 if r else -2048.0); ts(po, pf, 2048.0, OP.add)
            else:
                for a, b in ((0, 2), (2, 8)) if n in PO_SPLIT[r] else ((0, 8),):
                    ts(A(po[0], 16 * a, 16 * b), w, 2048.0 if r else 0.0, OP.add, off=(l[0], l[1] + a, l[1] + b) + l[3:])
                ts(pf, po, -2048.0, OP.add)
            start = None
            for b, c0, c1 in pieces(n):
                start = c0 if start is None else start; q = "V" if (n, b) in V_QUARTERS[r] else "S"
                if q == "S" and b in JOIN and n not in NOJOIN and (n, b + 1) not in V_QUARTERS[r]: continue
                gather(q, A("XG%d" % (n % 3), start, c1), A("X"), A(po[0], start // 16, c1 // 16), f=AF.Relu); start = None

        def pieces(n): return [(b, 512 * b + c, 512 * b + c + w) for b in range(4) for c, w in (((0, CUT), (CUT, 512 - CUT)) if (n, b) in HALVES[r] else ((0, 512),))]

        def hear(n):
            s, i = divmod(n, 3); c = (8 * i, 8 * i + 8); h = (128 * i, 128 * i + 128); zt = "ZT%d" % (n % NZT); nr = "NR%d" % (n % 2); key = A("KEY", 0, 128)
            mm(A("KEY", 128, 256), A("Z%d_%d" % (r, s), *h), A("NFI"), True, True)
            act(A(zt), A("KEY", 128, 256), AF.Copy)
            for b, c0, c1 in pieces(n):
                turn[0] += 1; d = A("D%d" % (turn[0] % 3), 0, c1 - c0); p = dict(p0=32 * b, p1=32 * b + 32); o = A(nr, c0, c1); ab = A("AB%d" % (turn[0] % 2), 0, c1 - c0)
                zx = [(A(zt, **p), A("SELC", c0 - 512 * b, c1 - 512 * b, **p)), (A("FI"), A("XG%d" % (n % 3), c0, c1))]
                if ZFIRST == 2: together(lambda: (mm(d, *zx[1], True, False), mm(d, *zx[0], False, True)))
                else: mm(d, *zx[1 - ZFIRST], True, False); mm(d, *zx[ZFIRST], False, True)
                if (n, b) in S_ABS[r]: act(ab, d, AF.Abs); ts(o, ab, 0.5, OP.is_lt)
                else: ts(o, d, MAG, OP.add, MAG, OP.is_equal)
            for p0, p1 in ((0, 96), (96, 128)) if n in KEY_SPLIT[r] else ((0, 128),):
                together(lambda: [mm(A("KEY", 0, 128, p0=p0, p1=p1), A("KL", p0, p1, p1=33), A("KB", 128 * s, 128 * s + 128, p1=33), True, False)] +
                         [mm(A("KEY", k, 128, 16, p0, p1), A(nr, 16 * p0 + k, 16 * p1, 16), A("W8"), False, k == 15) for k in range(16)])
            s1 = A("S1", *h); mb = A("MB%d_%d" % (r, s), *h) if s < 2 else A("MB2"); th = A("TH0") if MARKS or not s else A("TH%d_%d" % (r, s), *h); no = A("NO%d" % (n % 2))
            if s and MARKS:
                th = A("TH", *h); move(MARKS[1], A("TH", h[0], h[1], 16), A("FL%d_%d" % (r, s), *c))
            scan(s1, th, key, -1048576.0, OP.max)
            if s < 2 and MARKS:
                f = A("F%d_%d" % (r, s), *c); move(MARKS[0], f, A("S1", h[0] + 15, h[1], 16)); out = (A("FL%d_%d" % (r, s + 1), *c), f, "aF%d_%d_%d" % (r, s + 1, i))
                if s and c in PARTS[0]: bits(1, *c); sends([(1,) + out + (2,), (-1, A("GL%d_1" % r, *c), A("GO%d_1" % r, *c), "aG%d_1_%d" % (r, i), 2)])
                else: send(1, *out)
            scan(mb[:3] + (-1,) + mb[4:], A("RST"), s1[:3] + (-1,) + s1[4:], 0.0, OP.add); tt(no, key, mb, OP.is_ge)
            if s < 2 and not FUSE and not TH_LAST and not MARKS: send(1, A("TH%d_%d" % (r, s + 1), *h), mb, "aF%d_%d_%d" % (r, s + 1, i))
            sl = A("SEL%d" % (n % 2)) if s < 2 else A("SEL2", *h)
            together(lambda: (mm(A("MI", 0, 128), A("K2048", p1=1), A("ONE", 0, 128, p1=1), True, False), mm(A("MI", 0, 128), no, A("N6"), False, True)))
            tt(sl, A("MI", 0, 128), A("PF%d" % (n % 4)), OP.max)
            vm = A("MI", 160 + c[0], 160 + c[1])
            if s in DIRECT: together(lambda: (mm(vm, A("KV", p1=33), A("ONE", 0, 8, p1=33), True, False), mm(vm, sl, A("B8"), False, True)))
            else: mm(vm, sl, A("B8"), True, True)
            if s < 2:
                if n in BY_SCAN[r]:
                    y = A("MI", 384, 512)
                    together(lambda: (mm(y, A("ID"), A("OFFD"), True, False), mm(y, A("BDH"), sl, False, True)))
                    scan(A("LS"), A("RST"), y, 0.0, OP.add); ts(lu_(s, *c), A("LS", 15, 128, 16), -SUMK, OP.add)
                else: aslist(sl[0], lu_(s, *c))
                send(1, A("LV%d_%d" % (r, s + 1), *c), lu_(s, *c), "aV%d_%d_%d" % (r, s + 1, i), [A("UL0")])
                zo = A("ZO%d_%d" % (r, s), *h)
                gather("V" if n in ZO_V[r] else "S", zo, A("X"), lu_(s, *c), f=AF.Relu)
                if FUSE:
                    marks = [(A("TH%d_%d" % (r, s + 1), h[0] + j, h[0] + j + 64), A(mb[0], h[0] + j, h[0] + j + 64), "aF%d_%d_%d" % (r, s + 1, i), 4) for j in (0, 64)]
                    sends([(1, A("Z%d_%d" % (r, s + 1), *h), zo, "aZ%d_%d_%d" % (r, s + 1, i), 2)] + [(1,) + x for x in marks])
                else: send(1, A("Z%d_%d" % (r, s + 1), *h), zo, "aZ%d_%d_%d" % (r, s + 1, i))
                if TH_LAST: send(1, A("TH%d_%d" % (r, s + 1), *h), mb, "aF%d_%d_%d" % (r, s + 1, i), [zo if TH_LAST == 2 else lu_(s, *c)])
            else:
                y = A("MI", 240, 504)
                together(lambda: (mm(y, sl, A("BG"), True, False), mm(y, A("KM", p1=1), A("CG", p1=1), False, True)))
                act(A("HI2", 264 * i, 264 * i + 264), y, AF.Sign, A("HALF"))

        def aslist(sl, lu, h0=0):
            w = width(lu); o = A("MI", 128, 128 + w)
            together(lambda: [mm(o, A("DB", 15 - b, 143 - b), A(sl, h0 + b, h0 + 16 * w, 16), b == 0, b == 15) for b in range(16)])
            ts(lu, o, -SUMK, OP.add)

        def codes():
            together(lambda: [mm(A("MI", 256 + 8 * i, 264 + 8 * i), A(z0[0], 128 * i, 128 * i + 128), A("WU"), True, True) for i in range(3)] +
                     [mm(A("MI", 288, 312), A("KM4096", p1=1), A("ONE", 0, 24, p1=1), True, False)] +
                     [mm(A("MI", 288, 312), A("DUB", 15 - b, 143 - b), A(z0[0], b, 384, 16), False, b == 15) for b in range(16)])
            ts(A("UT"), A("MI", 256, 280), MAG, OP.add, MAG, OP.subtract); tt(A("U%d" % r), A("MI", 256, 280), A("UT"), OP.subtract)
            tt(A("FA"), A("MI", 288, 312), A("VL"), OP.add)
            send(1, A("UL%d" % r), A("U%d" % r), "aU%d" % r)
            gather("V" if "W" in ON_V[r] else "S", A("WG"), A("IW"), A("LW"))
            together(lambda: [mm(A("MI", 320 + 8 * i, 328 + 8 * i), A("WG", 128 * i, 128 * i + 128), A("B1"), True, True) for i in range(3)])
            act(A("W0"), A("MI", 320, 344), AF.Copy, -63.5); rows(0, A("W0"))

        def bits(s, c0, c1):
            tt(A("GO%d_%d" % (r, s), c0, c1), A("S1", 16 * c0 + 15, 16 * c1, 16), A("FL%d_%d" % (r, s), c0, c1) if MARKS else A("TH%d_%d" % (r, s), 16 * c0, 16 * c1, 16), OP.is_le)

        def move(q, out, a):
            if q == "S": act(out, a, AF.Copy)
            elif q == "V": cp(out, a)
            else: keep(out, a)

        def passed(s, c0, c1):
            if s == 1 and MARKS and c1 - c0 == 8: return
            bits(s, c0, c1)
            send(-1, A("GL%d_%d" % (r, s), c0, c1), A("GO%d_%d" % (r, s), c0, c1), "aG%d_%d_%d" % (r, s, c0 // 8))

        def named(s, c0, c1):
            if s in DIRECT: return A("MI", 160 + c0, 160 + c1)
            act(vm_(s, c0, c1), A("MI", 160 + c0, 160 + c1), AF.Copy, -63.5 - SUMK); return vm_(s, c0, c1)

        def rows(j, an, c0=0, c1=24):
            ts(A("NJ%d" % j, c0, c1), an, M128, OP.add, M128, OP.subtract); tt(A("LD%d" % j, c0, c1), A("NJ%d" % j, c0, c1), an, OP.subtract)
            for c in range(c0, c1):
                ld = A("LD%d" % j, c, c + 1)
                if j < 2: ts(low(j, c), A("IOL"), ld, OP.is_equal)
                elif c in S_ROWS[r][j - 2]: act(low(j, c), A("IOS"), AF.Sign, ld)
                else: ts(low(j, c), A("IOL"), ld, OP.is_le, 0.5, OP.subtract)

        def low(j, c): return A("LO%d" % j, 128 * c, 128 * c + 128)
        def pen(c): return A("PEN", c % 8, 264, 8)

        def entry(s):
            m = A("F%d_%d" % (r, s)) if MARKS else A("MB%d_%d" % (r, s), 0, 384, 16)
            ts(A("RR"), m, MAG, OP.add, MAG, OP.subtract); tt(A("FR"), m, A("RR"), OP.subtract)
            act(A("EH"), A("FR"), AF.Copy, (TIE[s] - 64 * (s == 0)) / 32, -2.0)
            if s: ts(A("EA"), A("ML%d" % r), 63.5, OP.add); ts(A("EC"), A("EA"), 896, OP.bitwise_and)
            act(A("ES"), A("EC" if s else "NJ0"), AF.Copy, 0.0, 1 / 32768); tt(A("XC%d" % s), A("EH"), A("ES"), OP.add)

        def give(s, c0, c1):
            tt(A("VA%d" % s, c0, c1), A("XC%d" % s, c0, c1), A("GL%d_%d" % (r, s + 1), c0, c1), OP.add)
            for c in range(c0, c1):
                y = A("HI%d" % s, 128 * c, 128 * c + 128)
                ts(y, A("IOH"), A("VA%d" % s, c, c + 1), OP.is_equal, A(("UL%d" if s else "U%d") % r, c, c + 1), OP.mult)
                together(lambda: [add(A("EX%d" % h, c % 8 * 64, c % 8 * 64 + 64), low(s, c), A(y[0], y[1] + 64 * h, y[1] + 64 * h + 64)) for h in range(2)])

        def name(j, go, c0, c1):
            for c in range(c0, c1):
                sg, nj, ng = A("SG%d" % j, 34 * c, 34 * c + 33), A("NJ%d" % j, c, c + 1), (go[0], go[1] + c - c0, go[1] + c - c0 + 1) + go[3:]
                if c in V_STEPS[r][j - 1]: ts(sg, A("J128"), nj, OP.is_le, ng, OP.mult)
                else: act(sg, A("I128"), AF.Sign, nj, ng)
                add(pen(c), low(j, c), sg)

        def third(c0, c1):
            rows(3, named(2, c0, c1), c0, c1)
            for c in range(c0, c1): add(pen(c), low(3, c), A("HI2", 33 * c, 33 * c + 33))

        def sums():
            begin(A("PEN", 0, 264), "K0")
            for h in range(2):
                e = "EX%d" % h; begin(A(e), "K1536")
                if r: add(A(e), A("ID16"), A("EXR", 512 * h, 512 * h + 512))
                else: together(lambda: [add(A(e, b, 512, 4), A("O16", 512 * h + 128 * b, 512 * h + 128 * b + 128), A("ID16")) for b in range(4)])

        def copy(name, out, a, bias=0.0):
            if name in ON_V[r]: ts(out, a, bias, OP.add)
            else: act(out, a, AF.Copy, bias)

        def settle():
            for j, (l, w) in enumerate(((lu_(0), 1.0), (lu_(1), 1.0), (A("LV%d_1" % r), 3.0), (A("LV%d_2" % r), 3.0))):
                ts(A("AL", 24 * j, 24 * j + 24), l, NOBOAT, OP.is_equal, w, OP.mult)
            mm(A("KEY", 256, 352), A("BD16"), A("AL"), True, True); reduce(A("AR"), A("KEY", 256, 352))
            cp(A("AI"), A("AR")); ts(A("AJ"), A("AI"), 3, OP.bitwise_and)
            ts(A("FCOL"), A("AJ"), -1 / 1024, OP.mult, 25 / 1024, OP.add)

        def boats():
            ts(A("BI2"), A("LH%d" % r), -NOBOAT, OP.add); ts(A("BB2"), A("LH%d" % r), NOBOAT, OP.is_equal)
            for c in (0, 24): tt(A("BD"), A("FA"), A("BB2", c, c + 24), OP.mult); tt(A("FA"), A("BD"), A("BI2", c, c + 24), OP.add)

        def own():
            z1, zn, y = A("ZO%d_0" % r), A("RD" if last else "Z%d_0" % (r + 1)), A("PEN", 0, 384); one = A("ONE", 0, 384, p1=1)
            mm(y, A("ID"), z0, True, False); mm(y, A("ID"), z1, False, True)
            act(A("RY"), y, AF.Copy, 1024.0, 0.4995); ts(A("RB"), A("RY"), -1024.0, OP.add)
            mm(y, A("ID"), z0, True, False); mm(y, A("NID"), z1, False, False); mm(y, A("K512", p1=1), one, False, True)
            tt(zn, y, A("RB"), OP.min)
            if last: dma("oyz", T.yz[:, :], ap(zn), 3 << 15, "Y", [zn], [])

        def ahead(f, n): a = len(ops); f(n); walk.update(range(a, len(ops)))
        for n in range(3): ahead(front, n)
        if r: spread("OF", r)
        codes()
        for n in range(9):
            ahead(hear, n)
            s, i = divmod(n, 3)
            def ending(parts): return [c for c in parts if c[1] == 8 * i + 8]
            for c in ending(PARTS[s - 1]) if s else (): passed(s, *c)
            if n < 6: ahead(front, n + 3)
            for c in ending(PARTS[3]) if s == 0 else ():
                named(0, *c); send(1, A("ML%d" % r, *c), vm_(0, *c), "aM%d_%d" % (r, i)); rows(1, A("ML%d" % r, *c), *c)
            if n == 2: own(); sums(); entry(0)
            for c in ending(PARTS[0]) if s == 1 else ():
                name(1, A("GO%d_1" % r, *c), *c); give(0, *c)
            for c in ending(PARTS[4]) if s == 1 else (): rows(2, named(1, *c), *c)
            if n == 5:
                copy("B", A("CB%d" % r), A("PEN", 0, 264)); begin(A("PEN", 0, 264), "K0"); send(-1, A("CL%d" % r), A("CB%d" % r), "aC%d" % r)
                send(-1, A("LH%d" % r, 24, 48), lu_(1), "aL%d_1" % r)
                entry(1); boats()
                if not last: settle()
            for c in ending(PARTS[1]) if s == 2 else (): name(2, A("GL%d_2" % r, *c), *c); give(1, *c)
            for c in ending(PARTS[2]) if s == 2 else (): third(*c)
        for c in HOME[r]:
            aslist("SEL2", lu_(2, *c), 16 * c[0]); send(-2, A("LL%d" % r, *c), lu_(2, *c), "aL%d_%d" % (r, 2 + c[0] // 8))
            ts(A("BI", *c), A("LL%d" % r, *c), 0.0, OP.add); ts(A("BB", *c), A("LL%d" % r, *c), NOBOAT, OP.is_equal)
            tt(A("BD", *c), A("FA", *c), A("BB", *c), OP.mult); tt(A("VL", *c), A("BD", *c), A("BI", *c), OP.add)
            ts(A("LWI", *c), A("VL", *c), 4095 if last else 1023, OP.bitwise_and); cp(A("FB" if last else "LW", *c), A("LWI", *c))
        if last: dma("oyv", T.yv[:, :], ap(A("FB")), 1 << 14, "Y", [A("FB")], [])
        else:
            act(A("FI"), A("ID"), AF.Copy, 0.0, A("FCOL")); act(A("NFI"), A("NID"), AF.Copy, 0.0, A("FCOL"))
        add(A("PEN", 0, 264), A("TRI"), A("CL%d" % r))
        copy("C", A("C16"), A("PEN", 0, 264))
        for h in range(2):
            y = A("PEN", 128 * h, 128 * h + 128) if h or not HT_APART else A("MI", 0, 128)
            together(lambda: [mm(y, A("C16", 128 * h + d, 128 * h + d + 128), A(w), d == 0, d == 8, True) for d, w in ((0, "DM"), (8, "NDM"))])
            if HT_APART:
                if "HI"[h] in ON_V[r]: ts(A("HT", 128 * h, 128 * h + 128), y, 0.0, OP.is_gt)
                else: act(A("HT", 128 * h, 128 * h + 128), y, AF.Sign)
        if not HT_APART:
            if "H" in ON_V[r]: ts(A("HT"), A("PEN", 0, 256), 0.0, OP.is_gt)
            else: act(A("HT"), A("PEN", 0, 256), AF.Sign)
        ends = [sum(STORES[:j + 1]) for j in range(len(STORES))]
        for c in range(8):
            x = A("X", 512 * c, 512 * c + 512); p = dict(p0=32 * (c % 4), p1=32 * (c % 4) + 32)
            bare = c in RELU_V[r] and not last
            banks = ("MI", "PEN") if bare else ("D0", "D1", "D2", "KEY") + ("MI",) * last
            d = banks[len([j for j in range(c) if (j in RELU_V[r] and not last) == bare]) % len(banks)]
            if not bare: mm(A(d), A("ID"), x, True, False)
            together(lambda: [mm(A(d, 128 * b, 128 * b + 128), A("WA", 128 * b, 128 * b + 128, **p), A("HT", 128 * (c // 4), 128 * (c // 4) + 128, **p), bare, bare or b == 3, True)
                              for b in range(4)])
            if bare: tt(x, x, A(d), OP.add)
            elif c in RELU_V[r]: ts(x, A(d), 0.0, OP.max)
            else: act(x, A(d), AF.Relu)
            if last and c + 1 in ends:
                c0 = 512 * (c + 1 - STORES[ends.index(c + 1)]); x = A("X", c0, 512 * c + 512)
                dma("oyx", T.yx[:, c0:512 * c + 512], ap(x), 256 * width(x), "Y", [x], [])
        for h in range(2):
            c = (512 * h, 512 * h + 512)
            copy("QR"[h], A("EXQ", *c), A("EX%d" % h), 1 / 8192); tt(A("EXR", *c), A("EX%d" % h), A("EXQ", *c), OP.subtract)
        def ex(h, b): return A("EXR", 512 * h + b, 512 * h + 512, 4)
        if last:
            together(lambda: [mm(A("EX0", 128 * b, 128 * b + 128), ex(h, b), A("D4" if h else "ID16"), h == 0, h == 1) for b in range(4) for h in range(2)])
            if "Y" in ON_V[r]: ts(A("YN"), A("EX0"), 4096.0, OP.mult, 2048.0 * 4097, OP.add)
            else: act(A("YN"), A("EX0"), AF.Copy, 2048.0 * 4097, 4096.0)
            dma("oyn", T.yn[:, :], ap(A("YN")), 1 << 18, "Y", [A("YN")], [])
        else:
            for h in range(2):
                e = "EX%d" % h
                together(lambda: [mm(A(e, 128 * b, 128 * b + 128), ex(h, b), A("D4"), True, True) for b in range(4)])
                copy("OP"[h], A("OF", 512 * h, 512 * h + 512), A(e))

    for r in range(RO):
        round_(r)
    if not ORDER: ORDER.extend(schedule(ops, [(i in walk) * (BIG if o[1] > 400 and o[0] in "VS" or o[3][-1][0] in ("SELC", "XG0", "XG1", "XG2") else 1.0) if o[3] else 0.0 for i, o in enumerate(ops)]))
    for i in ORDER: ops[i][5]()
    for sem in cnt:
        if known["G"].get(sem, 0) < cnt[sem]: g.wait_ge(T.sem[sem], cnt[sem])
